import numpy as np
import ml_dtypes


def mxq(x, axis, fmt="e4m3"):
    dtype, down = {"e4m3": (ml_dtypes.float8_e4m3fn, 7), "e5m2": (ml_dtypes.float8_e5m2, 14)}[fmt]
    v = np.moveaxis(np.asarray(x, np.float32).astype(ml_dtypes.bfloat16).astype(np.float64), axis, -1)
    blocks = v.reshape(v.shape[:-1] + (-1, 32))
    amax = np.abs(blocks).max(-1, keepdims=True)
    byte = np.maximum(np.where(amax > 0, np.frexp(amax)[1] - 1 + 127, 0) - down, 1)
    scale = np.exp2(byte - 127.0)
    codes = (blocks / scale).astype(np.float32).astype(dtype).astype(np.float64)
    return np.moveaxis((codes * scale).reshape(v.shape), -1, axis)


WIDE = False


def mx_kscale(k):
    if not WIDE:
        return np.ones(k)
    levels = np.array([10, -10, 5, -5, 0])
    if k % 512:
        return np.exp2(np.random.permutation(np.resize(levels, k // 32))).repeat(32)
    a = np.empty((k // 512, 16))
    for p in range(k // 512):
        a[p, :8] = np.random.permutation(np.resize(levels, 8))
        for g in range(8):
            far = levels[np.abs(levels - a[p, g]) >= 10]
            a[p, g + 8] = far[np.random.randint(len(far))]
    return np.exp2(a.ravel()).repeat(32)


def f64(x):
    return np.asarray(x).astype(np.float64)


def striped(idx):
    return np.tile(idx.reshape(-1, 16).T, (8, 1)).astype(np.uint16)


def unstriped(offs):
    return offs[:16].T.reshape(-1).astype(np.int64)


E2M1 = np.array([0.0, 0.5, 1.0, 1.5, 2.0, 3.0, 4.0, 6.0, -0.0, -0.5, -1.0, -1.5, -2.0, -3.0, -4.0, -6.0])


def pack_weight(w, fmt):
    k, n = w.shape
    w = f64(np.asarray(w, np.float32).astype(ml_dtypes.bfloat16)).reshape(k // 32, 32, n)
    amax = np.abs(w).max(1)
    if fmt == "e4m3":
        byte = np.frexp(amax)[1] - 1 + 127 - 7
    else:
        mant, ex = np.frexp(amax / 6.0)
        byte = np.where(mant > 0.5, ex, ex - 1) + 127
    byte = np.clip(np.where(amax > 0, byte, 1), 1, 254)
    scaled = (w * np.exp2(127.0 - byte)[:, None, :]).reshape(k, n).astype(np.float32)
    by_word = np.ascontiguousarray(scaled.reshape(k // 512, 128, 4, n).transpose(0, 1, 3, 2))
    if fmt == "e4m3":
        words = by_word.astype(ml_dtypes.float8_e4m3fn).view(np.uint8)
    else:
        c = by_word.astype(ml_dtypes.float4_e2m1fn).view(np.uint8) & 0xF
        words = (c[..., 0::2] | (c[..., 1::2] << 4)).reshape(k // 512, 128, 2 * n)
    return np.ascontiguousarray(words), np.ascontiguousarray(byte.astype(np.uint8).reshape(k // 512, 16, n))


def unpack_weight(words, scales, fmt):
    g, _, n = scales.shape
    words = np.ascontiguousarray(words).reshape(g, 128, n, -1)
    if fmt == "e4m3":
        vals = words.view(ml_dtypes.float8_e4m3fn).astype(np.float64)
    else:
        nib = np.empty((g, 128, n, 4), np.uint8)
        nib[..., 0::2] = words & 0xF
        nib[..., 1::2] = words >> 4
        vals = E2M1[nib]
    vals = vals * np.repeat(np.exp2(scales.astype(np.float64) - 127.0), 8, axis=1)[..., None]
    return vals.transpose(0, 1, 3, 2).reshape(g * 512, n)


def silu(v):
    return v / (1.0 + np.exp(-np.maximum(v, -700.0)))


K, T, E, C, H, N = 1024, 1280, 4, 256, 512, 256


def by_expert(wq, xq):
    return np.concatenate([wq[e].T @ xq[:, e * C:(e + 1) * C] for e in range(E)], axis=1)


def setup_inputs():
    n = np.random.standard_normal
    s = mx_kscale(K)[:, None]
    u = mx_kscale(H)
    x = pack_weight(n((K, T)) * s, "e4m3")
    return {
        "x_words": x[0],
        "x_scales": x[1],
        "w1": (n((E, K, H)) / np.sqrt(K) / s[None]).astype(np.float32),
        "w3": (n((E, K, H)) / np.sqrt(K) / s[None] * u[None, None, :]).astype(np.float32),
        "w2": (n((E, H, N)) / np.sqrt(H) / u[None, :, None]).astype(np.float32),
        "gate": np.tile(np.random.uniform(0.2, 1.0, E * C), (N, 1)).astype(np.float32),
        "offs": striped(np.random.permutation(T)[:E * C]),
    }


def reference(x_words, x_scales, w1, w3, w2, gate, offs):
    idx = unstriped(offs)
    xq = unpack_weight(x_words, x_scales, "e4m3")[:, idx]
    h = silu(by_expert(mxq(f64(w1), 1, "e4m3"), xq))
    h = h * by_expert(mxq(f64(w3), 1, "e4m3"), xq)
    y = by_expert(mxq(f64(w2), 1, "e4m3"), mxq(h, 0, "e4m3"))
    out = np.zeros((N, T))
    out[:, idx] = f64(gate) * y
    return out

@@ -1,0 +1,196 @@
+from contextlib import ExitStack
+
+import concourse.mybir as mybir
+
+K, T, E, C, H, N = 1024, 1280, 4, 256, 512, 256
+FLOPS = 2 * E * C * (2 * K * H + H * N)
+
+F32 = mybir.dt.float32
+BF16 = mybir.dt.bfloat16
+I32 = mybir.dt.int32
+U32 = mybir.dt.uint32
+U16 = mybir.dt.uint16
+U8 = mybir.dt.uint8
+FP8X4 = mybir.dt.float8_e4m3fn_x4
+MULT = mybir.AluOpType.mult
+SILU = mybir.ActivationFunctionType.Silu
+
+P = 128
+PACK = 4
+K_PASS = P * PACK
+PASSES = K // K_PASS
+LIST_COLS = C // 16
+GROUP = 128
+GROUPS = C // GROUP
+N_TILES = N // P
+RAW_SLOTS = 12
+RAW_BYTES = PACK * H * 4
+
+
+def tile_moe_pkd_glu_silu_kernel(tc, x_words, x_scales, w1, w3, w2, gate, offs, out):
+    nc = tc.nc
+
+    with ExitStack() as ctx:
+        keep = ctx.enter_context(tc.tile_pool(name="keep", bufs=1))
+        raws = ctx.enter_context(tc.tile_pool(name="raws", bufs=1))
+        stage = ctx.enter_context(tc.tile_pool(name="stage", bufs=4))
+        codes = ctx.enter_context(tc.tile_pool(name="codes", bufs=8))
+        small = ctx.enter_context(tc.tile_pool(name="small", bufs=4))
+        psum = ctx.enter_context(tc.psum_pool(name="psum", bufs=3))
+
+        offsets = keep.tile([P, E * LIST_COLS], U16, name="offsets")
+        nc.sync.dma_start(offsets[:], offs)
+
+        token_scales = keep.tile([P, T], U8, name="token_scales", align_bytes=64)
+        nc.vector.memset(token_scales[:].bitcast(I32), 0)
+        warm_in = keep.tile([P, 8], F32, name="warm_in")
+        warm_out = keep.tile([P, 8], F32, name="warm_out")
+        nc.vector.memset(warm_in[:], 0.0)
+        nc.scalar.activation(warm_out[:], warm_in[:], SILU)
+        results = [keep.tile([P, T], F32, name=f"result{nt}") for nt in range(N_TILES)]
+        for nt in range(N_TILES):
+            nc.gpsimd.memset(results[nt][:], 0.0)
+
+        def slot_offset(chunk):
+            return (chunk % RAW_SLOTS) * RAW_BYTES
+
+        def load_rows(w, e, o, chunk):
+            raw = raws.tile([P, PACK, H], F32, name=f"raw{chunk}", offset=slot_offset(chunk))
+            nc.sync.dma_start(raw[:], w[e, o * K_PASS : (o + 1) * K_PASS, :].rearrange("(p j) i -> p j i", j=PACK))
+            return raw
+
+        def quantize_first_layer(raw, split):
+            words = codes.tile([P, H], U32, name="w_words", align_bytes=64)
+            scales = codes.tile([P, H], U8, name="w_scales", align_bytes=64)
+            src = raw[:].rearrange("p (jj j2) (m t) -> p m jj t j2", j2=2, t=PACK)
+            if split:
+                parts = [(nc.vector.tensor_copy, 2, 4), (nc.scalar.copy, 0, 2)]
+            else:
+                parts = [(nc.scalar.copy, 0, 4)]
+            staged = []
+            for copy, t0, t1 in parts:
+                grouped = stage.tile([P, (t1 - t0) * K_PASS], BF16, name="grouped", align_bytes=64)
+                copy(grouped[:].rearrange("p (t m jj j2) -> p m jj t j2", t=t1 - t0, jj=2, j2=2), src[:, :, :, t0:t1, :])
+                staged.append((grouped, slice(t0 * P, t1 * P)))
+            for grouped, cols in staged:
+                nc.vector.quantize_mx(out=words[:, cols].bitcast(FP8X4), scales=scales[:, cols], in_=grouped[:])
+            return words, scales
+
+        def first_layer(weights, slot_words, slot_scales, g, tag, order):
+            bank = psum.tile([P, PACK, GROUP], F32, name=tag)
+            cols = slice(g * GROUP, (g + 1) * GROUP)
+            for t in order:
+                for o in range(PASSES):
+                    words, scales = weights[o]
+                    nc.tensor.matmul_mx(
+                        out=bank[:, t, :],
+                        lhsT=words[:, t * P : (t + 1) * P].bitcast(FP8X4),
+                        lhsT_scale=scales[:, t * P : (t + 1) * P],
+                        rhs=slot_words[o][:, cols].bitcast(FP8X4),
+                        rhs_scale=slot_scales[4 * o : P, cols],
+                        start=(o == 0),
+                        stop=(o == PASSES - 1),
+                    )
+            return bank
+
+        token_words = [keep.tile([P, T], I32, name=f"token_words{o}", align_bytes=64) for o in range(PASSES)]
+        gate_rows = gate.rearrange("(nt p) s -> p nt s", p=P)
+
+        def second_layer(e, w2q, hq, chunk):
+            last = e == E - 1
+            entries = offsets[:, e * LIST_COLS : (e + 1) * LIST_COLS]
+            weight = keep.tile([P, N_TILES, C], F32, name=f"gate{e}")
+            nc.sync.dma_start(weight[:], gate_rows[:, :, e * C : (e + 1) * C])
+            for nt in range(N_TILES):
+                rows = slice(nt * P, (nt + 1) * P)
+                y_bank = psum.tile([P, C], F32, name="y_bank", bufs=2)
+                nc.tensor.matmul_mx(
+                    out=y_bank[:],
+                    lhsT=w2q[0][:, rows].bitcast(FP8X4),
+                    lhsT_scale=w2q[1][:, rows],
+                    rhs=hq[0][:].bitcast(FP8X4),
+                    rhs_scale=hq[1][:],
+                    start=True,
+                    stop=True,
+                )
+                y = raws.tile([P, C], F32, name=f"y{e}_{nt}", offset=slot_offset(chunk) + nt * C * 4)
+                nc.scalar.copy(y[:], y_bank[:])
+                nc.vector.tensor_tensor(results[nt][:].indirect(entries), y[:], weight[:, nt, :], MULT)
+                if last:
+                    nc.sync.dma_start(out[rows, :], results[nt][:])
+
+        slot_scales = []
+        slot_words = []
+        pending = None
+        for e in range(E):
+            last = e == E - 1
+
+            w1q = []
+            for o in range(PASSES):
+                raw = load_rows(w1, e, o, 4 * e + o)
+                if e == 0:
+                    if o == 0:
+                        for q in range(4):
+                            nc.sync.dma_start(
+                                token_scales[32 * q : 32 * q + 4 * PASSES, :].bitcast(I32),
+                                x_scales[:, 4 * q : 4 * q + 4, :].bitcast(I32),
+                            )
+                    nc.sync.dma_start(token_words[o][:], x_words[o].rearrange("p t r -> p (t r)").bitcast(I32))
+                w1q.append(quantize_first_layer(raw, False))
+
+            if e == 0:
+                for x in range(E):
+                    entries = offsets[:, x * LIST_COLS : (x + 1) * LIST_COLS]
+                    picked_scales = keep.tile([P, C], U8, name=f"slot_scales{x}", align_bytes=64)
+                    nc.vector.tensor_copy(picked_scales[:], token_scales[:].indirect(entries))
+                    slot_scales.append(picked_scales)
+                    both = []
+                    for o in range(PASSES):
+                        picked = keep.tile([P, C], U32, name=f"slot_words{x}_{o}", align_bytes=64)
+                        nc.vector.tensor_copy(picked[:], token_words[o][:].bitcast(U32).indirect(entries))
+                        both.append(picked)
+                    slot_words.append(both)
+            else:
+                second_layer(e - 1, pending[0], pending[1], 4 * e + 1)
+
+            w3q = [quantize_first_layer(load_rows(w3, e, 0, 4 * e + 2), False)]
+
+            gates_in = []
+            for g in range(GROUPS):
+                bank = first_layer(w1q, slot_words[e], slot_scales[e], g, "a_bank", (0, 1, 2, 3))
+                act = raws.tile([P, GROUP, PACK], F32, name=f"act{e}_{g}", offset=slot_offset(4 * e + 2) + g * GROUP * PACK * 4)
+                nc.scalar.activation(act[:], bank[:].rearrange("p t c -> p c t"), SILU)
+                gates_in.append(act)
+
+            w3q.append(quantize_first_layer(load_rows(w3, e, 1, 4 * e + 3), True))
+
+            raw2 = small.tile([P, PACK, N], F32, name="raw2")
+            nc.sync.dma_start(raw2[:], w2[e].rearrange("(p j) n -> p j n", j=PACK))
+
+            h_words = small.tile([P, C], U32, name="h_words", align_bytes=64)
+            h_scales = small.tile([P, C], U8, name="h_scales", align_bytes=64)
+            hidden = []
+            for g in range(GROUPS):
+                bank = first_layer(w3q, slot_words[e], slot_scales[e], g, "b_bank", (2, 3, 0, 1))
+                h = small.tile([P, GROUP * PACK], BF16, name="h", align_bytes=64)
+                nc.vector.tensor_tensor(
+                    h[:].rearrange("p (c t) -> p c t", t=PACK), bank[:].rearrange("p t c -> p c t"), gates_in[g][:], MULT
+                )
+                hidden.append(h)
+
+            grouped2 = small.tile([P, N * PACK], BF16, name="grouped2", align_bytes=64)
+            copy2 = nc.scalar.copy if last else nc.vector.tensor_copy
+            copy2(
+                grouped2[:].rearrange("p (c i jj j2) -> p c jj i j2", i=4, jj=2, j2=2),
+                raw2[:].rearrange("p (jj j2) (c i) -> p c jj i j2", j2=2, i=4),
+            )
+            w2_words = small.tile([P, N], U32, name="w2_words", align_bytes=64)
+            w2_scales = small.tile([P, N], U8, name="w2_scales", align_bytes=64)
+            nc.vector.quantize_mx(out=w2_words[:].bitcast(FP8X4), scales=w2_scales[:], in_=grouped2[:])
+
+            for g in range(GROUPS):
+                cols = slice(g * GROUP, (g + 1) * GROUP)
+                nc.vector.quantize_mx(out=h_words[:, cols].bitcast(FP8X4), scales=h_scales[:, cols], in_=hidden[g][:])
+            pending = ((w2_words, w2_scales), (h_words, h_scales))
+
+        second_layer(E - 1, pending[0], pending[1], 4 * E - 1)

@@ -33,7 +33,7 @@ def tile_moe_pkd_glu_silu_kernel(tc, x_words, x_scales, w1, w3, w2, gate, offs, 
     with ExitStack() as ctx:
         keep = ctx.enter_context(tc.tile_pool(name="keep", bufs=1))
         raws = ctx.enter_context(tc.tile_pool(name="raws", bufs=1))
-        stage = ctx.enter_context(tc.tile_pool(name="stage", bufs=4))
+        stage = ctx.enter_context(tc.tile_pool(name="stage", bufs=6))
         codes = ctx.enter_context(tc.tile_pool(name="codes", bufs=8))
         small = ctx.enter_context(tc.tile_pool(name="small", bufs=4))
         psum = ctx.enter_context(tc.psum_pool(name="psum", bufs=3))
@@ -42,14 +42,19 @@ def tile_moe_pkd_glu_silu_kernel(tc, x_words, x_scales, w1, w3, w2, gate, offs, 
         nc.sync.dma_start(offsets[:], offs)
 
         token_scales = keep.tile([P, T], U8, name="token_scales", align_bytes=64)
-        nc.vector.memset(token_scales[:].bitcast(I32), 0)
+        nc.gpsimd.memset(token_scales[:].bitcast(I32), 0)
+        for q in range(4):
+            nc.sync.dma_start(
+                token_scales[32 * q : 32 * q + 4 * PASSES, :].bitcast(I32),
+                x_scales[:, 4 * q : 4 * q + 4, :].bitcast(I32),
+            )
         warm_in = keep.tile([P, 8], F32, name="warm_in")
         warm_out = keep.tile([P, 8], F32, name="warm_out")
         nc.vector.memset(warm_in[:], 0.0)
         nc.scalar.activation(warm_out[:], warm_in[:], SILU)
         results = [keep.tile([P, T], F32, name=f"result{nt}") for nt in range(N_TILES)]
         for nt in range(N_TILES):
-            nc.gpsimd.memset(results[nt][:], 0.0)
+            nc.vector.memset(results[nt][:], 0.0)
 
         def slot_offset(chunk):
             return (chunk % RAW_SLOTS) * RAW_BYTES
@@ -127,16 +132,10 @@ def tile_moe_pkd_glu_silu_kernel(tc, x_words, x_scales, w1, w3, w2, gate, offs, 
 
             w1q = []
             for o in range(PASSES):
-                raw = load_rows(w1, e, o, 4 * e + o)
                 if e == 0:
-                    if o == 0:
-                        for q in range(4):
-                            nc.sync.dma_start(
-                                token_scales[32 * q : 32 * q + 4 * PASSES, :].bitcast(I32),
-                                x_scales[:, 4 * q : 4 * q + 4, :].bitcast(I32),
-                            )
                     nc.sync.dma_start(token_words[o][:], x_words[o].rearrange("p t r -> p (t r)").bitcast(I32))
-                w1q.append(quantize_first_layer(raw, False))
+                raw = load_rows(w1, e, o, 4 * e + o)
+                w1q.append(quantize_first_layer(raw, e > 0 and o == 1))
 
             if e == 0:
                 for x in range(E):
@@ -155,17 +154,30 @@ def tile_moe_pkd_glu_silu_kernel(tc, x_words, x_scales, w1, w3, w2, gate, offs, 
 
             w3q = [quantize_first_layer(load_rows(w3, e, 0, 4 * e + 2), False)]
 
+            def load_second():
+                rows2 = small.tile([P, PACK, N], F32, name="raw2")
+                nc.sync.dma_start(rows2[:], w2[e].rearrange("(p j) n -> p j n", j=PACK))
+                return rows2
+
+            if not last:
+                raw2 = load_second()
+            w3q.append(quantize_first_layer(load_rows(w3, e, 1, 4 * e + 3), True))
+            if last:
+                raw2 = load_second()
+
             gates_in = []
             for g in range(GROUPS):
-                bank = first_layer(w1q, slot_words[e], slot_scales[e], g, "a_bank", (0, 1, 2, 3))
-                act = raws.tile([P, GROUP, PACK], F32, name=f"act{e}_{g}", offset=slot_offset(4 * e + 2) + g * GROUP * PACK * 4)
+                bank = first_layer(w1q, slot_words[e], slot_scales[e], g, "a_bank", (2, 3, 0, 1))
+                act = raws.tile([P, GROUP, PACK], F32, name=f"act{e}_{g}", offset=slot_offset(4 * e + 3) + g * GROUP * PACK * 4)
                 nc.scalar.activation(act[:], bank[:].rearrange("p t c -> p c t"), SILU)
                 gates_in.append(act)
 
-            w3q.append(quantize_first_layer(load_rows(w3, e, 1, 4 * e + 3), True))
-
-            raw2 = small.tile([P, PACK, N], F32, name="raw2")
-            nc.sync.dma_start(raw2[:], w2[e].rearrange("(p j) n -> p j n", j=PACK))
+            grouped2 = raws.tile([P, N * PACK], BF16, name=f"grouped2_{e}", align_bytes=64, offset=slot_offset(4 * e + 3) + C * PACK * 4)
+            copy2 = nc.scalar.copy if last else nc.vector.tensor_copy
+            copy2(
+                grouped2[:].rearrange("p (c i jj j2) -> p c jj i j2", i=4, jj=2, j2=2),
+                raw2[:].rearrange("p (jj j2) (c i) -> p c jj i j2", j2=2, i=4),
+            )
 
             h_words = small.tile([P, C], U32, name="h_words", align_bytes=64)
             h_scales = small.tile([P, C], U8, name="h_scales", align_bytes=64)
@@ -178,12 +190,6 @@ def tile_moe_pkd_glu_silu_kernel(tc, x_words, x_scales, w1, w3, w2, gate, offs, 
                 )
                 hidden.append(h)
 
-            grouped2 = small.tile([P, N * PACK], BF16, name="grouped2", align_bytes=64)
-            copy2 = nc.scalar.copy if last else nc.vector.tensor_copy
-            copy2(
-                grouped2[:].rearrange("p (c i jj j2) -> p c jj i j2", i=4, jj=2, j2=2),
-                raw2[:].rearrange("p (jj j2) (c i) -> p c jj i j2", j2=2, i=4),
-            )
             w2_words = small.tile([P, N], U32, name="w2_words", align_bytes=64)
             w2_scales = small.tile([P, N], U8, name="w2_scales", align_bytes=64)
             nc.vector.quantize_mx(out=w2_words[:].bitcast(FP8X4), scales=w2_scales[:], in_=grouped2[:])
@@ -193,4 +199,4 @@ def tile_moe_pkd_glu_silu_kernel(tc, x_words, x_scales, w1, w3, w2, gate, offs, 
                 nc.vector.quantize_mx(out=h_words[:, cols].bitcast(FP8X4), scales=h_scales[:, cols], in_=hidden[g][:])
             pending = ((w2_words, w2_scales), (h_words, h_scales))
 
-        second_layer(E - 1, pending[0], pending[1], 4 * E - 1)
+        second_layer(E - 1, pending[0], pending[1], 4 * E - 2)

@@ -23,8 +23,21 @@ LIST_COLS = C // 16
 GROUP = 128
 GROUPS = C // GROUP
 N_TILES = N // P
-RAW_SLOTS = 12
+LAST = E - 1
+CHUNKS = 2 * PASSES
 RAW_BYTES = PACK * H * 4
+W2_BYTES = PACK * N * 4
+GATE_BYTES = N_TILES * C * 4
+W2_AT = E * CHUNKS * RAW_BYTES
+GATE_AT = W2_AT + E * W2_BYTES
+WORDS_AT = GATE_AT + E * GATE_BYTES
+LOADS_END = WORDS_AT + T * 4
+ACT_BYTES = GROUP * PACK * 4
+GROUPED2_AT = GROUPS * ACT_BYTES
+Y_AT = GROUPED2_AT + N * PACK * 2
+Y_BYTES = C * 4
+BANK = 2048
+SHARED = ((3,), (1, 3), (1, 3), (2, 3))
 
 
 def tile_moe_pkd_glu_silu_kernel(tc, x_words, x_scales, w1, w3, w2, gate, offs, out):
@@ -32,11 +45,11 @@ def tile_moe_pkd_glu_silu_kernel(tc, x_words, x_scales, w1, w3, w2, gate, offs, 
 
     with ExitStack() as ctx:
         keep = ctx.enter_context(tc.tile_pool(name="keep", bufs=1))
-        raws = ctx.enter_context(tc.tile_pool(name="raws", bufs=1))
-        stage = ctx.enter_context(tc.tile_pool(name="stage", bufs=6))
-        codes = ctx.enter_context(tc.tile_pool(name="codes", bufs=8))
-        small = ctx.enter_context(tc.tile_pool(name="small", bufs=4))
-        psum = ctx.enter_context(tc.psum_pool(name="psum", bufs=3))
+        loads = ctx.enter_context(tc.tile_pool(name="loads", bufs=1))
+        stage = ctx.enter_context(tc.tile_pool(name="stage", bufs=4))
+        codes = ctx.enter_context(tc.tile_pool(name="codes", bufs=6))
+        small = ctx.enter_context(tc.tile_pool(name="small", bufs=2))
+        psum = ctx.enter_context(tc.psum_pool(name="psum", bufs=1))
 
         offsets = keep.tile([P, E * LIST_COLS], U16, name="offsets")
         nc.sync.dma_start(offsets[:], offs)
@@ -48,155 +61,161 @@ def tile_moe_pkd_glu_silu_kernel(tc, x_words, x_scales, w1, w3, w2, gate, offs, 
                 token_scales[32 * q : 32 * q + 4 * PASSES, :].bitcast(I32),
                 x_scales[:, 4 * q : 4 * q + 4, :].bitcast(I32),
             )
-        warm_in = keep.tile([P, 8], F32, name="warm_in")
+        warm_in = loads.tile([P, (LOADS_END - RAW_BYTES) // 4], F32, name="warm_in", offset=RAW_BYTES)
         warm_out = keep.tile([P, 8], F32, name="warm_out")
-        nc.vector.memset(warm_in[:], 0.0)
-        nc.scalar.activation(warm_out[:], warm_in[:], SILU)
+        nc.vector.memset(warm_in[:, 0:8], 0.0)
+        nc.scalar.activation(warm_out[:], warm_in[:, 0:8], SILU)
         results = [keep.tile([P, T], F32, name=f"result{nt}") for nt in range(N_TILES)]
         for nt in range(N_TILES):
-            nc.vector.memset(results[nt][:], 0.0)
+            nc.gpsimd.memset(results[nt][:], 0.0)
 
-        def slot_offset(chunk):
-            return (chunk % RAW_SLOTS) * RAW_BYTES
+        token_words = [
+            keep.tile([P, T], I32, name="token_words0", align_bytes=64),
+            loads.tile([P, T], I32, name="token_words1", align_bytes=64, offset=WORDS_AT),
+        ]
+        gate_rows = gate.rearrange("(nt p) s -> p nt s", p=P)
 
-        def load_rows(w, e, o, chunk):
-            raw = raws.tile([P, PACK, H], F32, name=f"raw{chunk}", offset=slot_offset(chunk))
+        def raw_at(e, chunk):
+            return (e * CHUNKS + chunk) * RAW_BYTES
+
+        def entries(e):
+            return offsets[:, e * LIST_COLS : (e + 1) * LIST_COLS]
+
+        def first_layer_codes(e, chunk):
+            w, o = (w1, w3)[chunk // PASSES], chunk % PASSES
+            raw = loads.tile([P, PACK, H], F32, name=f"raw{e}_{chunk}", offset=raw_at(e, chunk))
             nc.sync.dma_start(raw[:], w[e, o * K_PASS : (o + 1) * K_PASS, :].rearrange("(p j) i -> p j i", j=PACK))
-            return raw
-
-        def quantize_first_layer(raw, split):
             words = codes.tile([P, H], U32, name="w_words", align_bytes=64)
             scales = codes.tile([P, H], U8, name="w_scales", align_bytes=64)
             src = raw[:].rearrange("p (jj j2) (m t) -> p m jj t j2", j2=2, t=PACK)
-            if split:
+            if chunk in SHARED[e]:
                 parts = [(nc.vector.tensor_copy, 2, 4), (nc.scalar.copy, 0, 2)]
             else:
                 parts = [(nc.scalar.copy, 0, 4)]
             staged = []
             for copy, t0, t1 in parts:
-                grouped = stage.tile([P, (t1 - t0) * K_PASS], BF16, name="grouped", align_bytes=64)
+                grouped = stage.tile([P, (t1 - t0) * K_PASS], BF16, name=f"grouped{t1 - t0}", align_bytes=64)
                 copy(grouped[:].rearrange("p (t m jj j2) -> p m jj t j2", t=t1 - t0, jj=2, j2=2), src[:, :, :, t0:t1, :])
                 staged.append((grouped, slice(t0 * P, t1 * P)))
             for grouped, cols in staged:
                 nc.vector.quantize_mx(out=words[:, cols].bitcast(FP8X4), scales=scales[:, cols], in_=grouped[:])
             return words, scales
 
-        def first_layer(weights, slot_words, slot_scales, g, tag, order):
-            bank = psum.tile([P, PACK, GROUP], F32, name=tag)
+        def first_layer(weights, e, g, kind, bank_index):
+            bank = psum.tile([P, PACK, GROUP], F32, name=f"{kind}{e}_{g}", offset=bank_index * BANK)
             cols = slice(g * GROUP, (g + 1) * GROUP)
-            for t in order:
+            for t in (2, 3, 0, 1):
                 for o in range(PASSES):
                     words, scales = weights[o]
                     nc.tensor.matmul_mx(
                         out=bank[:, t, :],
                         lhsT=words[:, t * P : (t + 1) * P].bitcast(FP8X4),
                         lhsT_scale=scales[:, t * P : (t + 1) * P],
-                        rhs=slot_words[o][:, cols].bitcast(FP8X4),
-                        rhs_scale=slot_scales[4 * o : P, cols],
+                        rhs=slot_words[e][o][:, cols].bitcast(FP8X4),
+                        rhs_scale=slot_scales[e][4 * o : P, cols],
                         start=(o == 0),
                         stop=(o == PASSES - 1),
                     )
             return bank
 
-        token_words = [keep.tile([P, T], I32, name=f"token_words{o}", align_bytes=64) for o in range(PASSES)]
-        gate_rows = gate.rearrange("(nt p) s -> p nt s", p=P)
+        def load_w2(e):
+            raw2 = loads.tile([P, PACK, N], F32, name=f"raw2_{e}", offset=W2_AT + e * W2_BYTES)
+            nc.sync.dma_start(raw2[:], w2[e].rearrange("(p j) n -> p j n", j=PACK))
+            return raw2
 
-        def second_layer(e, w2q, hq, chunk):
-            last = e == E - 1
-            entries = offsets[:, e * LIST_COLS : (e + 1) * LIST_COLS]
-            weight = keep.tile([P, N_TILES, C], F32, name=f"gate{e}")
+        def load_gate(e):
+            weight = loads.tile([P, N_TILES, C], F32, name=f"gate{e}", offset=GATE_AT + e * GATE_BYTES)
             nc.sync.dma_start(weight[:], gate_rows[:, :, e * C : (e + 1) * C])
-            for nt in range(N_TILES):
-                rows = slice(nt * P, (nt + 1) * P)
-                y_bank = psum.tile([P, C], F32, name="y_bank", bufs=2)
-                nc.tensor.matmul_mx(
-                    out=y_bank[:],
-                    lhsT=w2q[0][:, rows].bitcast(FP8X4),
-                    lhsT_scale=w2q[1][:, rows],
-                    rhs=hq[0][:].bitcast(FP8X4),
-                    rhs_scale=hq[1][:],
-                    start=True,
-                    stop=True,
-                )
-                y = raws.tile([P, C], F32, name=f"y{e}_{nt}", offset=slot_offset(chunk) + nt * C * 4)
-                nc.scalar.copy(y[:], y_bank[:])
-                nc.vector.tensor_tensor(results[nt][:].indirect(entries), y[:], weight[:, nt, :], MULT)
-                if last:
-                    nc.sync.dma_start(out[rows, :], results[nt][:])
+            gates.append(weight)
+
+        def second_layer(e, nt, bank_index, y_at):
+            rows = slice(nt * P, (nt + 1) * P)
+            w2_words, w2_scales, h_words, h_scales = second[e]
+            y_bank = psum.tile([P, C], F32, name=f"y_bank{e}_{nt}", offset=bank_index * BANK)
+            nc.tensor.matmul_mx(
+                out=y_bank[:],
+                lhsT=w2_words[:, rows].bitcast(FP8X4),
+                lhsT_scale=w2_scales[:, rows],
+                rhs=h_words[:].bitcast(FP8X4),
+                rhs_scale=h_scales[:],
+                start=True,
+                stop=True,
+            )
+            y = loads.tile([P, C], F32, name=f"y{e}_{nt}", offset=y_at)
+            nc.scalar.copy(y[:], y_bank[:])
+            nc.vector.tensor_tensor(results[nt][:].indirect(entries(e)), y[:], gates[e][:, nt, :], MULT)
 
         slot_scales = []
         slot_words = []
-        pending = None
+        gates = []
+        second = []
         for e in range(E):
-            last = e == E - 1
-
             w1q = []
             for o in range(PASSES):
                 if e == 0:
                     nc.sync.dma_start(token_words[o][:], x_words[o].rearrange("p t r -> p (t r)").bitcast(I32))
-                raw = load_rows(w1, e, o, 4 * e + o)
-                w1q.append(quantize_first_layer(raw, e > 0 and o == 1))
+                w1q.append(first_layer_codes(e, o))
 
             if e == 0:
                 for x in range(E):
-                    entries = offsets[:, x * LIST_COLS : (x + 1) * LIST_COLS]
                     picked_scales = keep.tile([P, C], U8, name=f"slot_scales{x}", align_bytes=64)
-                    nc.vector.tensor_copy(picked_scales[:], token_scales[:].indirect(entries))
+                    nc.vector.tensor_copy(picked_scales[:], token_scales[:].indirect(entries(x)))
                     slot_scales.append(picked_scales)
                     both = []
                     for o in range(PASSES):
                         picked = keep.tile([P, C], U32, name=f"slot_words{x}_{o}", align_bytes=64)
-                        nc.vector.tensor_copy(picked[:], token_words[o][:].bitcast(U32).indirect(entries))
+                        nc.vector.tensor_copy(picked[:], token_words[o][:].bitcast(U32).indirect(entries(x)))
                         both.append(picked)
                     slot_words.append(both)
-            else:
-                second_layer(e - 1, pending[0], pending[1], 4 * e + 1)
+            elif e < LAST:
+                load_gate(e - 1)
+                for nt in range(N_TILES):
+                    second_layer(e - 1, nt, 6 + nt, raw_at(e, 1) + nt * Y_BYTES)
 
-            w3q = [quantize_first_layer(load_rows(w3, e, 0, 4 * e + 2), False)]
+            w3q = [first_layer_codes(e, 2)]
+            if e < LAST:
+                raw2 = load_w2(e)
+            w3q.append(first_layer_codes(e, 3))
+            if e == LAST:
+                load_gate(e - 1)
+                raw2 = load_w2(e)
+                load_gate(e)
+                second_layer(e - 1, 0, 6, raw_at(e, 3) + Y_AT)
 
-            def load_second():
-                rows2 = small.tile([P, PACK, N], F32, name="raw2")
-                nc.sync.dma_start(rows2[:], w2[e].rearrange("(p j) n -> p j n", j=PACK))
-                return rows2
-
-            if not last:
-                raw2 = load_second()
-            w3q.append(quantize_first_layer(load_rows(w3, e, 1, 4 * e + 3), True))
-            if last:
-                raw2 = load_second()
-
-            gates_in = []
+            acts = []
             for g in range(GROUPS):
-                bank = first_layer(w1q, slot_words[e], slot_scales[e], g, "a_bank", (2, 3, 0, 1))
-                act = raws.tile([P, GROUP, PACK], F32, name=f"act{e}_{g}", offset=slot_offset(4 * e + 3) + g * GROUP * PACK * 4)
+                bank = first_layer(w1q, e, g, "a_bank", (GROUPS * e + g) % 3)
+                act = loads.tile([P, GROUP, PACK], F32, name=f"act{e}_{g}", offset=raw_at(e, 3) + g * ACT_BYTES)
                 nc.scalar.activation(act[:], bank[:].rearrange("p t c -> p c t"), SILU)
-                gates_in.append(act)
+                acts.append(act)
 
-            grouped2 = raws.tile([P, N * PACK], BF16, name=f"grouped2_{e}", align_bytes=64, offset=slot_offset(4 * e + 3) + C * PACK * 4)
-            copy2 = nc.scalar.copy if last else nc.vector.tensor_copy
+            grouped2 = loads.tile([P, N * PACK], BF16, name=f"grouped2_{e}", align_bytes=64, offset=raw_at(e, 3) + GROUPED2_AT)
+            copy2 = nc.scalar.copy if e == LAST else nc.vector.tensor_copy
             copy2(
                 grouped2[:].rearrange("p (c i jj j2) -> p c jj i j2", i=4, jj=2, j2=2),
                 raw2[:].rearrange("p (jj j2) (c i) -> p c jj i j2", j2=2, i=4),
             )
 
-            h_words = small.tile([P, C], U32, name="h_words", align_bytes=64)
-            h_scales = small.tile([P, C], U8, name="h_scales", align_bytes=64)
             hidden = []
             for g in range(GROUPS):
-                bank = first_layer(w3q, slot_words[e], slot_scales[e], g, "b_bank", (2, 3, 0, 1))
-                h = small.tile([P, GROUP * PACK], BF16, name="h", align_bytes=64)
+                bank = first_layer(w3q, e, g, "b_bank", 3 + (GROUPS * e + g) % 3)
+                h = small.tile([P, GROUP * PACK], BF16, name="h", align_bytes=64, bufs=4)
                 nc.vector.tensor_tensor(
-                    h[:].rearrange("p (c t) -> p c t", t=PACK), bank[:].rearrange("p t c -> p c t"), gates_in[g][:], MULT
+                    h[:].rearrange("p (c t) -> p c t", t=PACK), bank[:].rearrange("p t c -> p c t"), acts[g][:], MULT
                 )
                 hidden.append(h)
 
             w2_words = small.tile([P, N], U32, name="w2_words", align_bytes=64)
             w2_scales = small.tile([P, N], U8, name="w2_scales", align_bytes=64)
             nc.vector.quantize_mx(out=w2_words[:].bitcast(FP8X4), scales=w2_scales[:], in_=grouped2[:])
-
+            h_words = small.tile([P, C], U32, name="h_words", align_bytes=64)
+            h_scales = small.tile([P, C], U8, name="h_scales", align_bytes=64)
             for g in range(GROUPS):
                 cols = slice(g * GROUP, (g + 1) * GROUP)
                 nc.vector.quantize_mx(out=h_words[:, cols].bitcast(FP8X4), scales=h_scales[:, cols], in_=hidden[g][:])
-            pending = ((w2_words, w2_scales), (h_words, h_scales))
+            second.append((w2_words, w2_scales, h_words, h_scales))
 
-        second_layer(E - 1, pending[0], pending[1], 4 * E - 2)
+        second_layer(LAST - 1, 1, 3 + (GROUPS * LAST) % 3, raw_at(LAST, 1))
+        for nt in range(N_TILES):
+            second_layer(LAST, nt, 7 - nt, raw_at(LAST, 0) + nt * Y_BYTES)
+            nc.sync.dma_start(out[nt * P : (nt + 1) * P, :], results[nt][:])

@@ -30,14 +30,13 @@ W2_BYTES = PACK * N * 4
 GATE_BYTES = N_TILES * C * 4
 W2_AT = E * CHUNKS * RAW_BYTES
 GATE_AT = W2_AT + E * W2_BYTES
-WORDS_AT = GATE_AT + E * GATE_BYTES
-LOADS_END = WORDS_AT + T * 4
+LOADS_END = GATE_AT + E * GATE_BYTES
 ACT_BYTES = GROUP * PACK * 4
 GROUPED2_AT = GROUPS * ACT_BYTES
 Y_AT = GROUPED2_AT + N * PACK * 2
 Y_BYTES = C * 4
 BANK = 2048
-SHARED = ((3,), (1, 3), (1, 3), (2, 3))
+SHARED = ((3,), (1, 3), (1, 3), (1, 2, 3))
 
 
 def tile_moe_pkd_glu_silu_kernel(tc, x_words, x_scales, w1, w3, w2, gate, offs, out):
@@ -71,7 +70,7 @@ def tile_moe_pkd_glu_silu_kernel(tc, x_words, x_scales, w1, w3, w2, gate, offs, 
 
         token_words = [
             keep.tile([P, T], I32, name="token_words0", align_bytes=64),
-            loads.tile([P, T], I32, name="token_words1", align_bytes=64, offset=WORDS_AT),
+            keep.tile([P, T], I32, name="token_words1", align_bytes=64),
         ]
         gate_rows = gate.rearrange("(nt p) s -> p nt s", p=P)
 
@@ -124,9 +123,9 @@ def tile_moe_pkd_glu_silu_kernel(tc, x_words, x_scales, w1, w3, w2, gate, offs, 
             return raw2
 
         def load_gate(e):
-            weight = loads.tile([P, N_TILES, C], F32, name=f"gate{e}", offset=GATE_AT + e * GATE_BYTES)
-            nc.sync.dma_start(weight[:], gate_rows[:, :, e * C : (e + 1) * C])
-            gates.append(weight)
+            weight = loads.tile([P, N_TILES, 2 * C], F32, name=f"gate{e}", offset=GATE_AT + e * GATE_BYTES)
+            nc.sync.dma_start(weight[:], gate_rows[:, :, e * C : (e + 2) * C])
+            gates.extend([weight[:, :, 0:C], weight[:, :, C : 2 * C]])
 
         def second_layer(e, nt, bank_index, y_at):
             rows = slice(nt * P, (nt + 1) * P)
@@ -168,7 +167,8 @@ def tile_moe_pkd_glu_silu_kernel(tc, x_words, x_scales, w1, w3, w2, gate, offs, 
                         both.append(picked)
                     slot_words.append(both)
             elif e < LAST:
-                load_gate(e - 1)
+                if e == 1:
+                    load_gate(0)
                 for nt in range(N_TILES):
                     second_layer(e - 1, nt, 6 + nt, raw_at(e, 1) + nt * Y_BYTES)
 
@@ -179,7 +179,6 @@ def tile_moe_pkd_glu_silu_kernel(tc, x_words, x_scales, w1, w3, w2, gate, offs, 
             if e == LAST:
                 load_gate(e - 1)
                 raw2 = load_w2(e)
-                load_gate(e)
                 second_layer(e - 1, 0, 6, raw_at(e, 3) + Y_AT)
 
             acts = []

@@ -1,6 +1,7 @@
 from contextlib import ExitStack
 
 import concourse.mybir as mybir
+from concourse.masks import make_identity
 
 K, T, E, C, H, N = 1024, 1280, 4, 256, 512, 256
 FLOPS = 2 * E * C * (2 * K * H + H * N)
@@ -19,6 +20,7 @@ P = 128
 PACK = 4
 K_PASS = P * PACK
 PASSES = K // K_PASS
+SLOTS = E * C
 LIST_COLS = C // 16
 GROUP = 128
 GROUPS = C // GROUP
@@ -27,16 +29,15 @@ LAST = E - 1
 CHUNKS = 2 * PASSES
 RAW_BYTES = PACK * H * 4
 W2_BYTES = PACK * N * 4
-GATE_BYTES = N_TILES * C * 4
 W2_AT = E * CHUNKS * RAW_BYTES
-GATE_AT = W2_AT + E * W2_BYTES
-LOADS_END = GATE_AT + E * GATE_BYTES
+LOADS_END = W2_AT + E * W2_BYTES
 ACT_BYTES = GROUP * PACK * 4
-GROUPED2_AT = GROUPS * ACT_BYTES
-Y_AT = GROUPED2_AT + N * PACK * 2
-Y_BYTES = C * 4
 BANK = 2048
-SHARED = ((3,), (1, 3), (1, 3), (1, 2, 3))
+BANK_COLS = 512
+GATE_COLS = SLOTS // P
+GATHER = 2 * C
+HALF = H // 2
+PIECES = (0, 224, 448, 608, 768)
 
 
 def tile_moe_pkd_glu_silu_kernel(tc, x_words, x_scales, w1, w3, w2, gate, offs, out):
@@ -45,34 +46,60 @@ def tile_moe_pkd_glu_silu_kernel(tc, x_words, x_scales, w1, w3, w2, gate, offs, 
     with ExitStack() as ctx:
         keep = ctx.enter_context(tc.tile_pool(name="keep", bufs=1))
         loads = ctx.enter_context(tc.tile_pool(name="loads", bufs=1))
-        stage = ctx.enter_context(tc.tile_pool(name="stage", bufs=4))
-        codes = ctx.enter_context(tc.tile_pool(name="codes", bufs=6))
+        stage = ctx.enter_context(tc.tile_pool(name="stage", bufs=8))
+        codes = ctx.enter_context(tc.tile_pool(name="codes", bufs=12))
         small = ctx.enter_context(tc.tile_pool(name="small", bufs=2))
         psum = ctx.enter_context(tc.psum_pool(name="psum", bufs=1))
 
         offsets = keep.tile([P, E * LIST_COLS], U16, name="offsets")
         nc.sync.dma_start(offsets[:], offs)
+        gate_row = keep.tile([P, GATE_COLS], F32, name="gate_row")
+        nc.sync.dma_start(gate_row[:], gate[0:1, :].rearrange("o (p m) -> (o p) m", m=GATE_COLS))
 
         token_scales = keep.tile([P, T], U8, name="token_scales", align_bytes=64)
         nc.gpsimd.memset(token_scales[:].bitcast(I32), 0)
+        holder = loads.tile([P, (LOADS_END - RAW_BYTES) // 4], F32, name="holder", offset=RAW_BYTES)
+        identity = holder[:, 0:P]
+        make_identity(nc, identity)
+        warm_out = keep.tile([P, 8], F32, name="warm_out")
+        nc.scalar.activation(warm_out[:], holder[:, 0:8], SILU)
+        results = [keep.tile([P, T], F32, name=f"result{nt}") for nt in range(N_TILES)]
+        for nt in range(N_TILES):
+            nc.gpsimd.memset(results[nt][:], 0.0)
+
+        token_words = []
+        for o in range(PASSES):
+            words = keep.tile([P, T], I32, name=f"token_words{o}", align_bytes=64)
+            nc.sync.dma_start(words[:], x_words[o].rearrange("p t r -> p (t r)").bitcast(I32))
+            token_words.append(words)
         for q in range(4):
             nc.sync.dma_start(
                 token_scales[32 * q : 32 * q + 4 * PASSES, :].bitcast(I32),
                 x_scales[:, 4 * q : 4 * q + 4, :].bitcast(I32),
             )
-        warm_in = loads.tile([P, (LOADS_END - RAW_BYTES) // 4], F32, name="warm_in", offset=RAW_BYTES)
-        warm_out = keep.tile([P, 8], F32, name="warm_out")
-        nc.vector.memset(warm_in[:, 0:8], 0.0)
-        nc.scalar.activation(warm_out[:], warm_in[:, 0:8], SILU)
-        results = [keep.tile([P, T], F32, name=f"result{nt}") for nt in range(N_TILES)]
-        for nt in range(N_TILES):
-            nc.gpsimd.memset(results[nt][:], 0.0)
 
-        token_words = [
-            keep.tile([P, T], I32, name="token_words0", align_bytes=64),
-            keep.tile([P, T], I32, name="token_words1", align_bytes=64),
-        ]
-        gate_rows = gate.rearrange("(nt p) s -> p nt s", p=P)
+        gates = keep.tile([P, P, GATE_COLS], F32, name="gates")
+        for half in range(GATE_COLS // PACK):
+            bank = psum.tile([P, PACK, P], F32, name=f"gate_bank{half}", offset=(6 + half) * BANK)
+            for m in range(PACK):
+                col = half * PACK + m
+                nc.tensor.transpose(bank[:, m, :], gate_row[:, col : col + 1].to_broadcast([P, P]), identity)
+            nc.scalar.copy(gates[:, :, half * PACK : (half + 1) * PACK], bank[:].rearrange("p m n -> p n m"))
+        gate_flat = gates[:].rearrange("p n m -> p (n m)")
+
+        slot_words = [[], []]
+        slot_scales = []
+        for o in range(PASSES):
+            for x in range(SLOTS // GATHER):
+                picked = keep.tile([P, GATHER], U32, name=f"slot_words{x}_{o}", align_bytes=64)
+                part = offsets[:, x * GATHER // 16 : (x + 1) * GATHER // 16]
+                nc.vector.tensor_copy(picked[:], token_words[o][:].bitcast(U32).indirect(part))
+                slot_words[o].append(picked)
+        for x in range(SLOTS // GATHER):
+            picked = keep.tile([P, GATHER], U8, name=f"slot_scales{x}", align_bytes=64)
+            part = offsets[:, x * GATHER // 16 : (x + 1) * GATHER // 16]
+            nc.vector.tensor_copy(picked[:], token_scales[:].indirect(part))
+            slot_scales.append(picked)
 
         def raw_at(e, chunk):
             return (e * CHUNKS + chunk) * RAW_BYTES
@@ -80,38 +107,44 @@ def tile_moe_pkd_glu_silu_kernel(tc, x_words, x_scales, w1, w3, w2, gate, offs, 
         def entries(e):
             return offsets[:, e * LIST_COLS : (e + 1) * LIST_COLS]
 
-        def first_layer_codes(e, chunk):
-            w, o = (w1, w3)[chunk // PASSES], chunk % PASSES
+        def first_layer_codes(e, chunk, w, o, copies):
             raw = loads.tile([P, PACK, H], F32, name=f"raw{e}_{chunk}", offset=raw_at(e, chunk))
             nc.sync.dma_start(raw[:], w[e, o * K_PASS : (o + 1) * K_PASS, :].rearrange("(p j) i -> p j i", j=PACK))
-            words = codes.tile([P, H], U32, name="w_words", align_bytes=64)
-            scales = codes.tile([P, H], U8, name="w_scales", align_bytes=64)
-            src = raw[:].rearrange("p (jj j2) (m t) -> p m jj t j2", j2=2, t=PACK)
-            if chunk in SHARED[e]:
-                parts = [(nc.vector.tensor_copy, 2, 4), (nc.scalar.copy, 0, 2)]
-            else:
-                parts = [(nc.scalar.copy, 0, 4)]
+            src = raw[:].rearrange("p j (a u r v) -> p u a j r v", u=2, r=2, v=2)
             staged = []
-            for copy, t0, t1 in parts:
-                grouped = stage.tile([P, (t1 - t0) * K_PASS], BF16, name=f"grouped{t1 - t0}", align_bytes=64)
-                copy(grouped[:].rearrange("p (t m jj j2) -> p m jj t j2", t=t1 - t0, jj=2, j2=2), src[:, :, :, t0:t1, :])
-                staged.append((grouped, slice(t0 * P, t1 * P)))
-            for grouped, cols in staged:
-                nc.vector.quantize_mx(out=words[:, cols].bitcast(FP8X4), scales=scales[:, cols], in_=grouped[:])
+            for half in range(2):
+                grouped = stage.tile([P, 2 * K_PASS], BF16, name="grouped", align_bytes=64)
+                copies[half](
+                    grouped[:].rearrange("p (v a r j) -> p a j r v", v=2, r=2, j=PACK),
+                    src[:, half, :, :, :, :],
+                )
+                staged.append(grouped)
+            return staged
+
+        def quantised(grouped, name=None, at=None):
+            if at is None:
+                words = codes.tile([P, HALF], U32, name="w_words", align_bytes=64)
+            else:
+                words = loads.tile([P, HALF], U32, name=name, align_bytes=64, offset=at)
+            scales = codes.tile([P, HALF], U8, name="w_scales", align_bytes=64)
+            nc.vector.quantize_mx(out=words[:].bitcast(FP8X4), scales=scales[:], in_=grouped[:])
             return words, scales
 
         def first_layer(weights, e, g, kind, bank_index):
             bank = psum.tile([P, PACK, GROUP], F32, name=f"{kind}{e}_{g}", offset=bank_index * BANK)
-            cols = slice(g * GROUP, (g + 1) * GROUP)
-            for t in (2, 3, 0, 1):
+            first = (e * C + g * GROUP) % GATHER
+            cols = slice(first, first + GROUP)
+            x = e * C // GATHER
+            for t in range(PACK):
+                part = slice(t % 2 * P, (t % 2 + 1) * P)
                 for o in range(PASSES):
-                    words, scales = weights[o]
+                    words, scales = weights[o][t // 2]
                     nc.tensor.matmul_mx(
                         out=bank[:, t, :],
-                        lhsT=words[:, t * P : (t + 1) * P].bitcast(FP8X4),
-                        lhsT_scale=scales[:, t * P : (t + 1) * P],
-                        rhs=slot_words[e][o][:, cols].bitcast(FP8X4),
-                        rhs_scale=slot_scales[e][4 * o : P, cols],
+                        lhsT=words[:, part].bitcast(FP8X4),
+                        lhsT_scale=scales[:, part],
+                        rhs=slot_words[o][x][:, cols].bitcast(FP8X4),
+                        rhs_scale=slot_scales[x][4 * o : P, cols],
                         start=(o == 0),
                         stop=(o == PASSES - 1),
                     )
@@ -119,102 +152,100 @@ def tile_moe_pkd_glu_silu_kernel(tc, x_words, x_scales, w1, w3, w2, gate, offs, 
 
         def load_w2(e):
             raw2 = loads.tile([P, PACK, N], F32, name=f"raw2_{e}", offset=W2_AT + e * W2_BYTES)
-            nc.sync.dma_start(raw2[:], w2[e].rearrange("(p j) n -> p j n", j=PACK))
+            rows = w2[e].rearrange("(a u r v) n -> u a r (v n)", u=2, r=2, v=2)
+            for u in range(2):
+                nc.sync.dma_start(raw2[:, 2 * u : 2 * u + 2, :].rearrange("p v n -> p (v n)"), rows[u])
             return raw2
 
-        def load_gate(e):
-            weight = loads.tile([P, N_TILES, 2 * C], F32, name=f"gate{e}", offset=GATE_AT + e * GATE_BYTES)
-            nc.sync.dma_start(weight[:], gate_rows[:, :, e * C : (e + 2) * C])
-            gates.extend([weight[:, :, 0:C], weight[:, :, C : 2 * C]])
-
-        def second_layer(e, nt, bank_index, y_at):
-            rows = slice(nt * P, (nt + 1) * P)
-            w2_words, w2_scales, h_words, h_scales = second[e]
-            y_bank = psum.tile([P, C], F32, name=f"y_bank{e}_{nt}", offset=bank_index * BANK)
-            nc.tensor.matmul_mx(
-                out=y_bank[:],
-                lhsT=w2_words[:, rows].bitcast(FP8X4),
-                lhsT_scale=w2_scales[:, rows],
-                rhs=h_words[:].bitcast(FP8X4),
-                rhs_scale=h_scales[:],
-                start=True,
-                stop=True,
-            )
-            y = loads.tile([P, C], F32, name=f"y{e}_{nt}", offset=y_at)
-            nc.scalar.copy(y[:], y_bank[:])
-            nc.vector.tensor_tensor(results[nt][:].indirect(entries(e)), y[:], gates[e][:, nt, :], MULT)
-
-        slot_scales = []
-        slot_words = []
-        gates = []
-        second = []
-        for e in range(E):
-            w1q = []
-            for o in range(PASSES):
-                if e == 0:
-                    nc.sync.dma_start(token_words[o][:], x_words[o].rearrange("p t r -> p (t r)").bitcast(I32))
-                w1q.append(first_layer_codes(e, o))
-
-            if e == 0:
-                for x in range(E):
-                    picked_scales = keep.tile([P, C], U8, name=f"slot_scales{x}", align_bytes=64)
-                    nc.vector.tensor_copy(picked_scales[:], token_scales[:].indirect(entries(x)))
-                    slot_scales.append(picked_scales)
-                    both = []
-                    for o in range(PASSES):
-                        picked = keep.tile([P, C], U32, name=f"slot_words{x}_{o}", align_bytes=64)
-                        nc.vector.tensor_copy(picked[:], token_words[o][:].bitcast(U32).indirect(entries(x)))
-                        both.append(picked)
-                    slot_words.append(both)
-            elif e < LAST:
-                if e == 1:
-                    load_gate(0)
-                for nt in range(N_TILES):
-                    second_layer(e - 1, nt, 6 + nt, raw_at(e, 1) + nt * Y_BYTES)
-
-            w3q = [first_layer_codes(e, 2)]
-            if e < LAST:
-                raw2 = load_w2(e)
-            w3q.append(first_layer_codes(e, 3))
-            if e == LAST:
-                load_gate(e - 1)
-                raw2 = load_w2(e)
-                second_layer(e - 1, 0, 6, raw_at(e, 3) + Y_AT)
-
-            acts = []
-            for g in range(GROUPS):
-                bank = first_layer(w1q, e, g, "a_bank", (GROUPS * e + g) % 3)
-                act = loads.tile([P, GROUP, PACK], F32, name=f"act{e}_{g}", offset=raw_at(e, 3) + g * ACT_BYTES)
-                nc.scalar.activation(act[:], bank[:].rearrange("p t c -> p c t"), SILU)
-                acts.append(act)
-
-            grouped2 = loads.tile([P, N * PACK], BF16, name=f"grouped2_{e}", align_bytes=64, offset=raw_at(e, 3) + GROUPED2_AT)
-            copy2 = nc.scalar.copy if e == LAST else nc.vector.tensor_copy
-            copy2(
+        def second_cast(e, raw2, copy):
+            grouped2 = stage.tile([P, N * PACK], BF16, name="grouped", align_bytes=64)
+            copy(
                 grouped2[:].rearrange("p (c i jj j2) -> p c jj i j2", i=4, jj=2, j2=2),
                 raw2[:].rearrange("p (jj j2) (c i) -> p c jj i j2", j2=2, i=4),
             )
+            return grouped2
+
+        def second_codes(e, grouped2):
+            w2_words = loads.tile([P, N], U32, name=f"w2_words{e}", align_bytes=64, offset=raw_at(e, 2))
+            w2_scales = small.tile([P, N], U8, name="w2_scales", align_bytes=64)
+            nc.vector.quantize_mx(out=w2_words[:].bitcast(FP8X4), scales=w2_scales[:], in_=grouped2[:])
+            return w2_words, w2_scales
+
+        def put_back(e, nt, y_bank, y_at):
+            y = loads.tile([P, C], F32, name=f"y{e}_{nt}", offset=y_at)
+            nc.scalar.copy(y[:], y_bank[:])
+            nc.vector.tensor_tensor(results[nt][:].indirect(entries(e)), y[:], gate_flat[:, e * C : (e + 1) * C], MULT)
+
+        def put_back_piece(index, y_at):
+            first, end = PIECES[index], PIECES[index + 1]
+            y = loads.tile([P, end - first], F32, name=f"piece{index}", offset=y_at)
+            for owner in range(first // C, (end - 1) // C + 1):
+                lo, hi = max(first, owner * C), min(end, (owner + 1) * C)
+                nc.scalar.copy(y[:, lo - first : hi - first], y_banks[owner][1][:, lo - owner * C : hi - owner * C])
+            part = offsets[:, first // 16 : end // 16]
+            nc.vector.tensor_tensor(results[1][:].indirect(part), y[:], gate_flat[:, first:end], MULT)
+
+        y_banks = []
+        for e in range(E):
+            on_scalar = (nc.scalar.copy, nc.scalar.copy)
+            on_vector = (nc.vector.tensor_copy, nc.vector.tensor_copy)
+            w1q = [[quantised(part) for part in first_layer_codes(e, 0, w1, 0, on_scalar)]]
+            if e > 0:
+                put_back(e - 1, 0, y_banks[e - 1][0], raw_at(e, 0))
+            w1q.append([quantised(part) for part in first_layer_codes(e, 1, w1, 1, on_scalar)])
+            staged0 = first_layer_codes(e, 2, w3, 0, on_scalar)
+            lower0 = quantised(staged0[0])
+            staged1 = first_layer_codes(e, 3, w3, 1, on_vector)
+            lower1 = quantised(staged1[0])
+            upper0 = quantised(staged0[1], f"upper0_{e}", raw_at(e, 3))
+            upper1 = quantised(staged1[1])
+            w3q = [[lower0, upper0], [lower1, upper1]]
+            raw2 = load_w2(e)
+
+            acts = []
+            for g in range(GROUPS):
+                bank = first_layer(w1q, e, g, "a_bank", g)
+                act = loads.tile([P, GROUP, PACK], F32, name=f"act{e}_{g}", offset=raw_at(e, 2) + g * ACT_BYTES)
+                nc.scalar.activation(act[:], bank[:].rearrange("p t c -> p c t"), SILU)
+                acts.append(act)
+                if e > 0 and g == 0:
+                    put_back_piece(e - 1, raw_at(e, 2) + GROUPS * ACT_BYTES)
+            grouped2 = second_cast(e, raw2, nc.scalar.copy)
 
             hidden = []
             for g in range(GROUPS):
-                bank = first_layer(w3q, e, g, "b_bank", 3 + (GROUPS * e + g) % 3)
+                bank = first_layer(w3q, e, g, "b_bank", 2 + g)
                 h = small.tile([P, GROUP * PACK], BF16, name="h", align_bytes=64, bufs=4)
                 nc.vector.tensor_tensor(
                     h[:].rearrange("p (c t) -> p c t", t=PACK), bank[:].rearrange("p t c -> p c t"), acts[g][:], MULT
                 )
                 hidden.append(h)
+            w2_words, w2_scales = second_codes(e, grouped2)
 
-            w2_words = small.tile([P, N], U32, name="w2_words", align_bytes=64)
-            w2_scales = small.tile([P, N], U8, name="w2_scales", align_bytes=64)
-            nc.vector.quantize_mx(out=w2_words[:].bitcast(FP8X4), scales=w2_scales[:], in_=grouped2[:])
             h_words = small.tile([P, C], U32, name="h_words", align_bytes=64)
             h_scales = small.tile([P, C], U8, name="h_scales", align_bytes=64)
             for g in range(GROUPS):
                 cols = slice(g * GROUP, (g + 1) * GROUP)
                 nc.vector.quantize_mx(out=h_words[:, cols].bitcast(FP8X4), scales=h_scales[:, cols], in_=hidden[g][:])
-            second.append((w2_words, w2_scales, h_words, h_scales))
 
-        second_layer(LAST - 1, 1, 3 + (GROUPS * LAST) % 3, raw_at(LAST, 1))
+            if e == LAST:
+                put_back_piece(LAST, raw_at(e, 2) + ACT_BYTES)
+            banks = []
+            for nt in range(N_TILES):
+                rows = slice(nt * P, (nt + 1) * P)
+                y_bank = psum.tile([P, C], F32, name=f"y_bank{e}_{nt}", offset=(4 + nt * (1 + e % 3)) * BANK)
+                nc.tensor.matmul_mx(
+                    out=y_bank[:],
+                    lhsT=w2_words[:, rows].bitcast(FP8X4),
+                    lhsT_scale=w2_scales[:, rows],
+                    rhs=h_words[:].bitcast(FP8X4),
+                    rhs_scale=h_scales[:],
+                    start=True,
+                    stop=True,
+                )
+                banks.append(y_bank)
+            y_banks.append(banks)
+
         for nt in range(N_TILES):
-            second_layer(LAST, nt, 7 - nt, raw_at(LAST, 0) + nt * Y_BYTES)
+            put_back(LAST, nt, y_banks[LAST][nt], raw_at(LAST, 1) + nt * C * 4)
             nc.sync.dma_start(out[nt * P : (nt + 1) * P, :], results[nt][:])

@@ -59,7 +59,9 @@ def tile_moe_pkd_glu_silu_kernel(tc, x_words, x_scales, w1, w3, w2, gate, offs, 
         token_scales = keep.tile([P, T], U8, name="token_scales", align_bytes=64)
         nc.gpsimd.memset(token_scales[:].bitcast(I32), 0)
         holder = loads.tile([P, (LOADS_END - RAW_BYTES) // 4], F32, name="holder", offset=RAW_BYTES)
-        identity = holder[:, 0:P]
+        nc.vector.memset(holder[:, 0:8], 0.0)
+        identity_tile = keep.tile([P, P], F32, name="identity")
+        identity = identity_tile[:]
         make_identity(nc, identity)
         warm_out = keep.tile([P, 8], F32, name="warm_out")
         nc.scalar.activation(warm_out[:], holder[:, 0:8], SILU)
@@ -165,8 +167,8 @@ def tile_moe_pkd_glu_silu_kernel(tc, x_words, x_scales, w1, w3, w2, gate, offs, 
             )
             return grouped2
 
-        def second_codes(e, grouped2):
-            w2_words = loads.tile([P, N], U32, name=f"w2_words{e}", align_bytes=64, offset=raw_at(e, 2))
+        def second_codes(e, grouped2, at):
+            w2_words = loads.tile([P, N], U32, name=f"w2_words{e}", align_bytes=64, offset=at)
             w2_scales = small.tile([P, N], U8, name="w2_scales", align_bytes=64)
             nc.vector.quantize_mx(out=w2_words[:].bitcast(FP8X4), scales=w2_scales[:], in_=grouped2[:])
             return w2_words, w2_scales
@@ -189,9 +191,13 @@ def tile_moe_pkd_glu_silu_kernel(tc, x_words, x_scales, w1, w3, w2, gate, offs, 
         for e in range(E):
             on_scalar = (nc.scalar.copy, nc.scalar.copy)
             on_vector = (nc.vector.tensor_copy, nc.vector.tensor_copy)
-            w1q = [[quantised(part) for part in first_layer_codes(e, 0, w1, 0, on_scalar)]]
+            staged = first_layer_codes(e, 0, w1, 0, on_scalar)
+            lower = quantised(staged[0])
             if e > 0:
-                put_back(e - 1, 0, y_banks[e - 1][0], raw_at(e, 0))
+                weighted = small.tile([P, C], F32, name="weighted")
+                nc.vector.tensor_tensor(weighted[:], y_banks[e - 1][0][:], gate_flat[:, (e - 1) * C : e * C], MULT)
+                nc.vector.tensor_copy(results[0][:].indirect(entries(e - 1)), weighted[:])
+            w1q = [[lower, quantised(staged[1])]]
             w1q.append([quantised(part) for part in first_layer_codes(e, 1, w1, 1, on_scalar)])
             staged0 = first_layer_codes(e, 2, w3, 0, on_scalar)
             lower0 = quantised(staged0[0])
@@ -201,35 +207,36 @@ def tile_moe_pkd_glu_silu_kernel(tc, x_words, x_scales, w1, w3, w2, gate, offs, 
             upper1 = quantised(staged1[1])
             w3q = [[lower0, upper0], [lower1, upper1]]
             raw2 = load_w2(e)
+            if e > 0:
+                put_back_piece(e - 1, raw_at(e, 2))
+            if e < LAST:
+                grouped2 = second_cast(e, raw2, nc.scalar.copy)
+                acts_at = W2_AT + e * W2_BYTES
+            else:
+                acts_at = raw_at(e, 2) + ACT_BYTES
 
             acts = []
             for g in range(GROUPS):
                 bank = first_layer(w1q, e, g, "a_bank", g)
-                act = loads.tile([P, GROUP, PACK], F32, name=f"act{e}_{g}", offset=raw_at(e, 2) + g * ACT_BYTES)
+                act = loads.tile([P, GROUP, PACK], F32, name=f"act{e}_{g}", offset=acts_at + g * ACT_BYTES)
                 nc.scalar.activation(act[:], bank[:].rearrange("p t c -> p c t"), SILU)
                 acts.append(act)
-                if e > 0 and g == 0:
-                    put_back_piece(e - 1, raw_at(e, 2) + GROUPS * ACT_BYTES)
-            grouped2 = second_cast(e, raw2, nc.scalar.copy)
+            if e == LAST:
+                grouped2 = second_cast(e, raw2, nc.scalar.copy)
 
-            hidden = []
+            h = small.tile([P, C * PACK], BF16, name="h", align_bytes=64)
             for g in range(GROUPS):
                 bank = first_layer(w3q, e, g, "b_bank", 2 + g)
-                h = small.tile([P, GROUP * PACK], BF16, name="h", align_bytes=64, bufs=4)
-                nc.vector.tensor_tensor(
-                    h[:].rearrange("p (c t) -> p c t", t=PACK), bank[:].rearrange("p t c -> p c t"), acts[g][:], MULT
-                )
-                hidden.append(h)
-            w2_words, w2_scales = second_codes(e, grouped2)
+                part = h[:, g * GROUP * PACK : (g + 1) * GROUP * PACK].rearrange("p (c t) -> p c t", t=PACK)
+                nc.vector.tensor_tensor(part, bank[:].rearrange("p t c -> p c t"), acts[g][:], MULT)
+            w2_words, w2_scales = second_codes(e, grouped2, acts_at)
 
             h_words = small.tile([P, C], U32, name="h_words", align_bytes=64)
             h_scales = small.tile([P, C], U8, name="h_scales", align_bytes=64)
-            for g in range(GROUPS):
-                cols = slice(g * GROUP, (g + 1) * GROUP)
-                nc.vector.quantize_mx(out=h_words[:, cols].bitcast(FP8X4), scales=h_scales[:, cols], in_=hidden[g][:])
+            nc.vector.quantize_mx(out=h_words[:].bitcast(FP8X4), scales=h_scales[:], in_=h[:])
 
             if e == LAST:
-                put_back_piece(LAST, raw_at(e, 2) + ACT_BYTES)
+                put_back_piece(LAST, acts_at + ACT_BYTES)
             banks = []
             for nt in range(N_TILES):
                 rows = slice(nt * P, (nt + 1) * P)

@@ -37,6 +37,7 @@ BANK_COLS = 512
 GATE_COLS = SLOTS // P
 GATHER = 2 * C
 HALF = H // 2
+OCTETS = H // 8
 PIECES = (0, 224, 448, 608, 768)
 
 
@@ -51,10 +52,13 @@ def tile_moe_pkd_glu_silu_kernel(tc, x_words, x_scales, w1, w3, w2, gate, offs, 
         small = ctx.enter_context(tc.tile_pool(name="small", bufs=2))
         psum = ctx.enter_context(tc.psum_pool(name="psum", bufs=1))
 
+        token_words = [keep.tile([P, T], I32, name=f"token_words{o}", align_bytes=64) for o in range(PASSES)]
+        nc.sync.dma_start(token_words[0][:], x_words[0].rearrange("p t r -> p (t r)").bitcast(I32))
         offsets = keep.tile([P, E * LIST_COLS], U16, name="offsets")
         nc.sync.dma_start(offsets[:], offs)
         gate_row = keep.tile([P, GATE_COLS], F32, name="gate_row")
         nc.sync.dma_start(gate_row[:], gate[0:1, :].rearrange("o (p m) -> (o p) m", m=GATE_COLS))
+        nc.sync.dma_start(token_words[1][:], x_words[1].rearrange("p t r -> p (t r)").bitcast(I32))
 
         token_scales = keep.tile([P, T], U8, name="token_scales", align_bytes=64)
         nc.gpsimd.memset(token_scales[:].bitcast(I32), 0)
@@ -69,11 +73,6 @@ def tile_moe_pkd_glu_silu_kernel(tc, x_words, x_scales, w1, w3, w2, gate, offs, 
         for nt in range(N_TILES):
             nc.gpsimd.memset(results[nt][:], 0.0)
 
-        token_words = []
-        for o in range(PASSES):
-            words = keep.tile([P, T], I32, name=f"token_words{o}", align_bytes=64)
-            nc.sync.dma_start(words[:], x_words[o].rearrange("p t r -> p (t r)").bitcast(I32))
-            token_words.append(words)
         for q in range(4):
             nc.sync.dma_start(
                 token_scales[32 * q : 32 * q + 4 * PASSES, :].bitcast(I32),
@@ -109,17 +108,19 @@ def tile_moe_pkd_glu_silu_kernel(tc, x_words, x_scales, w1, w3, w2, gate, offs, 
         def entries(e):
             return offsets[:, e * LIST_COLS : (e + 1) * LIST_COLS]
 
-        def first_layer_codes(e, chunk, w, o, copies):
+        def first_layer_codes(e, chunk, w, o, scalar_share):
             raw = loads.tile([P, PACK, H], F32, name=f"raw{e}_{chunk}", offset=raw_at(e, chunk))
             nc.sync.dma_start(raw[:], w[e, o * K_PASS : (o + 1) * K_PASS, :].rearrange("(p j) i -> p j i", j=PACK))
-            src = raw[:].rearrange("p j (a u r v) -> p u a j r v", u=2, r=2, v=2)
+            src = raw[:].rearrange("p j (a u r v) -> p u a j v r", u=2, r=2, v=2)
             staged = []
             for half in range(2):
                 grouped = stage.tile([P, 2 * K_PASS], BF16, name="grouped", align_bytes=64)
-                copies[half](
-                    grouped[:].rearrange("p (v a r j) -> p a j r v", v=2, r=2, j=PACK),
-                    src[:, half, :, :, :, :],
-                )
+                dst = grouped[:].rearrange("p (v a r j) -> p a j v r", v=2, r=2, j=PACK)
+                cut = scalar_share[half]
+                if cut > 0:
+                    nc.scalar.copy(dst[:, 0:cut, :, :, :], src[:, half, 0:cut, :, :, :])
+                if cut < OCTETS:
+                    nc.vector.tensor_copy(dst[:, cut:OCTETS, :, :, :], src[:, half, cut:OCTETS, :, :, :])
                 staged.append(grouped)
             return staged
 
@@ -189,8 +190,9 @@ def tile_moe_pkd_glu_silu_kernel(tc, x_words, x_scales, w1, w3, w2, gate, offs, 
 
         y_banks = []
         for e in range(E):
-            on_scalar = (nc.scalar.copy, nc.scalar.copy)
-            on_vector = (nc.vector.tensor_copy, nc.vector.tensor_copy)
+            on_scalar = (OCTETS, OCTETS)
+            on_vector = (0, 0)
+            shared = (OCTETS, OCTETS // 2 if e > 0 else 0)
             staged = first_layer_codes(e, 0, w1, 0, on_scalar)
             lower = quantised(staged[0])
             if e > 0:
@@ -198,7 +200,7 @@ def tile_moe_pkd_glu_silu_kernel(tc, x_words, x_scales, w1, w3, w2, gate, offs, 
                 nc.vector.tensor_tensor(weighted[:], y_banks[e - 1][0][:], gate_flat[:, (e - 1) * C : e * C], MULT)
                 nc.vector.tensor_copy(results[0][:].indirect(entries(e - 1)), weighted[:])
             w1q = [[lower, quantised(staged[1])]]
-            w1q.append([quantised(part) for part in first_layer_codes(e, 1, w1, 1, on_scalar)])
+            w1q.append([quantised(part) for part in first_layer_codes(e, 1, w1, 1, shared)])
             staged0 = first_layer_codes(e, 2, w3, 0, on_scalar)
             lower0 = quantised(staged0[0])
             staged1 = first_layer_codes(e, 3, w3, 1, on_vector)
@@ -209,7 +211,10 @@ def tile_moe_pkd_glu_silu_kernel(tc, x_words, x_scales, w1, w3, w2, gate, offs, 
             raw2 = load_w2(e)
             if e > 0:
                 put_back_piece(e - 1, raw_at(e, 2))
-            if e < LAST:
+            if e == 0:
+                grouped2 = second_cast(e, raw2, nc.vector.tensor_copy)
+                acts_at = raw_at(e, 2)
+            elif e < LAST:
                 grouped2 = second_cast(e, raw2, nc.scalar.copy)
                 acts_at = W2_AT + e * W2_BYTES
             else:

@@ -52,23 +52,19 @@ def tile_moe_pkd_glu_silu_kernel(tc, x_words, x_scales, w1, w3, w2, gate, offs, 
         small = ctx.enter_context(tc.tile_pool(name="small", bufs=2))
         psum = ctx.enter_context(tc.psum_pool(name="psum", bufs=1))
 
+        gate_row = keep.tile([P, GATE_COLS], F32, name="gate_row")
+        nc.sync.dma_start(gate_row[:], gate[0:1, :].rearrange("o (p m) -> (o p) m", m=GATE_COLS))
         token_words = [keep.tile([P, T], I32, name=f"token_words{o}", align_bytes=64) for o in range(PASSES)]
         nc.sync.dma_start(token_words[0][:], x_words[0].rearrange("p t r -> p (t r)").bitcast(I32))
         offsets = keep.tile([P, E * LIST_COLS], U16, name="offsets")
         nc.sync.dma_start(offsets[:], offs)
-        gate_row = keep.tile([P, GATE_COLS], F32, name="gate_row")
-        nc.sync.dma_start(gate_row[:], gate[0:1, :].rearrange("o (p m) -> (o p) m", m=GATE_COLS))
         nc.sync.dma_start(token_words[1][:], x_words[1].rearrange("p t r -> p (t r)").bitcast(I32))
 
         token_scales = keep.tile([P, T], U8, name="token_scales", align_bytes=64)
         nc.gpsimd.memset(token_scales[:].bitcast(I32), 0)
         holder = loads.tile([P, (LOADS_END - RAW_BYTES) // 4], F32, name="holder", offset=RAW_BYTES)
-        nc.vector.memset(holder[:, 0:8], 0.0)
-        identity_tile = keep.tile([P, P], F32, name="identity")
-        identity = identity_tile[:]
+        identity = holder[:, 0:P]
         make_identity(nc, identity)
-        warm_out = keep.tile([P, 8], F32, name="warm_out")
-        nc.scalar.activation(warm_out[:], holder[:, 0:8], SILU)
         results = [keep.tile([P, T], F32, name=f"result{nt}") for nt in range(N_TILES)]
         for nt in range(N_TILES):
             nc.gpsimd.memset(results[nt][:], 0.0)
@@ -192,7 +188,7 @@ def tile_moe_pkd_glu_silu_kernel(tc, x_words, x_scales, w1, w3, w2, gate, offs, 
         for e in range(E):
             on_scalar = (OCTETS, OCTETS)
             on_vector = (0, 0)
-            shared = (OCTETS, OCTETS // 2 if e > 0 else 0)
+            shared = (OCTETS, 0 if e == 0 else OCTETS if e == LAST else 3 * OCTETS // 4)
             staged = first_layer_codes(e, 0, w1, 0, on_scalar)
             lower = quantised(staged[0])
             if e > 0:

@@ -14,6 +14,7 @@ U16 = mybir.dt.uint16
 U8 = mybir.dt.uint8
 FP8X4 = mybir.dt.float8_e4m3fn_x4
 MULT = mybir.AluOpType.mult
+ADD = mybir.AluOpType.add
 SILU = mybir.ActivationFunctionType.Silu
 
 P = 128
@@ -38,7 +39,13 @@ GATE_COLS = SLOTS // P
 GATHER = 2 * C
 HALF = H // 2
 OCTETS = H // 8
-PIECES = (0, 224, 448, 608, 768)
+PIECES = (0, 256, 448, 608, 768)
+C1_VECTOR = (64, 0, 0, 0)
+C2_VECTOR = (0, 0, 0, 32)
+C3_SCALAR = (0, 32, 32, 56)
+C1_GPSIMD = (0, 48, 48, 48)
+HOLD_UPPER0 = (1, 1, 1, 0)
+W2_GPSIMD = (256, 128, 128, 128)
 
 
 def tile_moe_pkd_glu_silu_kernel(tc, x_words, x_scales, w1, w3, w2, gate, offs, out):
@@ -104,18 +111,33 @@ def tile_moe_pkd_glu_silu_kernel(tc, x_words, x_scales, w1, w3, w2, gate, offs, 
         def entries(e):
             return offsets[:, e * LIST_COLS : (e + 1) * LIST_COLS]
 
-        def first_layer_codes(e, chunk, w, o, scalar_share):
+        def first_layer_codes(e, chunk, w, o, scalar_share, upper_at=None, lower_at=None, rest=nc.vector):
             raw = loads.tile([P, PACK, H], F32, name=f"raw{e}_{chunk}", offset=raw_at(e, chunk))
             nc.sync.dma_start(raw[:], w[e, o * K_PASS : (o + 1) * K_PASS, :].rearrange("(p j) i -> p j i", j=PACK))
             src = raw[:].rearrange("p j (a u r v) -> p u a j v r", u=2, r=2, v=2)
             staged = []
             for half in range(2):
-                grouped = stage.tile([P, 2 * K_PASS], BF16, name="grouped", align_bytes=64)
+                if half == 1 and upper_at is not None:
+                    grouped = loads.tile([P, 2 * K_PASS], BF16, name=f"upper{e}_{chunk}", align_bytes=64, offset=upper_at)
+                elif half == 0 and lower_at is not None:
+                    grouped = loads.tile([P, 2 * K_PASS], BF16, name=f"under{e}_{chunk}", align_bytes=64, offset=lower_at)
+                else:
+                    grouped = stage.tile([P, 2 * K_PASS], BF16, name="grouped", align_bytes=64)
                 dst = grouped[:].rearrange("p (v a r j) -> p a j v r", v=2, r=2, j=PACK)
                 cut = scalar_share[half]
                 if cut > 0:
                     nc.scalar.copy(dst[:, 0:cut, :, :, :], src[:, half, 0:cut, :, :, :])
-                if cut < OCTETS:
+                if cut < OCTETS and rest is nc.gpsimd:
+                    for v in range(2):
+                        nc.gpsimd.tensor_scalar(
+                            grouped[:, v * K_PASS : (v + 1) * K_PASS].rearrange("p (a r j) -> p a r j", r=2, j=PACK)[:, cut:],
+                            raw[:].rearrange("p j (a u r v) -> p u v a r j", u=2, r=2, v=2)[:, half, v, cut:],
+                            1.0,
+                            0.0,
+                            MULT,
+                            ADD,
+                        )
+                elif cut < OCTETS:
                     nc.vector.tensor_copy(dst[:, cut:OCTETS, :, :, :], src[:, half, cut:OCTETS, :, :, :])
                 staged.append(grouped)
             return staged
@@ -156,19 +178,18 @@ def tile_moe_pkd_glu_silu_kernel(tc, x_words, x_scales, w1, w3, w2, gate, offs, 
                 nc.sync.dma_start(raw2[:, 2 * u : 2 * u + 2, :].rearrange("p v n -> p (v n)"), rows[u])
             return raw2
 
-        def second_cast(e, raw2, copy):
-            grouped2 = stage.tile([P, N * PACK], BF16, name="grouped", align_bytes=64)
-            copy(
-                grouped2[:].rearrange("p (c i jj j2) -> p c jj i j2", i=4, jj=2, j2=2),
-                raw2[:].rearrange("p (jj j2) (c i) -> p c jj i j2", j2=2, i=4),
-            )
+        def second_cast(e, raw2, at, on_gpsimd):
+            grouped2 = loads.tile([P, N * PACK], BF16, name=f"grouped2_{e}", align_bytes=64, offset=at)
+            dst = grouped2[:].rearrange("p (n j) -> p n j", j=PACK)
+            src = raw2[:].rearrange("p j n -> p n j")
+            if on_gpsimd > 0:
+                nc.gpsimd.tensor_scalar(dst[:, 0:on_gpsimd], src[:, 0:on_gpsimd], 1.0, 0.0, MULT, ADD)
+            if on_gpsimd < N:
+                nc.scalar.copy(
+                    grouped2[:, on_gpsimd * PACK :].rearrange("p (c i jj j2) -> p c jj i j2", i=4, jj=2, j2=2),
+                    raw2[:, :, on_gpsimd:].rearrange("p (jj j2) (c i) -> p c jj i j2", j2=2, i=4),
+                )
             return grouped2
-
-        def second_codes(e, grouped2, at):
-            w2_words = loads.tile([P, N], U32, name=f"w2_words{e}", align_bytes=64, offset=at)
-            w2_scales = small.tile([P, N], U8, name="w2_scales", align_bytes=64)
-            nc.vector.quantize_mx(out=w2_words[:].bitcast(FP8X4), scales=w2_scales[:], in_=grouped2[:])
-            return w2_words, w2_scales
 
         def put_back(e, nt, y_bank, y_at):
             y = loads.tile([P, C], F32, name=f"y{e}_{nt}", offset=y_at)
@@ -187,34 +208,34 @@ def tile_moe_pkd_glu_silu_kernel(tc, x_words, x_scales, w1, w3, w2, gate, offs, 
         y_banks = []
         for e in range(E):
             on_scalar = (OCTETS, OCTETS)
-            on_vector = (0, 0)
-            shared = (OCTETS, 0 if e == 0 else OCTETS if e == LAST else 3 * OCTETS // 4)
-            staged = first_layer_codes(e, 0, w1, 0, on_scalar)
-            lower = quantised(staged[0])
+            staged = first_layer_codes(e, 0, w1, 0, on_scalar, None, raw_at(e - 1, 0) if e > 0 else None)
+            lower = quantised(staged[0], f"lower{e}", raw_at(e - 1, 1) + 2 * ACT_BYTES if e > 0 else None)
             if e > 0:
-                weighted = small.tile([P, C], F32, name="weighted")
+                weighted = loads.tile([P, C], F32, name=f"weighted{e}", offset=raw_at(e - 1, 0))
                 nc.vector.tensor_tensor(weighted[:], y_banks[e - 1][0][:], gate_flat[:, (e - 1) * C : e * C], MULT)
-                nc.vector.tensor_copy(results[0][:].indirect(entries(e - 1)), weighted[:])
             w1q = [[lower, quantised(staged[1])]]
-            w1q.append([quantised(part) for part in first_layer_codes(e, 1, w1, 1, shared)])
-            staged0 = first_layer_codes(e, 2, w3, 0, on_scalar)
+            if e > 0:
+                nc.vector.tensor_copy(results[0][:].indirect(entries(e - 1)), weighted[:])
+            if C1_GPSIMD[e] > 0:
+                staged = first_layer_codes(e, 1, w1, 1, (OCTETS, OCTETS - C1_GPSIMD[e]), raw_at(e - 1, 0) + C * 4, None, nc.gpsimd)
+            else:
+                staged = first_layer_codes(e, 1, w1, 1, (OCTETS, OCTETS - C1_VECTOR[e]))
+            w1q.append([quantised(part) for part in staged])
+            staged0 = first_layer_codes(e, 2, w3, 0, (OCTETS, OCTETS - C2_VECTOR[e]))
             lower0 = quantised(staged0[0])
-            staged1 = first_layer_codes(e, 3, w3, 1, on_vector)
+            if not HOLD_UPPER0[e]:
+                upper0 = quantised(staged0[1])
+            staged1 = first_layer_codes(e, 3, w3, 1, (0, C3_SCALAR[e]), raw_at(e, 1) + 2 * ACT_BYTES)
             lower1 = quantised(staged1[0])
-            upper0 = quantised(staged0[1], f"upper0_{e}", raw_at(e, 3))
+            if HOLD_UPPER0[e]:
+                upper0 = quantised(staged0[1], f"upper0_{e}", raw_at(e, 3))
             upper1 = quantised(staged1[1])
             w3q = [[lower0, upper0], [lower1, upper1]]
             raw2 = load_w2(e)
+            after = raw_at(e, 3 if C3_SCALAR[e] > 0 else 2)
             if e > 0:
-                put_back_piece(e - 1, raw_at(e, 2))
-            if e == 0:
-                grouped2 = second_cast(e, raw2, nc.vector.tensor_copy)
-                acts_at = raw_at(e, 2)
-            elif e < LAST:
-                grouped2 = second_cast(e, raw2, nc.scalar.copy)
-                acts_at = W2_AT + e * W2_BYTES
-            else:
-                acts_at = raw_at(e, 2) + ACT_BYTES
+                put_back_piece(e - 1, after + C * 4)
+            acts_at = after + ACT_BYTES
 
             acts = []
             for g in range(GROUPS):
@@ -222,18 +243,20 @@ def tile_moe_pkd_glu_silu_kernel(tc, x_words, x_scales, w1, w3, w2, gate, offs, 
                 act = loads.tile([P, GROUP, PACK], F32, name=f"act{e}_{g}", offset=acts_at + g * ACT_BYTES)
                 nc.scalar.activation(act[:], bank[:].rearrange("p t c -> p c t"), SILU)
                 acts.append(act)
-            if e == LAST:
-                grouped2 = second_cast(e, raw2, nc.scalar.copy)
+            grouped2 = second_cast(e, raw2, raw_at(e, 1) + 2 * ACT_BYTES, W2_GPSIMD[e])
 
             h = small.tile([P, C * PACK], BF16, name="h", align_bytes=64)
             for g in range(GROUPS):
                 bank = first_layer(w3q, e, g, "b_bank", 2 + g)
                 part = h[:, g * GROUP * PACK : (g + 1) * GROUP * PACK].rearrange("p (c t) -> p c t", t=PACK)
                 nc.vector.tensor_tensor(part, bank[:].rearrange("p t c -> p c t"), acts[g][:], MULT)
-            w2_words, w2_scales = second_codes(e, grouped2, acts_at)
 
             h_words = small.tile([P, C], U32, name="h_words", align_bytes=64)
             h_scales = small.tile([P, C], U8, name="h_scales", align_bytes=64)
+            w2_words = loads.tile([P, N], U32, name=f"w2_words{e}", align_bytes=64, offset=acts_at)
+            w2_scales = small.tile([P, N], U8, name="w2_scales", align_bytes=64)
+
+            nc.vector.quantize_mx(out=w2_words[:].bitcast(FP8X4), scales=w2_scales[:], in_=grouped2[:])
             nc.vector.quantize_mx(out=h_words[:].bitcast(FP8X4), scales=h_scales[:], in_=h[:])
 
             if e == LAST:

@@ -42,10 +42,10 @@ OCTETS = H // 8
 PIECES = (0, 256, 448, 608, 768)
 C1_VECTOR = (64, 0, 0, 0)
 C2_VECTOR = (0, 0, 0, 32)
-C3_SCALAR = (0, 32, 32, 56)
-C1_GPSIMD = (0, 48, 48, 48)
+C3_SCALAR = (0, 32, 32, 48)
+C1_GPSIMD = (0, 32, 32, 32)
 HOLD_UPPER0 = (1, 1, 1, 0)
-W2_GPSIMD = (256, 128, 128, 128)
+W2_GPSIMD = (128, 64, 64, 80)
 
 
 def tile_moe_pkd_glu_silu_kernel(tc, x_words, x_scales, w1, w3, w2, gate, offs, out):
@@ -60,7 +60,7 @@ def tile_moe_pkd_glu_silu_kernel(tc, x_words, x_scales, w1, w3, w2, gate, offs, 
         psum = ctx.enter_context(tc.psum_pool(name="psum", bufs=1))
 
         gate_row = keep.tile([P, GATE_COLS], F32, name="gate_row")
-        nc.sync.dma_start(gate_row[:], gate[0:1, :].rearrange("o (p m) -> (o p) m", m=GATE_COLS))
+        nc.scalar.dma_start(gate_row[:], gate[0:1, :].rearrange("o (p m) -> (o p) m", m=GATE_COLS))
         token_words = [keep.tile([P, T], I32, name=f"token_words{o}", align_bytes=64) for o in range(PASSES)]
         nc.sync.dma_start(token_words[0][:], x_words[0].rearrange("p t r -> p (t r)").bitcast(I32))
         offsets = keep.tile([P, E * LIST_COLS], U16, name="offsets")

@@ -43,9 +43,9 @@ PIECES = (0, 256, 448, 608, 768)
 C1_VECTOR = (64, 0, 0, 0)
 C2_VECTOR = (0, 0, 0, 32)
 C3_SCALAR = (0, 32, 32, 48)
-C1_GPSIMD = (0, 32, 32, 32)
+C1_GPSIMD = (0, 16, 16, 16)
 HOLD_UPPER0 = (1, 1, 1, 0)
-W2_GPSIMD = (128, 64, 64, 80)
+W2_GPSIMD = (128, 96, 96, 64)
 
 
 def tile_moe_pkd_glu_silu_kernel(tc, x_words, x_scales, w1, w3, w2, gate, offs, out):
@@ -191,11 +191,6 @@ def tile_moe_pkd_glu_silu_kernel(tc, x_words, x_scales, w1, w3, w2, gate, offs, 
                 )
             return grouped2
 
-        def put_back(e, nt, y_bank, y_at):
-            y = loads.tile([P, C], F32, name=f"y{e}_{nt}", offset=y_at)
-            nc.scalar.copy(y[:], y_bank[:])
-            nc.vector.tensor_tensor(results[nt][:].indirect(entries(e)), y[:], gate_flat[:, e * C : (e + 1) * C], MULT)
-
         def put_back_piece(index, y_at):
             first, end = PIECES[index], PIECES[index + 1]
             y = loads.tile([P, end - first], F32, name=f"piece{index}", offset=y_at)
@@ -256,11 +251,11 @@ def tile_moe_pkd_glu_silu_kernel(tc, x_words, x_scales, w1, w3, w2, gate, offs, 
             w2_words = loads.tile([P, N], U32, name=f"w2_words{e}", align_bytes=64, offset=acts_at)
             w2_scales = small.tile([P, N], U8, name="w2_scales", align_bytes=64)
 
+            if e == LAST:
+                break
             nc.vector.quantize_mx(out=w2_words[:].bitcast(FP8X4), scales=w2_scales[:], in_=grouped2[:])
             nc.vector.quantize_mx(out=h_words[:].bitcast(FP8X4), scales=h_scales[:], in_=h[:])
 
-            if e == LAST:
-                put_back_piece(LAST, acts_at + ACT_BYTES)
             banks = []
             for nt in range(N_TILES):
                 rows = slice(nt * P, (nt + 1) * P)
@@ -277,6 +272,30 @@ def tile_moe_pkd_glu_silu_kernel(tc, x_words, x_scales, w1, w3, w2, gate, offs, 
                 banks.append(y_bank)
             y_banks.append(banks)
 
+        def quantise_h(g):
+            cols = slice(g * GROUP, (g + 1) * GROUP)
+            part = h[:, g * GROUP * PACK : (g + 1) * GROUP * PACK]
+            nc.vector.quantize_mx(out=h_words[:, cols].bitcast(FP8X4), scales=h_scales[:, cols], in_=part)
+
+        quantise_h(0)
+        nc.vector.quantize_mx(out=w2_words[:].bitcast(FP8X4), scales=w2_scales[:], in_=grouped2[:])
+        quantise_h(1)
+        put_back_piece(LAST, acts_at + ACT_BYTES)
         for nt in range(N_TILES):
-            put_back(LAST, nt, y_banks[LAST][nt], raw_at(LAST, 1) + nt * C * 4)
-            nc.sync.dma_start(out[nt * P : (nt + 1) * P, :], results[nt][:])
+            rows = slice(nt * P, (nt + 1) * P)
+            y = loads.tile([P, C], F32, name=f"y{nt}", offset=raw_at(LAST, 1) + nt * C * 4)
+            for g in range(GROUPS):
+                cols = slice(g * GROUP, (g + 1) * GROUP)
+                y_bank = psum.tile([P, GROUP], F32, name=f"y_last{nt}_{g}", offset=(nt * 4 + g) * BANK)
+                nc.tensor.matmul_mx(
+                    out=y_bank[:],
+                    lhsT=w2_words[:, rows].bitcast(FP8X4),
+                    lhsT_scale=w2_scales[:, rows],
+                    rhs=h_words[:, cols].bitcast(FP8X4),
+                    rhs_scale=h_scales[:, cols],
+                    start=True,
+                    stop=True,
+                )
+                nc.scalar.copy(y[:, cols], y_bank[:])
+            nc.vector.tensor_tensor(results[nt][:].indirect(entries(LAST)), y[:], gate_flat[:, LAST * C :], MULT)
+            nc.sync.dma_start(out[rows, :], results[nt][:])

@@ -41,11 +41,11 @@ HALF = H // 2
 OCTETS = H // 8
 PIECES = (0, 256, 448, 608, 768)
 C1_VECTOR = (64, 0, 0, 0)
-C2_VECTOR = (0, 0, 0, 32)
+C2_VECTOR = (0, 0, 0, 48)
 C3_SCALAR = (0, 32, 32, 48)
-C1_GPSIMD = (0, 16, 16, 16)
+C1_GPSIMD = (0, 0, 0, 0)
 HOLD_UPPER0 = (1, 1, 1, 0)
-W2_GPSIMD = (128, 96, 96, 64)
+W2_GPSIMD = (0, 0, 0, 0)
 
 
 def tile_moe_pkd_glu_silu_kernel(tc, x_words, x_scales, w1, w3, w2, gate, offs, out):
@@ -185,7 +185,7 @@ def tile_moe_pkd_glu_silu_kernel(tc, x_words, x_scales, w1, w3, w2, gate, offs, 
             if on_gpsimd > 0:
                 nc.gpsimd.tensor_scalar(dst[:, 0:on_gpsimd], src[:, 0:on_gpsimd], 1.0, 0.0, MULT, ADD)
             if on_gpsimd < N:
-                nc.scalar.copy(
+                (nc.vector.tensor_copy if e == 0 else nc.scalar.copy)(
                     grouped2[:, on_gpsimd * PACK :].rearrange("p (c i jj j2) -> p c jj i j2", i=4, jj=2, j2=2),
                     raw2[:, :, on_gpsimd:].rearrange("p (jj j2) (c i) -> p c jj i j2", j2=2, i=4),
                 )
@@ -203,12 +203,15 @@ def tile_moe_pkd_glu_silu_kernel(tc, x_words, x_scales, w1, w3, w2, gate, offs, 
         y_banks = []
         for e in range(E):
             on_scalar = (OCTETS, OCTETS)
-            staged = first_layer_codes(e, 0, w1, 0, on_scalar, None, raw_at(e - 1, 0) if e > 0 else None)
-            lower = quantised(staged[0], f"lower{e}", raw_at(e - 1, 1) + 2 * ACT_BYTES if e > 0 else None)
+            if e == 0:
+                staged = first_layer_codes(e, 0, w1, 0, on_scalar)
+            else:
+                staged = first_layer_codes(e, 0, w1, 0, (OCTETS, 16), raw_at(e - 1, 1) + 2 * ACT_BYTES, raw_at(e - 1, 0))
+            lower = quantised(staged[0])
             if e > 0:
-                weighted = loads.tile([P, C], F32, name=f"weighted{e}", offset=raw_at(e - 1, 0))
+                weighted = loads.tile([P, C], F32, name=f"weighted{e}", offset=raw_at(e, 0))
                 nc.vector.tensor_tensor(weighted[:], y_banks[e - 1][0][:], gate_flat[:, (e - 1) * C : e * C], MULT)
-            w1q = [[lower, quantised(staged[1])]]
+            w1q = [[lower, quantised(staged[1], f"upper{e}", raw_at(e - 1, 0) + C * 4 if e > 0 else None)]]
             if e > 0:
                 nc.vector.tensor_copy(results[0][:].indirect(entries(e - 1)), weighted[:])
             if C1_GPSIMD[e] > 0:

@@ -241,7 +241,15 @@ def tile_moe_pkd_glu_silu_kernel(tc, x_words, x_scales, w1, w3, w2, gate, offs, 
                 act = loads.tile([P, GROUP, PACK], F32, name=f"act{e}_{g}", offset=acts_at + g * ACT_BYTES)
                 nc.scalar.activation(act[:], bank[:].rearrange("p t c -> p c t"), SILU)
                 acts.append(act)
-            grouped2 = second_cast(e, raw2, raw_at(e, 1) + 2 * ACT_BYTES, W2_GPSIMD[e])
+            if e < LAST:
+                grouped2 = second_cast(e, raw2, raw_at(e, 1) + 2 * ACT_BYTES, W2_GPSIMD[e])
+            else:
+                grouped2 = loads.tile([P, N * PACK], BF16, name="grouped2_last", align_bytes=64, offset=raw_at(e, 1) + 2 * ACT_BYTES)
+                for nt in range(N_TILES):
+                    nc.scalar.copy(
+                        grouped2[:, nt * K_PASS : (nt + 1) * K_PASS].rearrange("p (c i jj j2) -> p c jj i j2", i=4, jj=2, j2=2),
+                        raw2[:, :, nt * P : (nt + 1) * P].rearrange("p (jj j2) (c i) -> p c jj i j2", j2=2, i=4),
+                    )
 
             h = small.tile([P, C * PACK], BF16, name="h", align_bytes=64)
             for g in range(GROUPS):
@@ -281,8 +289,9 @@ def tile_moe_pkd_glu_silu_kernel(tc, x_words, x_scales, w1, w3, w2, gate, offs, 
             nc.vector.quantize_mx(out=h_words[:, cols].bitcast(FP8X4), scales=h_scales[:, cols], in_=part)
 
         quantise_h(0)
-        nc.vector.quantize_mx(out=w2_words[:].bitcast(FP8X4), scales=w2_scales[:], in_=grouped2[:])
+        nc.vector.quantize_mx(out=w2_words[:, 0:P].bitcast(FP8X4), scales=w2_scales[:, 0:P], in_=grouped2[:, 0:K_PASS])
         quantise_h(1)
+        nc.vector.quantize_mx(out=w2_words[:, P:].bitcast(FP8X4), scales=w2_scales[:, P:], in_=grouped2[:, K_PASS:])
         put_back_piece(LAST, acts_at + ACT_BYTES)
         for nt in range(N_TILES):
             rows = slice(nt * P, (nt + 1) * P)

@@ -39,12 +39,16 @@ GATE_COLS = SLOTS // P
 GATHER = 2 * C
 HALF = H // 2
 OCTETS = H // 8
-PIECES = (0, 256, 448, 608, 768)
+PIECES = (0, 96, 256, 352, 512, 608, 768)
+LATE = 256
+THIN = 160
 C1_VECTOR = (64, 0, 0, 0)
-C2_VECTOR = (0, 0, 0, 48)
-C3_SCALAR = (0, 32, 32, 48)
-C1_GPSIMD = (0, 0, 0, 0)
-HOLD_UPPER0 = (1, 1, 1, 0)
+C2_VECTOR = (128, 0, 0, 48)
+C0_SCALAR = (64, 16, 16, 16)
+W2_VECTOR = (0, 0, 0)
+C3_SCALAR = (48, 32, 32, 48)
+PAIR1 = (0, 1, 1, 1)
+HOLD_UPPER0 = (0, 1, 1, 0)
 W2_GPSIMD = (0, 0, 0, 0)
 
 
@@ -54,7 +58,7 @@ def tile_moe_pkd_glu_silu_kernel(tc, x_words, x_scales, w1, w3, w2, gate, offs, 
     with ExitStack() as ctx:
         keep = ctx.enter_context(tc.tile_pool(name="keep", bufs=1))
         loads = ctx.enter_context(tc.tile_pool(name="loads", bufs=1))
-        stage = ctx.enter_context(tc.tile_pool(name="stage", bufs=8))
+        stage = ctx.enter_context(tc.tile_pool(name="stage", bufs=5))
         codes = ctx.enter_context(tc.tile_pool(name="codes", bufs=12))
         small = ctx.enter_context(tc.tile_pool(name="small", bufs=2))
         psum = ctx.enter_context(tc.psum_pool(name="psum", bufs=1))
@@ -68,13 +72,15 @@ def tile_moe_pkd_glu_silu_kernel(tc, x_words, x_scales, w1, w3, w2, gate, offs, 
         nc.sync.dma_start(token_words[1][:], x_words[1].rearrange("p t r -> p (t r)").bitcast(I32))
 
         token_scales = keep.tile([P, T], U8, name="token_scales", align_bytes=64)
-        nc.gpsimd.memset(token_scales[:].bitcast(I32), 0)
+        nc.vector.memset(token_scales[:].bitcast(I32), 0)
         holder = loads.tile([P, (LOADS_END - RAW_BYTES) // 4], F32, name="holder", offset=RAW_BYTES)
         identity = holder[:, 0:P]
         make_identity(nc, identity)
         results = [keep.tile([P, T], F32, name=f"result{nt}") for nt in range(N_TILES)]
         for nt in range(N_TILES):
-            nc.gpsimd.memset(results[nt][:], 0.0)
+            nc.vector.memset(results[nt][:], 0.0)
+        zeros = keep.tile([P, GROUP], F32, name="zeros")
+        nc.vector.memset(zeros[:], 0.0)
 
         for q in range(4):
             nc.sync.dma_start(
@@ -99,11 +105,12 @@ def tile_moe_pkd_glu_silu_kernel(tc, x_words, x_scales, w1, w3, w2, gate, offs, 
                 part = offsets[:, x * GATHER // 16 : (x + 1) * GATHER // 16]
                 nc.vector.tensor_copy(picked[:], token_words[o][:].bitcast(U32).indirect(part))
                 slot_words[o].append(picked)
-        for x in range(SLOTS // GATHER):
-            picked = keep.tile([P, GATHER], U8, name=f"slot_scales{x}", align_bytes=64)
-            part = offsets[:, x * GATHER // 16 : (x + 1) * GATHER // 16]
-            nc.vector.tensor_copy(picked[:], token_scales[:].indirect(part))
-            slot_scales.append(picked)
+
+        def gather_scales(picked, first, end):
+            nc.vector.tensor_copy(picked[:], token_scales[:].indirect(offsets[:, first // 16 : end // 16]))
+            slot_scales.extend(picked[:, at : at + C] for at in range(0, end - first, C))
+
+        gather_scales(keep.tile([P, SLOTS - LATE], U8, name="slot_scales", align_bytes=64), 0, SLOTS - LATE)
 
         def raw_at(e, chunk):
             return (e * CHUNKS + chunk) * RAW_BYTES
@@ -111,19 +118,21 @@ def tile_moe_pkd_glu_silu_kernel(tc, x_words, x_scales, w1, w3, w2, gate, offs, 
         def entries(e):
             return offsets[:, e * LIST_COLS : (e + 1) * LIST_COLS]
 
-        def first_layer_codes(e, chunk, w, o, scalar_share, upper_at=None, lower_at=None, rest=nc.vector):
+        def first_layer_codes(e, chunk, w, o, scalar_share, upper_at=None, lower_at=None, rest=nc.vector, into=(None, None)):
             raw = loads.tile([P, PACK, H], F32, name=f"raw{e}_{chunk}", offset=raw_at(e, chunk))
             nc.sync.dma_start(raw[:], w[e, o * K_PASS : (o + 1) * K_PASS, :].rearrange("(p j) i -> p j i", j=PACK))
             src = raw[:].rearrange("p j (a u r v) -> p u a j v r", u=2, r=2, v=2)
             staged = []
             for half in range(2):
-                if half == 1 and upper_at is not None:
+                if into[half] is not None:
+                    grouped = into[half]
+                elif half == 1 and upper_at is not None:
                     grouped = loads.tile([P, 2 * K_PASS], BF16, name=f"upper{e}_{chunk}", align_bytes=64, offset=upper_at)
                 elif half == 0 and lower_at is not None:
                     grouped = loads.tile([P, 2 * K_PASS], BF16, name=f"under{e}_{chunk}", align_bytes=64, offset=lower_at)
                 else:
                     grouped = stage.tile([P, 2 * K_PASS], BF16, name="grouped", align_bytes=64)
-                dst = grouped[:].rearrange("p (v a r j) -> p a j v r", v=2, r=2, j=PACK)
+                dst = grouped[:, :].rearrange("p (v a r j) -> p a j v r", v=2, r=2, j=PACK)
                 cut = scalar_share[half]
                 if cut > 0:
                     nc.scalar.copy(dst[:, 0:cut, :, :, :], src[:, half, 0:cut, :, :, :])
@@ -151,24 +160,31 @@ def tile_moe_pkd_glu_silu_kernel(tc, x_words, x_scales, w1, w3, w2, gate, offs, 
             nc.vector.quantize_mx(out=words[:].bitcast(FP8X4), scales=scales[:], in_=grouped[:])
             return words, scales
 
+        def quantised_pair(both):
+            words = small.tile([P, H], U32, name="pair_words", align_bytes=64, bufs=3)
+            scales = small.tile([P, H], U8, name="pair_scales", align_bytes=64, bufs=3)
+            nc.vector.quantize_mx(out=words[:].bitcast(FP8X4), scales=scales[:], in_=both[:])
+            return [(words[:, u * HALF : (u + 1) * HALF], scales[:, u * HALF : (u + 1) * HALF]) for u in range(2)]
+
         def first_layer(weights, e, g, kind, bank_index):
             bank = psum.tile([P, PACK, GROUP], F32, name=f"{kind}{e}_{g}", offset=bank_index * BANK)
             first = (e * C + g * GROUP) % GATHER
             cols = slice(first, first + GROUP)
             x = e * C // GATHER
-            for t in range(PACK):
+            order = ((0, 0), (1, 0), (0, 1), (1, 1)) if kind == "b_bank" and HOLD_UPPER0[e] else ((0, 0), (0, 1), (1, 0), (1, 1))
+            steps = [(o, 2 * u + v) for o, u in order for v in range(2)]
+            for step, (o, t) in enumerate(steps):
                 part = slice(t % 2 * P, (t % 2 + 1) * P)
-                for o in range(PASSES):
-                    words, scales = weights[o][t // 2]
-                    nc.tensor.matmul_mx(
-                        out=bank[:, t, :],
-                        lhsT=words[:, part].bitcast(FP8X4),
-                        lhsT_scale=scales[:, part],
-                        rhs=slot_words[o][x][:, cols].bitcast(FP8X4),
-                        rhs_scale=slot_scales[x][4 * o : P, cols],
-                        start=(o == 0),
-                        stop=(o == PASSES - 1),
-                    )
+                words, scales = weights[o][t // 2]
+                nc.tensor.matmul_mx(
+                    out=bank[:, t, :],
+                    lhsT=words[:, part].bitcast(FP8X4),
+                    lhsT_scale=scales[:, part],
+                    rhs=slot_words[o][x][:, cols].bitcast(FP8X4),
+                    rhs_scale=slot_scales[e][4 * o : P, g * GROUP : (g + 1) * GROUP],
+                    start=(step == 0),
+                    stop=(step == len(steps) - 1),
+                )
             return bank
 
         def load_w2(e):
@@ -185,20 +201,35 @@ def tile_moe_pkd_glu_silu_kernel(tc, x_words, x_scales, w1, w3, w2, gate, offs, 
             if on_gpsimd > 0:
                 nc.gpsimd.tensor_scalar(dst[:, 0:on_gpsimd], src[:, 0:on_gpsimd], 1.0, 0.0, MULT, ADD)
             if on_gpsimd < N:
-                (nc.vector.tensor_copy if e == 0 else nc.scalar.copy)(
+                (nc.vector.tensor_copy if W2_VECTOR[e] else nc.scalar.copy)(
                     grouped2[:, on_gpsimd * PACK :].rearrange("p (c i jj j2) -> p c jj i j2", i=4, jj=2, j2=2),
                     raw2[:, :, on_gpsimd:].rearrange("p (jj j2) (c i) -> p c jj i j2", j2=2, i=4),
                 )
             return grouped2
 
-        def put_back_piece(index, y_at):
+        def take_piece(index, y_at):
             first, end = PIECES[index], PIECES[index + 1]
+            if end == first:
+                return None
             y = loads.tile([P, end - first], F32, name=f"piece{index}", offset=y_at)
             for owner in range(first // C, (end - 1) // C + 1):
                 lo, hi = max(first, owner * C), min(end, (owner + 1) * C)
-                nc.scalar.copy(y[:, lo - first : hi - first], y_banks[owner][1][:, lo - owner * C : hi - owner * C])
-            part = offsets[:, first // 16 : end // 16]
-            nc.vector.tensor_tensor(results[1][:].indirect(part), y[:], gate_flat[:, first:end], MULT)
+                source = y_banks[owner][1][:, lo - owner * C : hi - owner * C]
+                if end - first >= THIN:
+                    nc.scalar.copy(y[:, lo - first : hi - first], source)
+                else:
+                    nc.vector.tensor_tensor(y[:, lo - first : hi - first], source, gate_flat[:, lo:hi], MULT)
+            return y
+
+        def put_back_piece(index, y):
+            first, end = PIECES[index], PIECES[index + 1]
+            if end == first:
+                return
+            window = results[1][:].indirect(offsets[:, first // 16 : end // 16])
+            if end - first >= THIN:
+                nc.vector.tensor_tensor(window, y[:], gate_flat[:, first:end], MULT)
+            else:
+                nc.vector.tensor_tensor(window, y[:], zeros[:, 0 : end - first], ADD)
 
         y_banks = []
         for e in range(E):
@@ -206,34 +237,44 @@ def tile_moe_pkd_glu_silu_kernel(tc, x_words, x_scales, w1, w3, w2, gate, offs, 
             if e == 0:
                 staged = first_layer_codes(e, 0, w1, 0, on_scalar)
             else:
-                staged = first_layer_codes(e, 0, w1, 0, (OCTETS, 16), raw_at(e - 1, 1) + 2 * ACT_BYTES, raw_at(e - 1, 0))
+                staged = first_layer_codes(e, 0, w1, 0, (OCTETS, C0_SCALAR[e]), raw_at(e - 1, 1) + 2 * ACT_BYTES, raw_at(e - 1, 0))
             lower = quantised(staged[0])
             if e > 0:
                 weighted = loads.tile([P, C], F32, name=f"weighted{e}", offset=raw_at(e, 0))
                 nc.vector.tensor_tensor(weighted[:], y_banks[e - 1][0][:], gate_flat[:, (e - 1) * C : e * C], MULT)
+            if 0 < e < LAST:
+                piece = take_piece(2 * e - 2, raw_at(e, 0) + ACT_BYTES)
             w1q = [[lower, quantised(staged[1], f"upper{e}", raw_at(e - 1, 0) + C * 4 if e > 0 else None)]]
             if e > 0:
                 nc.vector.tensor_copy(results[0][:].indirect(entries(e - 1)), weighted[:])
-            if C1_GPSIMD[e] > 0:
-                staged = first_layer_codes(e, 1, w1, 1, (OCTETS, OCTETS - C1_GPSIMD[e]), raw_at(e - 1, 0) + C * 4, None, nc.gpsimd)
+            if 0 < e < LAST:
+                put_back_piece(2 * e - 2, piece)
+            if PAIR1[e]:
+                both = small.tile([P, PACK * H], BF16, name="both", align_bytes=64)
+                first_layer_codes(e, 1, w1, 1, (OCTETS, OCTETS - C1_VECTOR[e]), into=(both[:, 0 : 2 * K_PASS], both[:, 2 * K_PASS :]))
+                w1q.append(quantised_pair(both))
             else:
                 staged = first_layer_codes(e, 1, w1, 1, (OCTETS, OCTETS - C1_VECTOR[e]))
-            w1q.append([quantised(part) for part in staged])
-            staged0 = first_layer_codes(e, 2, w3, 0, (OCTETS, OCTETS - C2_VECTOR[e]))
+                w1q.append([quantised(part) for part in staged])
+            staged0 = first_layer_codes(e, 2, w3, 0, (min(OCTETS, 2 * OCTETS - C2_VECTOR[e]), max(0, OCTETS - C2_VECTOR[e])))
             lower0 = quantised(staged0[0])
             if not HOLD_UPPER0[e]:
                 upper0 = quantised(staged0[1])
-            staged1 = first_layer_codes(e, 3, w3, 1, (0, C3_SCALAR[e]), raw_at(e, 1) + 2 * ACT_BYTES)
+            staged1 = first_layer_codes(e, 3, w3, 1, (0, C3_SCALAR[e]), raw_at(e, 1) + 2 * ACT_BYTES, raw_at(0, 1) if e == 0 else None)
             lower1 = quantised(staged1[0])
             if HOLD_UPPER0[e]:
                 upper0 = quantised(staged0[1], f"upper0_{e}", raw_at(e, 3))
-            upper1 = quantised(staged1[1])
-            w3q = [[lower0, upper0], [lower1, upper1]]
-            raw2 = load_w2(e)
             after = raw_at(e, 3 if C3_SCALAR[e] > 0 else 2)
             if e > 0:
-                put_back_piece(e - 1, after + C * 4)
-            acts_at = after + ACT_BYTES
+                piece = take_piece(min(2 * e - 1, 4), after + C * 4)
+            upper1 = quantised(staged1[1])
+            if e == 0 and LATE > 0:
+                gather_scales(loads.tile([P, LATE], U8, name="late_scales", align_bytes=64, offset=raw_at(0, 1)), SLOTS - LATE, SLOTS)
+            w3q = [[lower0, upper0], [lower1, upper1]]
+            raw2 = load_w2(e)
+            if e > 0:
+                put_back_piece(min(2 * e - 1, 4), piece)
+            acts_at = after + ACT_BYTES if e > 0 else raw_at(0, 0) + 2 * ACT_BYTES
 
             acts = []
             for g in range(GROUPS):
@@ -244,26 +285,25 @@ def tile_moe_pkd_glu_silu_kernel(tc, x_words, x_scales, w1, w3, w2, gate, offs, 
             if e < LAST:
                 grouped2 = second_cast(e, raw2, raw_at(e, 1) + 2 * ACT_BYTES, W2_GPSIMD[e])
             else:
-                grouped2 = loads.tile([P, N * PACK], BF16, name="grouped2_last", align_bytes=64, offset=raw_at(e, 1) + 2 * ACT_BYTES)
+                last = loads.tile([P, (N + C) * PACK], BF16, name="last", align_bytes=64, offset=raw_at(e, 1) + 2 * ACT_BYTES)
                 for nt in range(N_TILES):
                     nc.scalar.copy(
-                        grouped2[:, nt * K_PASS : (nt + 1) * K_PASS].rearrange("p (c i jj j2) -> p c jj i j2", i=4, jj=2, j2=2),
+                        last[:, 3 * nt * K_PASS : (3 * nt + 1) * K_PASS].rearrange("p (c i jj j2) -> p c jj i j2", i=4, jj=2, j2=2),
                         raw2[:, :, nt * P : (nt + 1) * P].rearrange("p (jj j2) (c i) -> p c jj i j2", j2=2, i=4),
                     )
 
-            h = small.tile([P, C * PACK], BF16, name="h", align_bytes=64)
+            h = small.tile([P, C * PACK], BF16, name="h", align_bytes=64) if e < LAST else last[:, K_PASS : 3 * K_PASS]
             for g in range(GROUPS):
                 bank = first_layer(w3q, e, g, "b_bank", 2 + g)
                 part = h[:, g * GROUP * PACK : (g + 1) * GROUP * PACK].rearrange("p (c t) -> p c t", t=PACK)
                 nc.vector.tensor_tensor(part, bank[:].rearrange("p t c -> p c t"), acts[g][:], MULT)
 
+            if e == LAST:
+                break
             h_words = small.tile([P, C], U32, name="h_words", align_bytes=64)
             h_scales = small.tile([P, C], U8, name="h_scales", align_bytes=64)
             w2_words = loads.tile([P, N], U32, name=f"w2_words{e}", align_bytes=64, offset=acts_at)
             w2_scales = small.tile([P, N], U8, name="w2_scales", align_bytes=64)
-
-            if e == LAST:
-                break
             nc.vector.quantize_mx(out=w2_words[:].bitcast(FP8X4), scales=w2_scales[:], in_=grouped2[:])
             nc.vector.quantize_mx(out=h_words[:].bitcast(FP8X4), scales=h_scales[:], in_=h[:])
 
@@ -283,16 +323,15 @@ def tile_moe_pkd_glu_silu_kernel(tc, x_words, x_scales, w1, w3, w2, gate, offs, 
                 banks.append(y_bank)
             y_banks.append(banks)
 
-        def quantise_h(g):
-            cols = slice(g * GROUP, (g + 1) * GROUP)
-            part = h[:, g * GROUP * PACK : (g + 1) * GROUP * PACK]
-            nc.vector.quantize_mx(out=h_words[:, cols].bitcast(FP8X4), scales=h_scales[:, cols], in_=part)
-
-        quantise_h(0)
-        nc.vector.quantize_mx(out=w2_words[:, 0:P].bitcast(FP8X4), scales=w2_scales[:, 0:P], in_=grouped2[:, 0:K_PASS])
-        quantise_h(1)
-        nc.vector.quantize_mx(out=w2_words[:, P:].bitcast(FP8X4), scales=w2_scales[:, P:], in_=grouped2[:, K_PASS:])
-        put_back_piece(LAST, acts_at + ACT_BYTES)
+        last_words = loads.tile([P, N + C], U32, name="last_words", align_bytes=64, offset=acts_at)
+        last_scales = small.tile([P, N + C], U8, name="last_scales", align_bytes=64, bufs=1)
+        piece = take_piece(5, acts_at + ACT_BYTES)
+        for g in range(GROUPS):
+            cols = slice(2 * g * P, 2 * (g + 1) * P)
+            nc.vector.quantize_mx(
+                out=last_words[:, cols].bitcast(FP8X4), scales=last_scales[:, cols], in_=last[:, cols.start * PACK : cols.stop * PACK]
+            )
+        put_back_piece(5, piece)
         for nt in range(N_TILES):
             rows = slice(nt * P, (nt + 1) * P)
             y = loads.tile([P, C], F32, name=f"y{nt}", offset=raw_at(LAST, 1) + nt * C * 4)
@@ -301,10 +340,10 @@ def tile_moe_pkd_glu_silu_kernel(tc, x_words, x_scales, w1, w3, w2, gate, offs, 
                 y_bank = psum.tile([P, GROUP], F32, name=f"y_last{nt}_{g}", offset=(nt * 4 + g) * BANK)
                 nc.tensor.matmul_mx(
                     out=y_bank[:],
-                    lhsT=w2_words[:, rows].bitcast(FP8X4),
-                    lhsT_scale=w2_scales[:, rows],
-                    rhs=h_words[:, cols].bitcast(FP8X4),
-                    rhs_scale=h_scales[:, cols],
+                    lhsT=last_words[:, 3 * nt * P : (3 * nt + 1) * P].bitcast(FP8X4),
+                    lhsT_scale=last_scales[:, 3 * nt * P : (3 * nt + 1) * P],
+                    rhs=last_words[:, (1 + g) * P : (2 + g) * P].bitcast(FP8X4),
+                    rhs_scale=last_scales[:, (1 + g) * P : (2 + g) * P],
                     start=True,
                     stop=True,
                 )

@@ -39,14 +39,14 @@ GATE_COLS = SLOTS // P
 GATHER = 2 * C
 HALF = H // 2
 OCTETS = H // 8
-PIECES = (0, 96, 256, 352, 512, 608, 768)
+PIECES = (0, 96, 256, 352, 512, 512, 608, 768)
 LATE = 256
 THIN = 160
-C1_VECTOR = (64, 0, 0, 0)
-C2_VECTOR = (128, 0, 0, 48)
-C0_SCALAR = (64, 16, 16, 16)
+C1_VECTOR = (32, 0, 0, 0)
+C2_VECTOR = (128, 0, 0, 40)
+C0_SCALAR = (64, 24, 24, 24)
 W2_VECTOR = (0, 0, 0)
-C3_SCALAR = (48, 32, 32, 48)
+C3_SCALAR = (48, 48, 48, 48)
 PAIR1 = (0, 1, 1, 1)
 HOLD_UPPER0 = (0, 1, 1, 0)
 W2_GPSIMD = (0, 0, 0, 0)
@@ -242,12 +242,12 @@ def tile_moe_pkd_glu_silu_kernel(tc, x_words, x_scales, w1, w3, w2, gate, offs, 
             if e > 0:
                 weighted = loads.tile([P, C], F32, name=f"weighted{e}", offset=raw_at(e, 0))
                 nc.vector.tensor_tensor(weighted[:], y_banks[e - 1][0][:], gate_flat[:, (e - 1) * C : e * C], MULT)
-            if 0 < e < LAST:
+            if e > 0:
                 piece = take_piece(2 * e - 2, raw_at(e, 0) + ACT_BYTES)
             w1q = [[lower, quantised(staged[1], f"upper{e}", raw_at(e - 1, 0) + C * 4 if e > 0 else None)]]
             if e > 0:
                 nc.vector.tensor_copy(results[0][:].indirect(entries(e - 1)), weighted[:])
-            if 0 < e < LAST:
+            if e > 0:
                 put_back_piece(2 * e - 2, piece)
             if PAIR1[e]:
                 both = small.tile([P, PACK * H], BF16, name="both", align_bytes=64)
@@ -266,14 +266,14 @@ def tile_moe_pkd_glu_silu_kernel(tc, x_words, x_scales, w1, w3, w2, gate, offs, 
                 upper0 = quantised(staged0[1], f"upper0_{e}", raw_at(e, 3))
             after = raw_at(e, 3 if C3_SCALAR[e] > 0 else 2)
             if e > 0:
-                piece = take_piece(min(2 * e - 1, 4), after + C * 4)
+                piece = take_piece(2 * e - 1, after + C * 4)
             upper1 = quantised(staged1[1])
             if e == 0 and LATE > 0:
                 gather_scales(loads.tile([P, LATE], U8, name="late_scales", align_bytes=64, offset=raw_at(0, 1)), SLOTS - LATE, SLOTS)
             w3q = [[lower0, upper0], [lower1, upper1]]
             raw2 = load_w2(e)
             if e > 0:
-                put_back_piece(min(2 * e - 1, 4), piece)
+                put_back_piece(2 * e - 1, piece)
             acts_at = after + ACT_BYTES if e > 0 else raw_at(0, 0) + 2 * ACT_BYTES
 
             acts = []
@@ -325,13 +325,14 @@ def tile_moe_pkd_glu_silu_kernel(tc, x_words, x_scales, w1, w3, w2, gate, offs, 
 
         last_words = loads.tile([P, N + C], U32, name="last_words", align_bytes=64, offset=acts_at)
         last_scales = small.tile([P, N + C], U8, name="last_scales", align_bytes=64, bufs=1)
-        piece = take_piece(5, acts_at + ACT_BYTES)
-        for g in range(GROUPS):
-            cols = slice(2 * g * P, 2 * (g + 1) * P)
+        parts = (slice(P, 2 * P), slice(0, P), slice(2 * P, 3 * P), slice(3 * P, 4 * P))
+        for at, cols in enumerate(parts):
+            if at == len(parts) // 2:
+                piece = take_piece(6, acts_at + ACT_BYTES)
             nc.vector.quantize_mx(
                 out=last_words[:, cols].bitcast(FP8X4), scales=last_scales[:, cols], in_=last[:, cols.start * PACK : cols.stop * PACK]
             )
-        put_back_piece(5, piece)
+        put_back_piece(6, piece)
         for nt in range(N_TILES):
             rows = slice(nt * P, (nt + 1) * P)
             y = loads.tile([P, C], F32, name=f"y{nt}", offset=raw_at(LAST, 1) + nt * C * 4)

@@ -279,8 +279,8 @@ def tile_moe_pkd_glu_silu_kernel(tc, x_words, x_scales, w1, w3, w2, gate, offs, 
             acts = []
             for g in range(GROUPS):
                 bank = first_layer(w1q, e, g, "a_bank", g)
-                act = loads.tile([P, GROUP, PACK], F32, name=f"act{e}_{g}", offset=acts_at + g * ACT_BYTES)
-                nc.scalar.activation(act[:], bank[:].rearrange("p t c -> p c t"), SILU)
+                act = loads.tile([P, GROUP // 2, PACK, 2], F32, name=f"act{e}_{g}", offset=acts_at + g * ACT_BYTES)
+                nc.scalar.activation(act[:], bank[:].rearrange("p t (c d) -> p c t d", d=2), SILU)
                 acts.append(act)
             if e < LAST:
                 grouped2 = second_cast(e, raw2, raw_at(e, 1) + 2 * ACT_BYTES, W2_GPSIMD[e])
@@ -295,8 +295,8 @@ def tile_moe_pkd_glu_silu_kernel(tc, x_words, x_scales, w1, w3, w2, gate, offs, 
             h = small.tile([P, C * PACK], BF16, name="h", align_bytes=64) if e < LAST else last[:, K_PASS : 3 * K_PASS]
             for g in range(GROUPS):
                 bank = first_layer(w3q, e, g, "b_bank", 2 + g)
-                part = h[:, g * GROUP * PACK : (g + 1) * GROUP * PACK].rearrange("p (c t) -> p c t", t=PACK)
-                nc.vector.tensor_tensor(part, bank[:].rearrange("p t c -> p c t"), acts[g][:], MULT)
+                part = h[:, g * GROUP * PACK : (g + 1) * GROUP * PACK].rearrange("p (c d t) -> p c t d", d=2, t=PACK)
+                nc.vector.tensor_tensor(part, bank[:].rearrange("p t (c d) -> p c t d", d=2), acts[g][:], MULT)
 
             if e == LAST:
                 break

@@ -14,8 +14,8 @@ U16 = mybir.dt.uint16
 U8 = mybir.dt.uint8
 FP8X4 = mybir.dt.float8_e4m3fn_x4
 MULT = mybir.AluOpType.mult
-ADD = mybir.AluOpType.add
 SILU = mybir.ActivationFunctionType.Silu
+COPY = mybir.ActivationFunctionType.Copy
 
 P = 128
 PACK = 4
@@ -27,29 +27,21 @@ GROUP = 128
 GROUPS = C // GROUP
 N_TILES = N // P
 LAST = E - 1
-CHUNKS = 2 * PASSES
-RAW_BYTES = PACK * H * 4
-W2_BYTES = PACK * N * 4
-W2_AT = E * CHUNKS * RAW_BYTES
-LOADS_END = W2_AT + E * W2_BYTES
-ACT_BYTES = GROUP * PACK * 4
 BANK = 2048
-BANK_COLS = 512
 GATE_COLS = SLOTS // P
 GATHER = 2 * C
+SCALAR_SHARE = (
+    ((64, 64), (64, 32), (0, 64), (0, 48)),
+    ((0, 64), (0, 0), (0, 48), (0, 48)),
+    ((0, 64), (0, 0), (0, 48), (0, 48)),
+    ((0, 64), (0, 0), (0, 0), (0, 48)),
+)
 HALF = H // 2
 OCTETS = H // 8
-PIECES = (0, 96, 256, 352, 512, 512, 608, 768)
-LATE = 256
-THIN = 160
-C1_VECTOR = (32, 0, 0, 0)
-C2_VECTOR = (128, 0, 0, 40)
-C0_SCALAR = (64, 24, 24, 24)
-W2_VECTOR = (0, 0, 0)
-C3_SCALAR = (48, 48, 48, 48)
-PAIR1 = (0, 1, 1, 1)
-HOLD_UPPER0 = (0, 1, 1, 0)
-W2_GPSIMD = (0, 0, 0, 0)
+ACT_BYTES = GROUP * PACK * 4
+HELD = (1, 1, 0, 0)
+RAW_BYTES = PACK * H * 4
+RING = 10
 
 
 def tile_moe_pkd_glu_silu_kernel(tc, x_words, x_scales, w1, w3, w2, gate, offs, out):
@@ -58,11 +50,13 @@ def tile_moe_pkd_glu_silu_kernel(tc, x_words, x_scales, w1, w3, w2, gate, offs, 
     with ExitStack() as ctx:
         keep = ctx.enter_context(tc.tile_pool(name="keep", bufs=1))
         loads = ctx.enter_context(tc.tile_pool(name="loads", bufs=1))
-        stage = ctx.enter_context(tc.tile_pool(name="stage", bufs=5))
-        codes = ctx.enter_context(tc.tile_pool(name="codes", bufs=12))
+        stage = ctx.enter_context(tc.tile_pool(name="stage", bufs=6))
+        codes = ctx.enter_context(tc.tile_pool(name="codes", bufs=16))
         small = ctx.enter_context(tc.tile_pool(name="small", bufs=2))
         psum = ctx.enter_context(tc.psum_pool(name="psum", bufs=1))
 
+        token_scales = keep.tile([P, T], U8, name="token_scales", align_bytes=64)
+        nc.vector.memset(token_scales[:].bitcast(I32), 0)
         gate_row = keep.tile([P, GATE_COLS], F32, name="gate_row")
         nc.scalar.dma_start(gate_row[:], gate[0:1, :].rearrange("o (p m) -> (o p) m", m=GATE_COLS))
         token_words = [keep.tile([P, T], I32, name=f"token_words{o}", align_bytes=64) for o in range(PASSES)]
@@ -70,284 +64,194 @@ def tile_moe_pkd_glu_silu_kernel(tc, x_words, x_scales, w1, w3, w2, gate, offs, 
         offsets = keep.tile([P, E * LIST_COLS], U16, name="offsets")
         nc.sync.dma_start(offsets[:], offs)
         nc.sync.dma_start(token_words[1][:], x_words[1].rearrange("p t r -> p (t r)").bitcast(I32))
-
-        token_scales = keep.tile([P, T], U8, name="token_scales", align_bytes=64)
-        nc.vector.memset(token_scales[:].bitcast(I32), 0)
-        holder = loads.tile([P, (LOADS_END - RAW_BYTES) // 4], F32, name="holder", offset=RAW_BYTES)
-        identity = holder[:, 0:P]
-        make_identity(nc, identity)
-        results = [keep.tile([P, T], F32, name=f"result{nt}") for nt in range(N_TILES)]
-        for nt in range(N_TILES):
-            nc.vector.memset(results[nt][:], 0.0)
-        zeros = keep.tile([P, GROUP], F32, name="zeros")
-        nc.vector.memset(zeros[:], 0.0)
-
         for q in range(4):
             nc.sync.dma_start(
                 token_scales[32 * q : 32 * q + 4 * PASSES, :].bitcast(I32),
                 x_scales[:, 4 * q : 4 * q + 4, :].bitcast(I32),
             )
 
+        identity = keep.tile([P, P], F32, name="identity")
+        make_identity(nc, identity[:])
+        results = [keep.tile([P, T], F32, name=f"result{nt}") for nt in range(N_TILES)]
+        nc.vector.memset(results[0][:], 0.0)
+        zero = keep.tile([P, 1], F32, name="zero")
+        nc.vector.memset(zero[:], 0.0)
+        nc.scalar.activation(results[1][:], zero[:].to_broadcast([P, T]), SILU)
+
         gates = keep.tile([P, P, GATE_COLS], F32, name="gates")
         for half in range(GATE_COLS // PACK):
             bank = psum.tile([P, PACK, P], F32, name=f"gate_bank{half}", offset=(6 + half) * BANK)
             for m in range(PACK):
                 col = half * PACK + m
-                nc.tensor.transpose(bank[:, m, :], gate_row[:, col : col + 1].to_broadcast([P, P]), identity)
+                nc.tensor.transpose(bank[:, m, :], gate_row[:, col : col + 1].to_broadcast([P, P]), identity[:])
             nc.scalar.copy(gates[:, :, half * PACK : (half + 1) * PACK], bank[:].rearrange("p m n -> p n m"))
         gate_flat = gates[:].rearrange("p n m -> p (n m)")
 
-        slot_words = [[], []]
+        slot_words = []
         slot_scales = []
-        for o in range(PASSES):
-            for x in range(SLOTS // GATHER):
+        for x in range(SLOTS // GATHER):
+            part = offsets[:, x * GATHER // 16 : (x + 1) * GATHER // 16]
+            both = []
+            for o in range(PASSES):
                 picked = keep.tile([P, GATHER], U32, name=f"slot_words{x}_{o}", align_bytes=64)
-                part = offsets[:, x * GATHER // 16 : (x + 1) * GATHER // 16]
                 nc.vector.tensor_copy(picked[:], token_words[o][:].bitcast(U32).indirect(part))
-                slot_words[o].append(picked)
+                both.append(picked)
+            slot_words.append(both)
 
-        def gather_scales(picked, first, end):
-            nc.vector.tensor_copy(picked[:], token_scales[:].indirect(offsets[:, first // 16 : end // 16]))
-            slot_scales.extend(picked[:, at : at + C] for at in range(0, end - first, C))
+        def gather_scales(picked, x):
+            nc.vector.tensor_copy(picked[:], token_scales[:].indirect(offsets[:, x * GATHER // 16 : (x + 1) * GATHER // 16]))
+            slot_scales.append(picked)
 
-        gather_scales(keep.tile([P, SLOTS - LATE], U8, name="slot_scales", align_bytes=64), 0, SLOTS - LATE)
-
-        def raw_at(e, chunk):
-            return (e * CHUNKS + chunk) * RAW_BYTES
+        gather_scales(keep.tile([P, GATHER], U8, name="slot_scales", align_bytes=64), 0)
 
         def entries(e):
             return offsets[:, e * LIST_COLS : (e + 1) * LIST_COLS]
 
-        def first_layer_codes(e, chunk, w, o, scalar_share, upper_at=None, lower_at=None, rest=nc.vector, into=(None, None)):
+        def raw_at(e, chunk):
+            n = e * 2 * PASSES + chunk
+            return (0 if n == 0 else 1 + (n - 1) % RING) * RAW_BYTES
+
+        def put_back(e, nt, y_bank, y):
+            nc.vector.tensor_tensor(y[:], y_bank[:], gate_flat[:, e * C : (e + 1) * C], MULT)
+            nc.scalar.activation(results[nt][:].indirect(entries(e)), y[:], COPY)
+
+        def first_layer_codes(w, e, o, chunk):
             raw = loads.tile([P, PACK, H], F32, name=f"raw{e}_{chunk}", offset=raw_at(e, chunk))
             nc.sync.dma_start(raw[:], w[e, o * K_PASS : (o + 1) * K_PASS, :].rearrange("(p j) i -> p j i", j=PACK))
             src = raw[:].rearrange("p j (a u r v) -> p u a j v r", u=2, r=2, v=2)
             staged = []
-            for half in range(2):
-                if into[half] is not None:
-                    grouped = into[half]
-                elif half == 1 and upper_at is not None:
-                    grouped = loads.tile([P, 2 * K_PASS], BF16, name=f"upper{e}_{chunk}", align_bytes=64, offset=upper_at)
-                elif half == 0 and lower_at is not None:
-                    grouped = loads.tile([P, 2 * K_PASS], BF16, name=f"under{e}_{chunk}", align_bytes=64, offset=lower_at)
-                else:
-                    grouped = stage.tile([P, 2 * K_PASS], BF16, name="grouped", align_bytes=64)
-                dst = grouped[:, :].rearrange("p (v a r j) -> p a j v r", v=2, r=2, j=PACK)
-                cut = scalar_share[half]
+            for u in range(2):
+                grouped = stage.tile([P, 2 * K_PASS], BF16, name="grouped", align_bytes=64)
+                dst = grouped[:].rearrange("p (v a r j) -> p a j v r", v=2, r=2, j=PACK)
+                cut = SCALAR_SHARE[e][chunk][u]
                 if cut > 0:
-                    nc.scalar.copy(dst[:, 0:cut, :, :, :], src[:, half, 0:cut, :, :, :])
-                if cut < OCTETS and rest is nc.gpsimd:
-                    for v in range(2):
-                        nc.gpsimd.tensor_scalar(
-                            grouped[:, v * K_PASS : (v + 1) * K_PASS].rearrange("p (a r j) -> p a r j", r=2, j=PACK)[:, cut:],
-                            raw[:].rearrange("p j (a u r v) -> p u v a r j", u=2, r=2, v=2)[:, half, v, cut:],
-                            1.0,
-                            0.0,
-                            MULT,
-                            ADD,
-                        )
-                elif cut < OCTETS:
-                    nc.vector.tensor_copy(dst[:, cut:OCTETS, :, :, :], src[:, half, cut:OCTETS, :, :, :])
+                    nc.scalar.copy(dst[:, 0:cut], src[:, u, 0:cut])
+                if cut < OCTETS:
+                    nc.vector.tensor_copy(dst[:, cut:OCTETS], src[:, u, cut:OCTETS])
                 staged.append(grouped)
-            return staged
-
-        def quantised(grouped, name=None, at=None):
-            if at is None:
+            made = []
+            for grouped in staged:
                 words = codes.tile([P, HALF], U32, name="w_words", align_bytes=64)
-            else:
-                words = loads.tile([P, HALF], U32, name=name, align_bytes=64, offset=at)
-            scales = codes.tile([P, HALF], U8, name="w_scales", align_bytes=64)
-            nc.vector.quantize_mx(out=words[:].bitcast(FP8X4), scales=scales[:], in_=grouped[:])
-            return words, scales
-
-        def quantised_pair(both):
-            words = small.tile([P, H], U32, name="pair_words", align_bytes=64, bufs=3)
-            scales = small.tile([P, H], U8, name="pair_scales", align_bytes=64, bufs=3)
-            nc.vector.quantize_mx(out=words[:].bitcast(FP8X4), scales=scales[:], in_=both[:])
-            return [(words[:, u * HALF : (u + 1) * HALF], scales[:, u * HALF : (u + 1) * HALF]) for u in range(2)]
+                scales = codes.tile([P, HALF], U8, name="w_scales", align_bytes=64)
+                nc.vector.quantize_mx(out=words[:].bitcast(FP8X4), scales=scales[:], in_=grouped[:])
+                made.append((words, scales))
+            return made
 
         def first_layer(weights, e, g, kind, bank_index):
             bank = psum.tile([P, PACK, GROUP], F32, name=f"{kind}{e}_{g}", offset=bank_index * BANK)
-            first = (e * C + g * GROUP) % GATHER
+            x, first = divmod(e * C + g * GROUP, GATHER)
             cols = slice(first, first + GROUP)
-            x = e * C // GATHER
-            order = ((0, 0), (1, 0), (0, 1), (1, 1)) if kind == "b_bank" and HOLD_UPPER0[e] else ((0, 0), (0, 1), (1, 0), (1, 1))
-            steps = [(o, 2 * u + v) for o, u in order for v in range(2)]
-            for step, (o, t) in enumerate(steps):
-                part = slice(t % 2 * P, (t % 2 + 1) * P)
-                words, scales = weights[o][t // 2]
-                nc.tensor.matmul_mx(
-                    out=bank[:, t, :],
-                    lhsT=words[:, part].bitcast(FP8X4),
-                    lhsT_scale=scales[:, part],
-                    rhs=slot_words[o][x][:, cols].bitcast(FP8X4),
-                    rhs_scale=slot_scales[e][4 * o : P, g * GROUP : (g + 1) * GROUP],
-                    start=(step == 0),
-                    stop=(step == len(steps) - 1),
-                )
+            for o in range(PASSES):
+                for t in range(PACK):
+                    words, scales = weights[o][t // 2]
+                    part = slice(t % 2 * P, (t % 2 + 1) * P)
+                    nc.tensor.matmul_mx(
+                        out=bank[:, t, :],
+                        lhsT=words[:, part].bitcast(FP8X4),
+                        lhsT_scale=scales[:, part],
+                        rhs=slot_words[x][o][:, cols].bitcast(FP8X4),
+                        rhs_scale=slot_scales[x][4 * o : P, cols],
+                        start=(o == 0 and t == 0),
+                        stop=(o == PASSES - 1 and t == PACK - 1),
+                    )
             return bank
 
-        def load_w2(e):
-            raw2 = loads.tile([P, PACK, N], F32, name=f"raw2_{e}", offset=W2_AT + e * W2_BYTES)
+        def second_layer_codes(e):
+            raw2 = small.tile([P, PACK, N], F32, name="raw2", bufs=3)
             rows = w2[e].rearrange("(a u r v) n -> u a r (v n)", u=2, r=2, v=2)
             for u in range(2):
                 nc.sync.dma_start(raw2[:, 2 * u : 2 * u + 2, :].rearrange("p v n -> p (v n)"), rows[u])
-            return raw2
-
-        def second_cast(e, raw2, at, on_gpsimd):
-            grouped2 = loads.tile([P, N * PACK], BF16, name=f"grouped2_{e}", align_bytes=64, offset=at)
-            dst = grouped2[:].rearrange("p (n j) -> p n j", j=PACK)
-            src = raw2[:].rearrange("p j n -> p n j")
-            if on_gpsimd > 0:
-                nc.gpsimd.tensor_scalar(dst[:, 0:on_gpsimd], src[:, 0:on_gpsimd], 1.0, 0.0, MULT, ADD)
-            if on_gpsimd < N:
-                (nc.vector.tensor_copy if W2_VECTOR[e] else nc.scalar.copy)(
-                    grouped2[:, on_gpsimd * PACK :].rearrange("p (c i jj j2) -> p c jj i j2", i=4, jj=2, j2=2),
-                    raw2[:, :, on_gpsimd:].rearrange("p (jj j2) (c i) -> p c jj i j2", j2=2, i=4),
+            made = []
+            for nt in range(N_TILES):
+                grouped2 = small.tile([P, P * PACK], BF16, name=f"grouped2_{nt}", align_bytes=64)
+                (nc.vector.tensor_copy if nt == 0 else nc.scalar.copy)(
+                    grouped2[:].rearrange("p (c i j) -> p c j i", i=4, j=PACK),
+                    raw2[:, :, nt * P : (nt + 1) * P].rearrange("p j (c i) -> p c j i", i=4),
                 )
-            return grouped2
+                made.append(grouped2)
+            result = [None] * N_TILES
+            for nt in reversed(range(N_TILES)):
+                words = small.tile([P, P], U32, name=f"w2_words{nt}", align_bytes=64)
+                scales = small.tile([P, P], U8, name=f"w2_scales{nt}", align_bytes=64)
+                nc.vector.quantize_mx(out=words[:].bitcast(FP8X4), scales=scales[:], in_=made[nt][:])
+                result[nt] = (words, scales)
+            return result
 
-        def take_piece(index, y_at):
-            first, end = PIECES[index], PIECES[index + 1]
-            if end == first:
-                return None
-            y = loads.tile([P, end - first], F32, name=f"piece{index}", offset=y_at)
-            for owner in range(first // C, (end - 1) // C + 1):
-                lo, hi = max(first, owner * C), min(end, (owner + 1) * C)
-                source = y_banks[owner][1][:, lo - owner * C : hi - owner * C]
-                if end - first >= THIN:
-                    nc.scalar.copy(y[:, lo - first : hi - first], source)
-                else:
-                    nc.vector.tensor_tensor(y[:, lo - first : hi - first], source, gate_flat[:, lo:hi], MULT)
-            return y
-
-        def put_back_piece(index, y):
-            first, end = PIECES[index], PIECES[index + 1]
-            if end == first:
-                return
-            window = results[1][:].indirect(offsets[:, first // 16 : end // 16])
-            if end - first >= THIN:
-                nc.vector.tensor_tensor(window, y[:], gate_flat[:, first:end], MULT)
-            else:
-                nc.vector.tensor_tensor(window, y[:], zeros[:, 0 : end - first], ADD)
-
-        y_banks = []
         for e in range(E):
-            on_scalar = (OCTETS, OCTETS)
+            w1q = [first_layer_codes(w1, e, 0, 0)]
             if e == 0:
-                staged = first_layer_codes(e, 0, w1, 0, on_scalar)
-            else:
-                staged = first_layer_codes(e, 0, w1, 0, (OCTETS, C0_SCALAR[e]), raw_at(e - 1, 1) + 2 * ACT_BYTES, raw_at(e - 1, 0))
-            lower = quantised(staged[0])
-            if e > 0:
-                weighted = loads.tile([P, C], F32, name=f"weighted{e}", offset=raw_at(e, 0))
-                nc.vector.tensor_tensor(weighted[:], y_banks[e - 1][0][:], gate_flat[:, (e - 1) * C : e * C], MULT)
-            if e > 0:
-                piece = take_piece(2 * e - 2, raw_at(e, 0) + ACT_BYTES)
-            w1q = [[lower, quantised(staged[1], f"upper{e}", raw_at(e - 1, 0) + C * 4 if e > 0 else None)]]
-            if e > 0:
-                nc.vector.tensor_copy(results[0][:].indirect(entries(e - 1)), weighted[:])
-            if e > 0:
-                put_back_piece(2 * e - 2, piece)
-            if PAIR1[e]:
-                both = small.tile([P, PACK * H], BF16, name="both", align_bytes=64)
-                first_layer_codes(e, 1, w1, 1, (OCTETS, OCTETS - C1_VECTOR[e]), into=(both[:, 0 : 2 * K_PASS], both[:, 2 * K_PASS :]))
-                w1q.append(quantised_pair(both))
-            else:
-                staged = first_layer_codes(e, 1, w1, 1, (OCTETS, OCTETS - C1_VECTOR[e]))
-                w1q.append([quantised(part) for part in staged])
-            staged0 = first_layer_codes(e, 2, w3, 0, (min(OCTETS, 2 * OCTETS - C2_VECTOR[e]), max(0, OCTETS - C2_VECTOR[e])))
-            lower0 = quantised(staged0[0])
-            if not HOLD_UPPER0[e]:
-                upper0 = quantised(staged0[1])
-            staged1 = first_layer_codes(e, 3, w3, 1, (0, C3_SCALAR[e]), raw_at(e, 1) + 2 * ACT_BYTES, raw_at(0, 1) if e == 0 else None)
-            lower1 = quantised(staged1[0])
-            if HOLD_UPPER0[e]:
-                upper0 = quantised(staged0[1], f"upper0_{e}", raw_at(e, 3))
-            after = raw_at(e, 3 if C3_SCALAR[e] > 0 else 2)
-            if e > 0:
-                piece = take_piece(2 * e - 1, after + C * 4)
-            upper1 = quantised(staged1[1])
-            if e == 0 and LATE > 0:
-                gather_scales(loads.tile([P, LATE], U8, name="late_scales", align_bytes=64, offset=raw_at(0, 1)), SLOTS - LATE, SLOTS)
-            w3q = [[lower0, upper0], [lower1, upper1]]
-            raw2 = load_w2(e)
-            if e > 0:
-                put_back_piece(2 * e - 1, piece)
-            acts_at = after + ACT_BYTES if e > 0 else raw_at(0, 0) + 2 * ACT_BYTES
-
+                gather_scales(loads.tile([P, GATHER], U8, name="late_scales", align_bytes=64, offset=0), 1)
+            w1q.append(first_layer_codes(w1, e, 1, 1))
+            w3q = [first_layer_codes(w3, e, 0, 2)]
             acts = []
             for g in range(GROUPS):
                 bank = first_layer(w1q, e, g, "a_bank", g)
-                act = loads.tile([P, GROUP // 2, PACK, 2], F32, name=f"act{e}_{g}", offset=acts_at + g * ACT_BYTES)
+                if SCALAR_SHARE[e][2][1] > 0:
+                    act = loads.tile([P, GROUP // 2, PACK, 2], F32, name=f"act{e}_{g}", offset=raw_at(e, 2) + g * ACT_BYTES)
+                else:
+                    act = small.tile([P, GROUP // 2, PACK, 2], F32, name=f"act{g}")
                 nc.scalar.activation(act[:], bank[:].rearrange("p t (c d) -> p c t d", d=2), SILU)
                 acts.append(act)
-            if e < LAST:
-                grouped2 = second_cast(e, raw2, raw_at(e, 1) + 2 * ACT_BYTES, W2_GPSIMD[e])
-            else:
-                last = loads.tile([P, (N + C) * PACK], BF16, name="last", align_bytes=64, offset=raw_at(e, 1) + 2 * ACT_BYTES)
-                for nt in range(N_TILES):
-                    nc.scalar.copy(
-                        last[:, 3 * nt * K_PASS : (3 * nt + 1) * K_PASS].rearrange("p (c i jj j2) -> p c jj i j2", i=4, jj=2, j2=2),
-                        raw2[:, :, nt * P : (nt + 1) * P].rearrange("p (jj j2) (c i) -> p c jj i j2", j2=2, i=4),
-                    )
+            w3q.append(first_layer_codes(w3, e, 1, 3))
+            if e > 0 and HELD[e - 1]:
+                put_back(e - 1, 1, held, loads.tile([P, C], F32, name=f"held{e}", offset=raw_at(e, 3)))
+            w2q = second_layer_codes(e)
 
-            h = small.tile([P, C * PACK], BF16, name="h", align_bytes=64) if e < LAST else last[:, K_PASS : 3 * K_PASS]
+            h = small.tile([P, C * PACK], BF16, name="h", align_bytes=64)
             for g in range(GROUPS):
                 bank = first_layer(w3q, e, g, "b_bank", 2 + g)
                 part = h[:, g * GROUP * PACK : (g + 1) * GROUP * PACK].rearrange("p (c d t) -> p c t d", d=2, t=PACK)
                 nc.vector.tensor_tensor(part, bank[:].rearrange("p t (c d) -> p c t d", d=2), acts[g][:], MULT)
-
-            if e == LAST:
-                break
             h_words = small.tile([P, C], U32, name="h_words", align_bytes=64)
             h_scales = small.tile([P, C], U8, name="h_scales", align_bytes=64)
-            w2_words = loads.tile([P, N], U32, name=f"w2_words{e}", align_bytes=64, offset=acts_at)
-            w2_scales = small.tile([P, N], U8, name="w2_scales", align_bytes=64)
-            nc.vector.quantize_mx(out=w2_words[:].bitcast(FP8X4), scales=w2_scales[:], in_=grouped2[:])
-            nc.vector.quantize_mx(out=h_words[:].bitcast(FP8X4), scales=h_scales[:], in_=h[:])
-
-            banks = []
+            width = C if e < LAST else GROUP
+            for at in range(0, C, width):
+                nc.vector.quantize_mx(
+                    out=h_words[:, at : at + width].bitcast(FP8X4),
+                    scales=h_scales[:, at : at + width],
+                    in_=h[:, at * PACK : (at + width) * PACK],
+                )
+            if e < LAST:
+                for nt in range(N_TILES):
+                    y_bank = psum.tile([P, C], F32, name=f"y_bank{e}_{nt}", offset=(4 + nt) * BANK)
+                    nc.tensor.matmul_mx(
+                        out=y_bank[:],
+                        lhsT=w2q[nt][0][:].bitcast(FP8X4),
+                        lhsT_scale=w2q[nt][1][:],
+                        rhs=h_words[:].bitcast(FP8X4),
+                        rhs_scale=h_scales[:],
+                        start=True,
+                        stop=True,
+                    )
+                    if nt == 1 and HELD[e]:
+                        held = y_bank
+                    else:
+                        put_back(e, nt, y_bank, small.tile([P, C], F32, name=f"y{nt}"))
+                continue
+            ys = [small.tile([P, C], F32, name=f"y{nt}") for nt in range(N_TILES)]
+            for at in range(0, C, width):
+                cols = slice(at, at + width)
+                for nt in range(N_TILES):
+                    y_bank = psum.tile([P, width], F32, name=f"y_bank{e}_{nt}_{at}", offset=(4 + nt + 2 * (at // GROUP)) * BANK)
+                    nc.tensor.matmul_mx(
+                        out=y_bank[:],
+                        lhsT=w2q[nt][0][:].bitcast(FP8X4),
+                        lhsT_scale=w2q[nt][1][:],
+                        rhs=h_words[:, cols].bitcast(FP8X4),
+                        rhs_scale=h_scales[:, cols],
+                        start=True,
+                        stop=True,
+                    )
+                    if e == LAST and nt == N_TILES - 1:
+                        nc.scalar.copy(ys[nt][:, cols], y_bank[:])
+                    else:
+                        nc.vector.tensor_tensor(ys[nt][:, cols], y_bank[:], gate_flat[:, e * C + at : e * C + at + width], MULT)
             for nt in range(N_TILES):
-                rows = slice(nt * P, (nt + 1) * P)
-                y_bank = psum.tile([P, C], F32, name=f"y_bank{e}_{nt}", offset=(4 + nt * (1 + e % 3)) * BANK)
-                nc.tensor.matmul_mx(
-                    out=y_bank[:],
-                    lhsT=w2_words[:, rows].bitcast(FP8X4),
-                    lhsT_scale=w2_scales[:, rows],
-                    rhs=h_words[:].bitcast(FP8X4),
-                    rhs_scale=h_scales[:],
-                    start=True,
-                    stop=True,
-                )
-                banks.append(y_bank)
-            y_banks.append(banks)
+                window = results[nt][:].indirect(entries(e))
+                if e == LAST and nt == N_TILES - 1:
+                    nc.vector.tensor_tensor(window, ys[nt][:], gate_flat[:, e * C : (e + 1) * C], MULT)
+                else:
+                    nc.scalar.activation(window, ys[nt][:], COPY)
 
-        last_words = loads.tile([P, N + C], U32, name="last_words", align_bytes=64, offset=acts_at)
-        last_scales = small.tile([P, N + C], U8, name="last_scales", align_bytes=64, bufs=1)
-        parts = (slice(P, 2 * P), slice(0, P), slice(2 * P, 3 * P), slice(3 * P, 4 * P))
-        for at, cols in enumerate(parts):
-            if at == len(parts) // 2:
-                piece = take_piece(6, acts_at + ACT_BYTES)
-            nc.vector.quantize_mx(
-                out=last_words[:, cols].bitcast(FP8X4), scales=last_scales[:, cols], in_=last[:, cols.start * PACK : cols.stop * PACK]
-            )
-        put_back_piece(6, piece)
         for nt in range(N_TILES):
-            rows = slice(nt * P, (nt + 1) * P)
-            y = loads.tile([P, C], F32, name=f"y{nt}", offset=raw_at(LAST, 1) + nt * C * 4)
-            for g in range(GROUPS):
-                cols = slice(g * GROUP, (g + 1) * GROUP)
-                y_bank = psum.tile([P, GROUP], F32, name=f"y_last{nt}_{g}", offset=(nt * 4 + g) * BANK)
-                nc.tensor.matmul_mx(
-                    out=y_bank[:],
-                    lhsT=last_words[:, 3 * nt * P : (3 * nt + 1) * P].bitcast(FP8X4),
-                    lhsT_scale=last_scales[:, 3 * nt * P : (3 * nt + 1) * P],
-                    rhs=last_words[:, (1 + g) * P : (2 + g) * P].bitcast(FP8X4),
-                    rhs_scale=last_scales[:, (1 + g) * P : (2 + g) * P],
-                    start=True,
-                    stop=True,
-                )
-                nc.scalar.copy(y[:, cols], y_bank[:])
-            nc.vector.tensor_tensor(results[nt][:].indirect(entries(LAST)), y[:], gate_flat[:, LAST * C :], MULT)
-            nc.sync.dma_start(out[rows, :], results[nt][:])
+            nc.sync.dma_start(out[nt * P : (nt + 1) * P, :], results[nt][:])

@@ -14,6 +14,7 @@ U16 = mybir.dt.uint16
 U8 = mybir.dt.uint8
 FP8X4 = mybir.dt.float8_e4m3fn_x4
 MULT = mybir.AluOpType.mult
+ADD = mybir.AluOpType.add
 SILU = mybir.ActivationFunctionType.Silu
 COPY = mybir.ActivationFunctionType.Copy
 
@@ -34,12 +35,14 @@ SCALAR_SHARE = (
     ((64, 64), (64, 32), (0, 64), (0, 48)),
     ((0, 64), (0, 0), (0, 48), (0, 48)),
     ((0, 64), (0, 0), (0, 48), (0, 48)),
-    ((0, 64), (0, 0), (0, 0), (0, 48)),
+    ((0, 64), (0, 0), (0, 16), (0, 48)),
 )
 HALF = H // 2
 OCTETS = H // 8
 ACT_BYTES = GROUP * PACK * 4
 HELD = (1, 1, 0, 0)
+KEPT = 32
+W2_SCALAR = ((0, 32), (32, 0))
 RAW_BYTES = PACK * H * 4
 RING = 10
 
@@ -74,9 +77,10 @@ def tile_moe_pkd_glu_silu_kernel(tc, x_words, x_scales, w1, w3, w2, gate, offs, 
         make_identity(nc, identity[:])
         results = [keep.tile([P, T], F32, name=f"result{nt}") for nt in range(N_TILES)]
         nc.vector.memset(results[0][:], 0.0)
-        zero = keep.tile([P, 1], F32, name="zero")
+        zero = keep.tile([P, GROUP], F32, name="zero")
         nc.vector.memset(zero[:], 0.0)
-        nc.scalar.activation(results[1][:], zero[:].to_broadcast([P, T]), SILU)
+        nc.scalar.activation(results[1][:], zero[:, 0:1].to_broadcast([P, T]), SILU)
+        ending = keep.tile([P, 2 * C], F32, name="ending")
 
         gates = keep.tile([P, P, GATE_COLS], F32, name="gates")
         for half in range(GATE_COLS // PACK):
@@ -130,10 +134,16 @@ def tile_moe_pkd_glu_silu_kernel(tc, x_words, x_scales, w1, w3, w2, gate, offs, 
                     nc.vector.tensor_copy(dst[:, cut:OCTETS], src[:, u, cut:OCTETS])
                 staged.append(grouped)
             made = []
+            width = P if (e, chunk) == (LAST, 3) else HALF
             for grouped in staged:
                 words = codes.tile([P, HALF], U32, name="w_words", align_bytes=64)
                 scales = codes.tile([P, HALF], U8, name="w_scales", align_bytes=64)
-                nc.vector.quantize_mx(out=words[:].bitcast(FP8X4), scales=scales[:], in_=grouped[:])
+                for at in range(0, HALF, width):
+                    nc.vector.quantize_mx(
+                        out=words[:, at : at + width].bitcast(FP8X4),
+                        scales=scales[:, at : at + width],
+                        in_=grouped[:, at * PACK : (at + width) * PACK],
+                    )
                 made.append((words, scales))
             return made
 
@@ -141,36 +151,44 @@ def tile_moe_pkd_glu_silu_kernel(tc, x_words, x_scales, w1, w3, w2, gate, offs, 
             bank = psum.tile([P, PACK, GROUP], F32, name=f"{kind}{e}_{g}", offset=bank_index * BANK)
             x, first = divmod(e * C + g * GROUP, GATHER)
             cols = slice(first, first + GROUP)
-            for o in range(PASSES):
-                for t in range(PACK):
-                    words, scales = weights[o][t // 2]
-                    part = slice(t % 2 * P, (t % 2 + 1) * P)
-                    nc.tensor.matmul_mx(
-                        out=bank[:, t, :],
-                        lhsT=words[:, part].bitcast(FP8X4),
-                        lhsT_scale=scales[:, part],
-                        rhs=slot_words[x][o][:, cols].bitcast(FP8X4),
-                        rhs_scale=slot_scales[x][4 * o : P, cols],
-                        start=(o == 0 and t == 0),
-                        stop=(o == PASSES - 1 and t == PACK - 1),
-                    )
+            steps = [(o, t) for o in range(PASSES) for t in range(PACK)]
+            if g > 0:
+                steps = steps[:PACK] + steps[: PACK - 1 : -1]
+            for step, (o, t) in enumerate(steps):
+                words, scales = weights[o][t // 2]
+                part = slice(t % 2 * P, (t % 2 + 1) * P)
+                nc.tensor.matmul_mx(
+                    out=bank[:, t, :],
+                    lhsT=words[:, part].bitcast(FP8X4),
+                    lhsT_scale=scales[:, part],
+                    rhs=slot_words[x][o][:, cols].bitcast(FP8X4),
+                    rhs_scale=slot_scales[x][4 * o : P, cols],
+                    start=(step == 0),
+                    stop=(step == len(steps) - 1),
+                )
             return bank
 
         def second_layer_codes(e):
-            raw2 = small.tile([P, PACK, N], F32, name="raw2", bufs=3)
+            if e < LAST:
+                raw2 = small.tile([P, PACK, N], F32, name="raw2", bufs=3)
+            else:
+                raw2 = loads.tile([P, PACK, N], F32, name="raw2_last", offset=(RING + 1) * RAW_BYTES)
             rows = w2[e].rearrange("(a u r v) n -> u a r (v n)", u=2, r=2, v=2)
             for u in range(2):
                 nc.sync.dma_start(raw2[:, 2 * u : 2 * u + 2, :].rearrange("p v n -> p (v n)"), rows[u])
             made = []
             for nt in range(N_TILES):
                 grouped2 = small.tile([P, P * PACK], BF16, name=f"grouped2_{nt}", align_bytes=64)
-                (nc.vector.tensor_copy if nt == 0 else nc.scalar.copy)(
-                    grouped2[:].rearrange("p (c i j) -> p c j i", i=4, j=PACK),
-                    raw2[:, :, nt * P : (nt + 1) * P].rearrange("p j (c i) -> p c j i", i=4),
-                )
+                dst = grouped2[:].rearrange("p (c i j) -> p c j i", i=4, j=PACK)
+                src = raw2[:, :, nt * P : (nt + 1) * P].rearrange("p j (c i) -> p c j i", i=4)
+                cut = W2_SCALAR[e == LAST][nt]
+                if cut > 0:
+                    nc.scalar.copy(dst[:, 0:cut], src[:, 0:cut])
+                if cut < P // 4:
+                    nc.vector.tensor_copy(dst[:, cut:], src[:, cut:])
                 made.append(grouped2)
             result = [None] * N_TILES
-            for nt in reversed(range(N_TILES)):
+            for nt in (1, 0):
                 words = small.tile([P, P], U32, name=f"w2_words{nt}", align_bytes=64)
                 scales = small.tile([P, P], U8, name=f"w2_scales{nt}", align_bytes=64)
                 nc.vector.quantize_mx(out=words[:].bitcast(FP8X4), scales=scales[:], in_=made[nt][:])
@@ -184,74 +202,88 @@ def tile_moe_pkd_glu_silu_kernel(tc, x_words, x_scales, w1, w3, w2, gate, offs, 
             w1q.append(first_layer_codes(w1, e, 1, 1))
             w3q = [first_layer_codes(w3, e, 0, 2)]
             acts = []
-            for g in range(GROUPS):
-                bank = first_layer(w1q, e, g, "a_bank", g)
-                if SCALAR_SHARE[e][2][1] > 0:
-                    act = loads.tile([P, GROUP // 2, PACK, 2], F32, name=f"act{e}_{g}", offset=raw_at(e, 2) + g * ACT_BYTES)
-                else:
-                    act = small.tile([P, GROUP // 2, PACK, 2], F32, name=f"act{g}")
-                nc.scalar.activation(act[:], bank[:].rearrange("p t (c d) -> p c t d", d=2), SILU)
+            a_banks = [first_layer(w1q, e, g, "a_bank", g) for g in range(GROUPS)]
+
+            def silu(g, at):
+                act = loads.tile([P, GROUP // 2, PACK, 2], F32, name=f"act{e}_{g}", offset=at)
+                nc.scalar.activation(act[:], a_banks[g][:].rearrange("p t (c d) -> p c t d", d=2), SILU)
                 acts.append(act)
+
+            if e < LAST:
+                for g in range(GROUPS):
+                    silu(g, raw_at(e, 2) + g * ACT_BYTES)
             w3q.append(first_layer_codes(w3, e, 1, 3))
             if e > 0 and HELD[e - 1]:
                 put_back(e - 1, 1, held, loads.tile([P, C], F32, name=f"held{e}", offset=raw_at(e, 3)))
+            if e == LAST:
+                silu(0, raw_at(e, 3))
             w2q = second_layer_codes(e)
+            if e == LAST:
+                silu(1, (RING + 1) * RAW_BYTES)
 
             h = small.tile([P, C * PACK], BF16, name="h", align_bytes=64)
-            for g in range(GROUPS):
-                bank = first_layer(w3q, e, g, "b_bank", 2 + g)
-                part = h[:, g * GROUP * PACK : (g + 1) * GROUP * PACK].rearrange("p (c d t) -> p c t d", d=2, t=PACK)
-                nc.vector.tensor_tensor(part, bank[:].rearrange("p t (c d) -> p c t d", d=2), acts[g][:], MULT)
             h_words = small.tile([P, C], U32, name="h_words", align_bytes=64)
             h_scales = small.tile([P, C], U8, name="h_scales", align_bytes=64)
-            width = C if e < LAST else GROUP
-            for at in range(0, C, width):
+
+            b_banks = [first_layer(w3q, e, g, "b_bank", 2 + g) for g in range(GROUPS)]
+
+            def product(g, pairs=slice(0, GROUP // 2)):
+                part = h[:, g * GROUP * PACK : (g + 1) * GROUP * PACK].rearrange("p (c d t) -> p c t d", d=2, t=PACK)
+                sums = b_banks[g][:].rearrange("p t (c d) -> p c t d", d=2)
+                nc.vector.tensor_tensor(part[:, pairs], sums[:, pairs], acts[g][:, pairs], MULT)
+
+            def h_codes(cols):
                 nc.vector.quantize_mx(
-                    out=h_words[:, at : at + width].bitcast(FP8X4),
-                    scales=h_scales[:, at : at + width],
-                    in_=h[:, at * PACK : (at + width) * PACK],
+                    out=h_words[:, cols].bitcast(FP8X4), scales=h_scales[:, cols], in_=h[:, cols.start * PACK : cols.stop * PACK]
                 )
-            if e < LAST:
-                for nt in range(N_TILES):
-                    y_bank = psum.tile([P, C], F32, name=f"y_bank{e}_{nt}", offset=(4 + nt) * BANK)
-                    nc.tensor.matmul_mx(
-                        out=y_bank[:],
-                        lhsT=w2q[nt][0][:].bitcast(FP8X4),
-                        lhsT_scale=w2q[nt][1][:],
-                        rhs=h_words[:].bitcast(FP8X4),
-                        rhs_scale=h_scales[:],
-                        start=True,
-                        stop=True,
-                    )
-                    if nt == 1 and HELD[e]:
-                        held = y_bank
-                    else:
-                        put_back(e, nt, y_bank, small.tile([P, C], F32, name=f"y{nt}"))
-                continue
-            ys = [small.tile([P, C], F32, name=f"y{nt}") for nt in range(N_TILES)]
-            for at in range(0, C, width):
-                cols = slice(at, at + width)
-                for nt in range(N_TILES):
-                    y_bank = psum.tile([P, width], F32, name=f"y_bank{e}_{nt}_{at}", offset=(4 + nt + 2 * (at // GROUP)) * BANK)
-                    nc.tensor.matmul_mx(
-                        out=y_bank[:],
-                        lhsT=w2q[nt][0][:].bitcast(FP8X4),
-                        lhsT_scale=w2q[nt][1][:],
-                        rhs=h_words[:, cols].bitcast(FP8X4),
-                        rhs_scale=h_scales[:, cols],
-                        start=True,
-                        stop=True,
-                    )
-                    if e == LAST and nt == N_TILES - 1:
-                        nc.scalar.copy(ys[nt][:, cols], y_bank[:])
-                    else:
-                        nc.vector.tensor_tensor(ys[nt][:, cols], y_bank[:], gate_flat[:, e * C + at : e * C + at + width], MULT)
+
+            def second_layer(nt, cols, bank_index):
+                y_bank = psum.tile([P, cols.stop - cols.start], F32, name=f"y_bank{e}_{nt}_{cols.start}", offset=bank_index * BANK)
+                nc.tensor.matmul_mx(
+                    out=y_bank[:],
+                    lhsT=w2q[nt][0][:].bitcast(FP8X4),
+                    lhsT_scale=w2q[nt][1][:],
+                    rhs=h_words[:, cols].bitcast(FP8X4),
+                    rhs_scale=h_scales[:, cols],
+                    start=True,
+                    stop=True,
+                )
+                return y_bank
+
+            if e == LAST:
+                break
+            for g in range(GROUPS):
+                product(g)
+            h_codes(slice(0, C))
             for nt in range(N_TILES):
-                window = results[nt][:].indirect(entries(e))
-                if e == LAST and nt == N_TILES - 1:
-                    nc.vector.tensor_tensor(window, ys[nt][:], gate_flat[:, e * C : (e + 1) * C], MULT)
+                y_bank = second_layer(nt, slice(0, C), 4 + nt)
+                if nt == 1 and HELD[e]:
+                    held = y_bank
+                elif nt == 0 and e == LAST - 1:
+                    nc.vector.tensor_tensor(ending[:, 0:C], y_bank[:], gate_flat[:, e * C : (e + 1) * C], MULT)
+                    window = results[0][:].indirect(offsets[:, e * LIST_COLS : (e + 1) * LIST_COLS - KEPT // 16])
+                    nc.scalar.activation(window, ending[:, 0 : C - KEPT], COPY)
                 else:
-                    nc.scalar.activation(window, ys[nt][:], COPY)
+                    put_back(e, nt, y_bank, small.tile([P, C], F32, name=f"y{nt}"))
+
+        first, second = slice(0, GROUP), slice(GROUP, C)
+        base = LAST * C
+        other = small.tile([P, C], F32, name="y1")
+        product(0)
+        product(1, slice(0, GROUP // 4))
+        h_codes(first)
+        early = [second_layer(nt, first, 4 + nt) for nt in range(N_TILES)]
+        product(1, slice(GROUP // 4, GROUP // 2))
+        h_codes(second)
+        late = [second_layer(nt, second, 6 + nt) for nt in range(N_TILES)]
+        nc.vector.tensor_tensor(ending[:, C : C + GROUP], early[0][:], gate_flat[:, base : base + GROUP], MULT)
+        window = results[0][:].indirect(offsets[:, (base - KEPT) // 16 : (base + GROUP) // 16])
+        nc.scalar.activation(window, ending[:, C - KEPT : C + GROUP], COPY)
+        nc.vector.tensor_tensor(other[:, first], early[1][:], gate_flat[:, base : base + GROUP], MULT)
+        nc.vector.tensor_tensor(ending[:, C + GROUP :], late[0][:], gate_flat[:, base + GROUP :], MULT)
+        nc.vector.tensor_tensor(other[:, second], late[1][:], gate_flat[:, base + GROUP :], MULT)
+        nc.vector.tensor_tensor(results[0][:].indirect(offsets[:, (base + GROUP) // 16 :]), ending[:, C + GROUP :], zero[:], ADD)
+        nc.scalar.activation(results[1][:].indirect(entries(LAST)), other[:], COPY)
 
         for nt in range(N_TILES):
             nc.sync.dma_start(out[nt * P : (nt + 1) * P, :], results[nt][:])

@@ -35,14 +35,15 @@ SCALAR_SHARE = (
     ((64, 64), (64, 32), (0, 64), (0, 48)),
     ((0, 64), (0, 0), (0, 48), (0, 48)),
     ((0, 64), (0, 0), (0, 48), (0, 48)),
-    ((0, 64), (0, 0), (0, 16), (0, 48)),
+    ((32, 64), (0, 0), (0, 32), (0, 48)),
 )
 HALF = H // 2
 OCTETS = H // 8
 ACT_BYTES = GROUP * PACK * 4
-HELD = (1, 1, 0, 0)
+THIN = 160
+FILL = 24
 KEPT = 32
-W2_SCALAR = ((0, 32), (32, 0))
+W2_SCALAR = ((0, 32), (0, 32))
 RAW_BYTES = PACK * H * 4
 RING = 10
 
@@ -115,9 +116,15 @@ def tile_moe_pkd_glu_silu_kernel(tc, x_words, x_scales, w1, w3, w2, gate, offs, 
             n = e * 2 * PASSES + chunk
             return (0 if n == 0 else 1 + (n - 1) % RING) * RAW_BYTES
 
+        def times_gate(y, sums, first):
+            nc.vector.tensor_tensor(y, sums, gate_flat[:, first : first + y.shape[1]], MULT)
+
+        def scatter(nt, y, first):
+            nc.scalar.activation(results[nt][:].indirect(offsets[:, first // 16 : (first + y.shape[1]) // 16]), y, COPY)
+
         def put_back(e, nt, y_bank, y):
-            nc.vector.tensor_tensor(y[:], y_bank[:], gate_flat[:, e * C : (e + 1) * C], MULT)
-            nc.scalar.activation(results[nt][:].indirect(entries(e)), y[:], COPY)
+            times_gate(y[:], y_bank[:], e * C)
+            scatter(nt, y[:], e * C)
 
         def first_layer_codes(w, e, o, chunk):
             raw = loads.tile([P, PACK, H], F32, name=f"raw{e}_{chunk}", offset=raw_at(e, chunk))
@@ -169,10 +176,7 @@ def tile_moe_pkd_glu_silu_kernel(tc, x_words, x_scales, w1, w3, w2, gate, offs, 
             return bank
 
         def second_layer_codes(e):
-            if e < LAST:
-                raw2 = small.tile([P, PACK, N], F32, name="raw2", bufs=3)
-            else:
-                raw2 = loads.tile([P, PACK, N], F32, name="raw2_last", offset=(RING + 1) * RAW_BYTES)
+            raw2 = small.tile([P, PACK, N], F32, name="raw2", bufs=3)
             rows = w2[e].rearrange("(a u r v) n -> u a r (v n)", u=2, r=2, v=2)
             for u in range(2):
                 nc.sync.dma_start(raw2[:, 2 * u : 2 * u + 2, :].rearrange("p v n -> p (v n)"), rows[u])
@@ -187,13 +191,13 @@ def tile_moe_pkd_glu_silu_kernel(tc, x_words, x_scales, w1, w3, w2, gate, offs, 
                 if cut < P // 4:
                     nc.vector.tensor_copy(dst[:, cut:], src[:, cut:])
                 made.append(grouped2)
-            result = [None] * N_TILES
-            for nt in (1, 0):
-                words = small.tile([P, P], U32, name=f"w2_words{nt}", align_bytes=64)
-                scales = small.tile([P, P], U8, name=f"w2_scales{nt}", align_bytes=64)
-                nc.vector.quantize_mx(out=words[:].bitcast(FP8X4), scales=scales[:], in_=made[nt][:])
-                result[nt] = (words, scales)
-            return result
+            return made
+
+        def w2_codes(grouped2, nt):
+            words = small.tile([P, P], U32, name=f"w2_words{nt}", align_bytes=64)
+            scales = small.tile([P, P], U8, name=f"w2_scales{nt}", align_bytes=64)
+            nc.vector.quantize_mx(out=words[:].bitcast(FP8X4), scales=scales[:], in_=grouped2[:])
+            return words, scales
 
         for e in range(E):
             w1q = [first_layer_codes(w1, e, 0, 0)]
@@ -213,14 +217,22 @@ def tile_moe_pkd_glu_silu_kernel(tc, x_words, x_scales, w1, w3, w2, gate, offs, 
                 for g in range(GROUPS):
                     silu(g, raw_at(e, 2) + g * ACT_BYTES)
             w3q.append(first_layer_codes(w3, e, 1, 3))
-            if e > 0 and HELD[e - 1]:
-                put_back(e - 1, 1, held, loads.tile([P, C], F32, name=f"held{e}", offset=raw_at(e, 3)))
+            if e == 1:
+                put_back(0, 1, held, loads.tile([P, C], F32, name="held1", offset=raw_at(e, 3)))
+            if e == 2:
+                run = loads.tile([P, 2 * C - THIN], F32, name="run", offset=raw_at(e, 3))
+                times_gate(run[:, 0:C], held[:], C)
+                scatter(1, run[:, 0 : 2 * C - 2 * THIN], C)
             if e == LAST:
-                silu(0, raw_at(e, 3))
-            w2q = second_layer_codes(e)
+                for g in range(GROUPS):
+                    silu(g, raw_at(e, 3) + g * ACT_BYTES)
+            w2_rounded = second_layer_codes(e)
             if e == LAST:
-                silu(1, (RING + 1) * RAW_BYTES)
+                rest = loads.tile([P, THIN], F32, name="rest", offset=raw_at(e, 3) + GROUPS * ACT_BYTES)
+                times_gate(rest[:], held[:, C - THIN :], LAST * C - THIN)
+                scatter(1, rest[:], LAST * C - THIN)
 
+            w2q = {nt: w2_codes(w2_rounded[nt], nt) for nt in ((1, 0) if e < LAST else (0,))}
             h = small.tile([P, C * PACK], BF16, name="h", align_bytes=64)
             h_words = small.tile([P, C], U32, name="h_words", align_bytes=64)
             h_scales = small.tile([P, C], U8, name="h_scales", align_bytes=64)
@@ -257,8 +269,11 @@ def tile_moe_pkd_glu_silu_kernel(tc, x_words, x_scales, w1, w3, w2, gate, offs, 
             h_codes(slice(0, C))
             for nt in range(N_TILES):
                 y_bank = second_layer(nt, slice(0, C), 4 + nt)
-                if nt == 1 and HELD[e]:
+                if nt == 1:
                     held = y_bank
+                    if e == LAST - 1:
+                        times_gate(run[:, C:], y_bank[:, 0 : C - THIN], e * C)
+                        scatter(1, run[:, 2 * C - 2 * THIN :], LAST * C - 2 * THIN)
                 elif nt == 0 and e == LAST - 1:
                     nc.vector.tensor_tensor(ending[:, 0:C], y_bank[:], gate_flat[:, e * C : (e + 1) * C], MULT)
                     window = results[0][:].indirect(offsets[:, e * LIST_COLS : (e + 1) * LIST_COLS - KEPT // 16])
@@ -270,12 +285,14 @@ def tile_moe_pkd_glu_silu_kernel(tc, x_words, x_scales, w1, w3, w2, gate, offs, 
         base = LAST * C
         other = small.tile([P, C], F32, name="y1")
         product(0)
-        product(1, slice(0, GROUP // 4))
         h_codes(first)
-        early = [second_layer(nt, first, 4 + nt) for nt in range(N_TILES)]
-        product(1, slice(GROUP // 4, GROUP // 2))
+        early = [second_layer(0, first, 4)]
+        product(1, slice(0, FILL))
+        product(1, slice(FILL, GROUP // 2))
+        w2q[1] = w2_codes(w2_rounded[1], 1)
+        early.append(second_layer(1, first, 6))
         h_codes(second)
-        late = [second_layer(nt, second, 6 + nt) for nt in range(N_TILES)]
+        late = [second_layer(nt, second, 7 * (1 - nt)) for nt in range(N_TILES)]
         nc.vector.tensor_tensor(ending[:, C : C + GROUP], early[0][:], gate_flat[:, base : base + GROUP], MULT)
         window = results[0][:].indirect(offsets[:, (base - KEPT) // 16 : (base + GROUP) // 16])
         nc.scalar.activation(window, ending[:, C - KEPT : C + GROUP], COPY)

@@ -35,7 +35,7 @@ SCALAR_SHARE = (
     ((64, 64), (64, 32), (0, 64), (0, 48)),
     ((0, 64), (0, 0), (0, 48), (0, 48)),
     ((0, 64), (0, 0), (0, 48), (0, 48)),
-    ((32, 64), (0, 0), (0, 32), (0, 48)),
+    ((0, 64), (0, 0), (0, 0), (24, 24)),
 )
 HALF = H // 2
 OCTETS = H // 8
@@ -43,7 +43,7 @@ ACT_BYTES = GROUP * PACK * 4
 THIN = 160
 FILL = 24
 KEPT = 32
-W2_SCALAR = ((0, 32), (0, 32))
+W2_SCALAR = ((0, 32), (32, 8))
 RAW_BYTES = PACK * H * 4
 RING = 10
 
@@ -216,6 +216,8 @@ def tile_moe_pkd_glu_silu_kernel(tc, x_words, x_scales, w1, w3, w2, gate, offs, 
             if e < LAST:
                 for g in range(GROUPS):
                     silu(g, raw_at(e, 2) + g * ACT_BYTES)
+            else:
+                silu(0, raw_at(e, 1))
             w3q.append(first_layer_codes(w3, e, 1, 3))
             if e == 1:
                 put_back(0, 1, held, loads.tile([P, C], F32, name="held1", offset=raw_at(e, 3)))
@@ -224,15 +226,14 @@ def tile_moe_pkd_glu_silu_kernel(tc, x_words, x_scales, w1, w3, w2, gate, offs, 
                 times_gate(run[:, 0:C], held[:], C)
                 scatter(1, run[:, 0 : 2 * C - 2 * THIN], C)
             if e == LAST:
-                for g in range(GROUPS):
-                    silu(g, raw_at(e, 3) + g * ACT_BYTES)
+                silu(1, raw_at(e, 3))
             w2_rounded = second_layer_codes(e)
             if e == LAST:
-                rest = loads.tile([P, THIN], F32, name="rest", offset=raw_at(e, 3) + GROUPS * ACT_BYTES)
+                rest = loads.tile([P, THIN], F32, name="rest", offset=raw_at(e, 3) + ACT_BYTES)
                 times_gate(rest[:], held[:, C - THIN :], LAST * C - THIN)
                 scatter(1, rest[:], LAST * C - THIN)
 
-            w2q = {nt: w2_codes(w2_rounded[nt], nt) for nt in ((1, 0) if e < LAST else (0,))}
+            w2q = {nt: w2_codes(w2_rounded[nt], nt) for nt in ((1, 0) if e < LAST else ())}
             h = small.tile([P, C * PACK], BF16, name="h", align_bytes=64)
             h_words = small.tile([P, C], U32, name="h_words", align_bytes=64)
             h_scales = small.tile([P, C], U8, name="h_scales", align_bytes=64)
@@ -285,17 +286,17 @@ def tile_moe_pkd_glu_silu_kernel(tc, x_words, x_scales, w1, w3, w2, gate, offs, 
         base = LAST * C
         other = small.tile([P, C], F32, name="y1")
         product(0)
+        w2q[0] = w2_codes(w2_rounded[0], 0)
+        product(1, slice(0, FILL))
         h_codes(first)
         early = [second_layer(0, first, 4)]
-        product(1, slice(0, FILL))
         product(1, slice(FILL, GROUP // 2))
         w2q[1] = w2_codes(w2_rounded[1], 1)
         early.append(second_layer(1, first, 6))
+        times_gate(ending[:, C : C + GROUP], early[0][:], base)
+        scatter(0, ending[:, C - KEPT : C + GROUP], base - KEPT)
         h_codes(second)
         late = [second_layer(nt, second, 7 * (1 - nt)) for nt in range(N_TILES)]
-        nc.vector.tensor_tensor(ending[:, C : C + GROUP], early[0][:], gate_flat[:, base : base + GROUP], MULT)
-        window = results[0][:].indirect(offsets[:, (base - KEPT) // 16 : (base + GROUP) // 16])
-        nc.scalar.activation(window, ending[:, C - KEPT : C + GROUP], COPY)
         nc.vector.tensor_tensor(other[:, first], early[1][:], gate_flat[:, base : base + GROUP], MULT)
         nc.vector.tensor_tensor(ending[:, C + GROUP :], late[0][:], gate_flat[:, base + GROUP :], MULT)
         nc.vector.tensor_tensor(other[:, second], late[1][:], gate_flat[:, base + GROUP :], MULT)

@@ -38,7 +38,6 @@ SCALAR_SHARE = (
     ((0, 64), (0, 0), (0, 0), (24, 24)),
 )
 HALF = H // 2
-OCTETS = H // 8
 ACT_BYTES = GROUP * PACK * 4
 THIN = 160
 FILL = 24
@@ -129,16 +128,16 @@ def tile_moe_pkd_glu_silu_kernel(tc, x_words, x_scales, w1, w3, w2, gate, offs, 
         def first_layer_codes(w, e, o, chunk):
             raw = loads.tile([P, PACK, H], F32, name=f"raw{e}_{chunk}", offset=raw_at(e, chunk))
             nc.sync.dma_start(raw[:], w[e, o * K_PASS : (o + 1) * K_PASS, :].rearrange("(p j) i -> p j i", j=PACK))
-            src = raw[:].rearrange("p j (a u r v) -> p u a j v r", u=2, r=2, v=2)
+            src = raw[:].rearrange("p j (m u v) -> p u m j v", u=2, v=2)
             staged = []
             for u in range(2):
                 grouped = stage.tile([P, 2 * K_PASS], BF16, name="grouped", align_bytes=64)
-                dst = grouped[:].rearrange("p (v a r j) -> p a j v r", v=2, r=2, j=PACK)
-                cut = SCALAR_SHARE[e][chunk][u]
+                dst = grouped[:].rearrange("p (v m j) -> p m j v", v=2, j=PACK)
+                cut = 2 * SCALAR_SHARE[e][chunk][u]
                 if cut > 0:
                     nc.scalar.copy(dst[:, 0:cut], src[:, u, 0:cut])
-                if cut < OCTETS:
-                    nc.vector.tensor_copy(dst[:, cut:OCTETS], src[:, u, cut:OCTETS])
+                if cut < P:
+                    nc.vector.tensor_copy(dst[:, cut:P], src[:, u, cut:P])
                 staged.append(grouped)
             made = []
             width = P if (e, chunk) == (LAST, 3) else HALF
@@ -177,9 +176,7 @@ def tile_moe_pkd_glu_silu_kernel(tc, x_words, x_scales, w1, w3, w2, gate, offs, 
 
         def second_layer_codes(e):
             raw2 = small.tile([P, PACK, N], F32, name="raw2", bufs=3)
-            rows = w2[e].rearrange("(a u r v) n -> u a r (v n)", u=2, r=2, v=2)
-            for u in range(2):
-                nc.sync.dma_start(raw2[:, 2 * u : 2 * u + 2, :].rearrange("p v n -> p (v n)"), rows[u])
+            nc.sync.dma_start(raw2[:], w2[e].rearrange("(p j) n -> p j n", j=PACK))
             made = []
             for nt in range(N_TILES):
                 grouped2 = small.tile([P, P * PACK], BF16, name=f"grouped2_{nt}", align_bytes=64)

@@ -32,17 +32,16 @@ BANK = 2048
 GATE_COLS = SLOTS // P
 GATHER = 2 * C
 SCALAR_SHARE = (
-    ((64, 64), (64, 32), (0, 64), (0, 48)),
-    ((0, 64), (0, 0), (0, 48), (0, 48)),
-    ((0, 64), (0, 0), (0, 48), (0, 48)),
-    ((0, 64), (0, 0), (0, 0), (24, 24)),
+    ((64, 64), (64, 32), (0, 64), (24, 24)),
+    ((0, 64), (0, 0), (0, 64), (24, 24)),
+    ((0, 64), (0, 0), (0, 64), (24, 24)),
+    ((32, 64), (0, 0), (0, 24), (24, 24)),
 )
 HALF = H // 2
 ACT_BYTES = GROUP * PACK * 4
 THIN = 160
 FILL = 24
 KEPT = 32
-W2_SCALAR = ((0, 32), (32, 8))
 RAW_BYTES = PACK * H * 4
 RING = 10
 
@@ -182,11 +181,7 @@ def tile_moe_pkd_glu_silu_kernel(tc, x_words, x_scales, w1, w3, w2, gate, offs, 
                 grouped2 = small.tile([P, P * PACK], BF16, name=f"grouped2_{nt}", align_bytes=64)
                 dst = grouped2[:].rearrange("p (c i j) -> p c j i", i=4, j=PACK)
                 src = raw2[:, :, nt * P : (nt + 1) * P].rearrange("p j (c i) -> p c j i", i=4)
-                cut = W2_SCALAR[e == LAST][nt]
-                if cut > 0:
-                    nc.scalar.copy(dst[:, 0:cut], src[:, 0:cut])
-                if cut < P // 4:
-                    nc.vector.tensor_copy(dst[:, cut:], src[:, cut:])
+                nc.scalar.copy(dst, src)
                 made.append(grouped2)
             return made
 
@@ -214,7 +209,7 @@ def tile_moe_pkd_glu_silu_kernel(tc, x_words, x_scales, w1, w3, w2, gate, offs, 
                 for g in range(GROUPS):
                     silu(g, raw_at(e, 2) + g * ACT_BYTES)
             else:
-                silu(0, raw_at(e, 1))
+                silu(0, raw_at(e, 2))
             w3q.append(first_layer_codes(w3, e, 1, 3))
             if e == 1:
                 put_back(0, 1, held, loads.tile([P, C], F32, name="held1", offset=raw_at(e, 3)))
@@ -230,7 +225,7 @@ def tile_moe_pkd_glu_silu_kernel(tc, x_words, x_scales, w1, w3, w2, gate, offs, 
                 times_gate(rest[:], held[:, C - THIN :], LAST * C - THIN)
                 scatter(1, rest[:], LAST * C - THIN)
 
-            w2q = {nt: w2_codes(w2_rounded[nt], nt) for nt in ((1, 0) if e < LAST else ())}
+            w2q = {}
             h = small.tile([P, C * PACK], BF16, name="h", align_bytes=64)
             h_words = small.tile([P, C], U32, name="h_words", align_bytes=64)
             h_scales = small.tile([P, C], U8, name="h_scales", align_bytes=64)
@@ -264,6 +259,8 @@ def tile_moe_pkd_glu_silu_kernel(tc, x_words, x_scales, w1, w3, w2, gate, offs, 
                 break
             for g in range(GROUPS):
                 product(g)
+            for nt in range(N_TILES):
+                w2q[nt] = w2_codes(w2_rounded[nt], nt)
             h_codes(slice(0, C))
             for nt in range(N_TILES):
                 y_bank = second_layer(nt, slice(0, C), 4 + nt)

@@ -66,6 +66,17 @@ def tile_moe_pkd_glu_silu_kernel(tc, x_words, x_scales, w1, w3, w2, gate, offs, 
         offsets = keep.tile([P, E * LIST_COLS], U16, name="offsets")
         nc.sync.dma_start(offsets[:], offs)
         nc.sync.dma_start(token_words[1][:], x_words[1].rearrange("p t r -> p (t r)").bitcast(I32))
+
+        def raw_at(e, chunk):
+            n = e * 2 * PASSES + chunk
+            return (0 if n == 0 else 1 + (n - 1) % RING) * RAW_BYTES
+
+        def load_chunk(w, e, o, chunk):
+            raw = loads.tile([P, PACK, H], F32, name=f"raw{e}_{chunk}", offset=raw_at(e, chunk))
+            nc.sync.dma_start(raw[:], w[e, o * K_PASS : (o + 1) * K_PASS, :].rearrange("(p j) i -> p j i", j=PACK))
+            return raw
+
+        first_chunk = load_chunk(w1, 0, 0, 0)
         for q in range(4):
             nc.sync.dma_start(
                 token_scales[32 * q : 32 * q + 4 * PASSES, :].bitcast(I32),
@@ -110,10 +121,6 @@ def tile_moe_pkd_glu_silu_kernel(tc, x_words, x_scales, w1, w3, w2, gate, offs, 
         def entries(e):
             return offsets[:, e * LIST_COLS : (e + 1) * LIST_COLS]
 
-        def raw_at(e, chunk):
-            n = e * 2 * PASSES + chunk
-            return (0 if n == 0 else 1 + (n - 1) % RING) * RAW_BYTES
-
         def times_gate(y, sums, first):
             nc.vector.tensor_tensor(y, sums, gate_flat[:, first : first + y.shape[1]], MULT)
 
@@ -125,8 +132,7 @@ def tile_moe_pkd_glu_silu_kernel(tc, x_words, x_scales, w1, w3, w2, gate, offs, 
             scatter(nt, y[:], e * C)
 
         def first_layer_codes(w, e, o, chunk):
-            raw = loads.tile([P, PACK, H], F32, name=f"raw{e}_{chunk}", offset=raw_at(e, chunk))
-            nc.sync.dma_start(raw[:], w[e, o * K_PASS : (o + 1) * K_PASS, :].rearrange("(p j) i -> p j i", j=PACK))
+            raw = first_chunk if (e, chunk) == (0, 0) else load_chunk(w, e, o, chunk)
             src = raw[:].rearrange("p j (m u v) -> p u m j v", u=2, v=2)
             staged = []
             for u in range(2):

from contextlib import ExitStack

import concourse.mybir as mybir
from concourse.masks import make_identity

K, T, E, C, H, N = 1024, 1280, 4, 256, 512, 256
FLOPS = 2 * E * C * (2 * K * H + H * N)

F32 = mybir.dt.float32
BF16 = mybir.dt.bfloat16
I32 = mybir.dt.int32
U32 = mybir.dt.uint32
U16 = mybir.dt.uint16
U8 = mybir.dt.uint8
FP8X4 = mybir.dt.float8_e4m3fn_x4
MULT = mybir.AluOpType.mult
ADD = mybir.AluOpType.add
SILU = mybir.ActivationFunctionType.Silu
COPY = mybir.ActivationFunctionType.Copy

P = 128
PACK = 4
K_PASS = P * PACK
PASSES = K // K_PASS
SLOTS = E * C
LIST_COLS = C // 16
GROUP = 128
GROUPS = C // GROUP
N_TILES = N // P
LAST = E - 1
BANK = 2048
GATE_COLS = SLOTS // P
GATHER = 2 * C
SCALAR_SHARE = (
    ((64, 64), (64, 32), (0, 64), (24, 24)),
    ((0, 64), (0, 0), (0, 64), (24, 24)),
    ((0, 64), (0, 0), (0, 64), (24, 24)),
    ((32, 64), (0, 0), (0, 24), (24, 24)),
)
HALF = H // 2
ACT_BYTES = GROUP * PACK * 4
THIN = 160
FILL = 24
KEPT = 32
RAW_BYTES = PACK * H * 4
RING = 10


def tile_moe_pkd_glu_silu_kernel(tc, x_words, x_scales, w1, w3, w2, gate, offs, out):
    nc = tc.nc

    with ExitStack() as ctx:
        keep = ctx.enter_context(tc.tile_pool(name="keep", bufs=1))
        loads = ctx.enter_context(tc.tile_pool(name="loads", bufs=1))
        stage = ctx.enter_context(tc.tile_pool(name="stage", bufs=6))
        codes = ctx.enter_context(tc.tile_pool(name="codes", bufs=16))
        small = ctx.enter_context(tc.tile_pool(name="small", bufs=2))
        psum = ctx.enter_context(tc.psum_pool(name="psum", bufs=1))

        token_scales = keep.tile([P, T], U8, name="token_scales", align_bytes=64)
        nc.vector.memset(token_scales[:].bitcast(I32), 0)
        gate_row = keep.tile([P, GATE_COLS], F32, name="gate_row")
        nc.scalar.dma_start(gate_row[:], gate[0:1, :].rearrange("o (p m) -> (o p) m", m=GATE_COLS))
        token_words = [keep.tile([P, T], I32, name=f"token_words{o}", align_bytes=64) for o in range(PASSES)]
        nc.sync.dma_start(token_words[0][:], x_words[0].rearrange("p t r -> p (t r)").bitcast(I32))
        offsets = keep.tile([P, E * LIST_COLS], U16, name="offsets")
        nc.sync.dma_start(offsets[:], offs)
        nc.sync.dma_start(token_words[1][:], x_words[1].rearrange("p t r -> p (t r)").bitcast(I32))

        def raw_at(e, chunk):
            n = e * 2 * PASSES + chunk
            return (0 if n == 0 else 1 + (n - 1) % RING) * RAW_BYTES

        def load_chunk(w, e, o, chunk):
            raw = loads.tile([P, PACK, H], F32, name=f"raw{e}_{chunk}", offset=raw_at(e, chunk))
            nc.sync.dma_start(raw[:], w[e, o * K_PASS : (o + 1) * K_PASS, :].rearrange("(p j) i -> p j i", j=PACK))
            return raw

        first_chunk = load_chunk(w1, 0, 0, 0)
        for q in range(4):
            nc.sync.dma_start(
                token_scales[32 * q : 32 * q + 4 * PASSES, :].bitcast(I32),
                x_scales[:, 4 * q : 4 * q + 4, :].bitcast(I32),
            )

        identity = keep.tile([P, P], F32, name="identity")
        make_identity(nc, identity[:])
        results = [keep.tile([P, T], F32, name=f"result{nt}") for nt in range(N_TILES)]
        nc.vector.memset(results[0][:], 0.0)
        zero = keep.tile([P, GROUP], F32, name="zero")
        nc.vector.memset(zero[:], 0.0)
        nc.scalar.activation(results[1][:], zero[:, 0:1].to_broadcast([P, T]), SILU)
        ending = keep.tile([P, 2 * C], F32, name="ending")

        gates = keep.tile([P, P, GATE_COLS], F32, name="gates")
        for half in range(GATE_COLS // PACK):
            bank = psum.tile([P, PACK, P], F32, name=f"gate_bank{half}", offset=(6 + half) * BANK)
            for m in range(PACK):
                col = half * PACK + m
                nc.tensor.transpose(bank[:, m, :], gate_row[:, col : col + 1].to_broadcast([P, P]), identity[:])
            nc.scalar.copy(gates[:, :, half * PACK : (half + 1) * PACK], bank[:].rearrange("p m n -> p n m"))
        gate_flat = gates[:].rearrange("p n m -> p (n m)")

        slot_words = []
        slot_scales = []
        for x in range(SLOTS // GATHER):
            part = offsets[:, x * GATHER // 16 : (x + 1) * GATHER // 16]
            both = []
            for o in range(PASSES):
                picked = keep.tile([P, GATHER], U32, name=f"slot_words{x}_{o}", align_bytes=64)
                nc.vector.tensor_copy(picked[:], token_words[o][:].bitcast(U32).indirect(part))
                both.append(picked)
            slot_words.append(both)

        def gather_scales(picked, x):
            nc.vector.tensor_copy(picked[:], token_scales[:].indirect(offsets[:, x * GATHER // 16 : (x + 1) * GATHER // 16]))
            slot_scales.append(picked)

        gather_scales(keep.tile([P, GATHER], U8, name="slot_scales", align_bytes=64), 0)

        def entries(e):
            return offsets[:, e * LIST_COLS : (e + 1) * LIST_COLS]

        def times_gate(y, sums, first):
            nc.vector.tensor_tensor(y, sums, gate_flat[:, first : first + y.shape[1]], MULT)

        def scatter(nt, y, first):
            nc.scalar.activation(results[nt][:].indirect(offsets[:, first // 16 : (first + y.shape[1]) // 16]), y, COPY)

        def put_back(e, nt, y_bank, y):
            times_gate(y[:], y_bank[:], e * C)
            scatter(nt, y[:], e * C)

        def first_layer_codes(w, e, o, chunk):
            raw = first_chunk if (e, chunk) == (0, 0) else load_chunk(w, e, o, chunk)
            src = raw[:].rearrange("p j (m u v) -> p u m j v", u=2, v=2)
            staged = []
            for u in range(2):
                grouped = stage.tile([P, 2 * K_PASS], BF16, name="grouped", align_bytes=64)
                dst = grouped[:].rearrange("p (v m j) -> p m j v", v=2, j=PACK)
                cut = 2 * SCALAR_SHARE[e][chunk][u]
                if cut > 0:
                    nc.scalar.copy(dst[:, 0:cut], src[:, u, 0:cut])
                if cut < P:
                    nc.vector.tensor_copy(dst[:, cut:P], src[:, u, cut:P])
                staged.append(grouped)
            made = []
            width = P if (e, chunk) == (LAST, 3) else HALF
            for grouped in staged:
                words = codes.tile([P, HALF], U32, name="w_words", align_bytes=64)
                scales = codes.tile([P, HALF], U8, name="w_scales", align_bytes=64)
                for at in range(0, HALF, width):
                    nc.vector.quantize_mx(
                        out=words[:, at : at + width].bitcast(FP8X4),
                        scales=scales[:, at : at + width],
                        in_=grouped[:, at * PACK : (at + width) * PACK],
                    )
                made.append((words, scales))
            return made

        def first_layer(weights, e, g, kind, bank_index):
            bank = psum.tile([P, PACK, GROUP], F32, name=f"{kind}{e}_{g}", offset=bank_index * BANK)
            x, first = divmod(e * C + g * GROUP, GATHER)
            cols = slice(first, first + GROUP)
            steps = [(o, t) for o in range(PASSES) for t in range(PACK)]
            if g > 0:
                steps = steps[:PACK] + steps[: PACK - 1 : -1]
            for step, (o, t) in enumerate(steps):
                words, scales = weights[o][t // 2]
                part = slice(t % 2 * P, (t % 2 + 1) * P)
                nc.tensor.matmul_mx(
                    out=bank[:, t, :],
                    lhsT=words[:, part].bitcast(FP8X4),
                    lhsT_scale=scales[:, part],
                    rhs=slot_words[x][o][:, cols].bitcast(FP8X4),
                    rhs_scale=slot_scales[x][4 * o : P, cols],
                    start=(step == 0),
                    stop=(step == len(steps) - 1),
                )
            return bank

        def second_layer_codes(e):
            raw2 = small.tile([P, PACK, N], F32, name="raw2", bufs=3)
            nc.sync.dma_start(raw2[:], w2[e].rearrange("(p j) n -> p j n", j=PACK))
            made = []
            for nt in range(N_TILES):
                grouped2 = small.tile([P, P * PACK], BF16, name=f"grouped2_{nt}", align_bytes=64)
                dst = grouped2[:].rearrange("p (c i j) -> p c j i", i=4, j=PACK)
                src = raw2[:, :, nt * P : (nt + 1) * P].rearrange("p j (c i) -> p c j i", i=4)
                nc.scalar.copy(dst, src)
                made.append(grouped2)
            return made

        def w2_codes(grouped2, nt):
            words = small.tile([P, P], U32, name=f"w2_words{nt}", align_bytes=64)
            scales = small.tile([P, P], U8, name=f"w2_scales{nt}", align_bytes=64)
            nc.vector.quantize_mx(out=words[:].bitcast(FP8X4), scales=scales[:], in_=grouped2[:])
            return words, scales

        for e in range(E):
            w1q = [first_layer_codes(w1, e, 0, 0)]
            if e == 0:
                gather_scales(loads.tile([P, GATHER], U8, name="late_scales", align_bytes=64, offset=0), 1)
            w1q.append(first_layer_codes(w1, e, 1, 1))
            w3q = [first_layer_codes(w3, e, 0, 2)]
            acts = []
            a_banks = [first_layer(w1q, e, g, "a_bank", g) for g in range(GROUPS)]

            def silu(g, at):
                act = loads.tile([P, GROUP // 2, PACK, 2], F32, name=f"act{e}_{g}", offset=at)
                nc.scalar.activation(act[:], a_banks[g][:].rearrange("p t (c d) -> p c t d", d=2), SILU)
                acts.append(act)

            if e < LAST:
                for g in range(GROUPS):
                    silu(g, raw_at(e, 2) + g * ACT_BYTES)
            else:
                silu(0, raw_at(e, 2))
            w3q.append(first_layer_codes(w3, e, 1, 3))
            if e == 1:
                put_back(0, 1, held, loads.tile([P, C], F32, name="held1", offset=raw_at(e, 3)))
            if e == 2:
                run = loads.tile([P, 2 * C - THIN], F32, name="run", offset=raw_at(e, 3))
                times_gate(run[:, 0:C], held[:], C)
                scatter(1, run[:, 0 : 2 * C - 2 * THIN], C)
            if e == LAST:
                silu(1, raw_at(e, 3))
            w2_rounded = second_layer_codes(e)
            if e == LAST:
                rest = loads.tile([P, THIN], F32, name="rest", offset=raw_at(e, 3) + ACT_BYTES)
                times_gate(rest[:], held[:, C - THIN :], LAST * C - THIN)
                scatter(1, rest[:], LAST * C - THIN)

            w2q = {}
            h = small.tile([P, C * PACK], BF16, name="h", align_bytes=64)
            h_words = small.tile([P, C], U32, name="h_words", align_bytes=64)
            h_scales = small.tile([P, C], U8, name="h_scales", align_bytes=64)

            b_banks = [first_layer(w3q, e, g, "b_bank", 2 + g) for g in range(GROUPS)]

            def product(g, pairs=slice(0, GROUP // 2)):
                part = h[:, g * GROUP * PACK : (g + 1) * GROUP * PACK].rearrange("p (c d t) -> p c t d", d=2, t=PACK)
                sums = b_banks[g][:].rearrange("p t (c d) -> p c t d", d=2)
                nc.vector.tensor_tensor(part[:, pairs], sums[:, pairs], acts[g][:, pairs], MULT)

            def h_codes(cols):
                nc.vector.quantize_mx(
                    out=h_words[:, cols].bitcast(FP8X4), scales=h_scales[:, cols], in_=h[:, cols.start * PACK : cols.stop * PACK]
                )

            def second_layer(nt, cols, bank_index):
                y_bank = psum.tile([P, cols.stop - cols.start], F32, name=f"y_bank{e}_{nt}_{cols.start}", offset=bank_index * BANK)
                nc.tensor.matmul_mx(
                    out=y_bank[:],
                    lhsT=w2q[nt][0][:].bitcast(FP8X4),
                    lhsT_scale=w2q[nt][1][:],
                    rhs=h_words[:, cols].bitcast(FP8X4),
                    rhs_scale=h_scales[:, cols],
                    start=True,
                    stop=True,
                )
                return y_bank

            if e == LAST:
                break
            for g in range(GROUPS):
                product(g)
            for nt in range(N_TILES):
                w2q[nt] = w2_codes(w2_rounded[nt], nt)
            h_codes(slice(0, C))
            for nt in range(N_TILES):
                y_bank = second_layer(nt, slice(0, C), 4 + nt)
                if nt == 1:
                    held = y_bank
                    if e == LAST - 1:
                        times_gate(run[:, C:], y_bank[:, 0 : C - THIN], e * C)
                        scatter(1, run[:, 2 * C - 2 * THIN :], LAST * C - 2 * THIN)
                elif nt == 0 and e == LAST - 1:
                    nc.vector.tensor_tensor(ending[:, 0:C], y_bank[:], gate_flat[:, e * C : (e + 1) * C], MULT)
                    window = results[0][:].indirect(offsets[:, e * LIST_COLS : (e + 1) * LIST_COLS - KEPT // 16])
                    nc.scalar.activation(window, ending[:, 0 : C - KEPT], COPY)
                else:
                    put_back(e, nt, y_bank, small.tile([P, C], F32, name=f"y{nt}"))

        first, second = slice(0, GROUP), slice(GROUP, C)
        base = LAST * C
        other = small.tile([P, C], F32, name="y1")
        product(0)
        w2q[0] = w2_codes(w2_rounded[0], 0)
        product(1, slice(0, FILL))
        h_codes(first)
        early = [second_layer(0, first, 4)]
        product(1, slice(FILL, GROUP // 2))
        w2q[1] = w2_codes(w2_rounded[1], 1)
        early.append(second_layer(1, first, 6))
        times_gate(ending[:, C : C + GROUP], early[0][:], base)
        scatter(0, ending[:, C - KEPT : C + GROUP], base - KEPT)
        h_codes(second)
        late = [second_layer(nt, second, 7 * (1 - nt)) for nt in range(N_TILES)]
        nc.vector.tensor_tensor(other[:, first], early[1][:], gate_flat[:, base : base + GROUP], MULT)
        nc.vector.tensor_tensor(ending[:, C + GROUP :], late[0][:], gate_flat[:, base + GROUP :], MULT)
        nc.vector.tensor_tensor(other[:, second], late[1][:], gate_flat[:, base + GROUP :], MULT)
        nc.vector.tensor_tensor(results[0][:].indirect(offsets[:, (base + GROUP) // 16 :]), ending[:, C + GROUP :], zero[:], ADD)
        nc.scalar.activation(results[1][:].indirect(entries(LAST)), other[:], COPY)

        for nt in range(N_TILES):
            nc.sync.dma_start(out[nt * P : (nt + 1) * P, :], results[nt][:])
